import numpy as np
import ml_dtypes


def mxq(x, axis, fmt="e4m3"):
    dtype, down = {"e4m3": (ml_dtypes.float8_e4m3fn, 7), "e5m2": (ml_dtypes.float8_e5m2, 14)}[fmt]
    v = np.moveaxis(np.asarray(x, np.float32).astype(ml_dtypes.bfloat16).astype(np.float64), axis, -1)
    blocks = v.reshape(v.shape[:-1] + (-1, 32))
    amax = np.abs(blocks).max(-1, keepdims=True)
    byte = np.maximum(np.where(amax > 0, np.frexp(amax)[1] - 1 + 127, 0) - down, 1)
    scale = np.exp2(byte - 127.0)
    codes = (blocks / scale).astype(np.float32).astype(dtype).astype(np.float64)
    return np.moveaxis((codes * scale).reshape(v.shape), -1, axis)


WIDE = False


def mx_kscale(k):
    if not WIDE:
        return np.ones(k)
    levels = np.array([10, -10, 5, -5, 0])
    if k % 512:
        return np.exp2(np.random.permutation(np.resize(levels, k // 32))).repeat(32)
    a = np.empty((k // 512, 16))
    for p in range(k // 512):
        a[p, :8] = np.random.permutation(np.resize(levels, 8))
        for g in range(8):
            far = levels[np.abs(levels - a[p, g]) >= 10]
            a[p, g + 8] = far[np.random.randint(len(far))]
    return np.exp2(a.ravel()).repeat(32)


BF16 = ml_dtypes.bfloat16


def bf(x):
    return np.asarray(x, np.float32).astype(BF16)


def f64(x):
    return np.asarray(x).astype(np.float64)


E2M1 = np.array([0.0, 0.5, 1.0, 1.5, 2.0, 3.0, 4.0, 6.0, -0.0, -0.5, -1.0, -1.5, -2.0, -3.0, -4.0, -6.0])


def pack_weight(w, fmt):
    k, n = w.shape
    w = f64(bf(w)).reshape(k // 32, 32, n)
    amax = np.abs(w).max(1)
    if fmt == "e4m3":
        byte = np.frexp(amax)[1] - 1 + 127 - 7
    else:
        mant, ex = np.frexp(amax / 6.0)
        byte = np.where(mant > 0.5, ex, ex - 1) + 127
    byte = np.clip(np.where(amax > 0, byte, 1), 1, 254)
    scaled = (w * np.exp2(127.0 - byte)[:, None, :]).reshape(k, n).astype(np.float32)
    by_word = np.ascontiguousarray(scaled.reshape(k // 512, 128, 4, n).transpose(0, 1, 3, 2))
    if fmt == "e4m3":
        words = by_word.astype(ml_dtypes.float8_e4m3fn).view(np.uint8)
    else:
        c = by_word.astype(ml_dtypes.float4_e2m1fn).view(np.uint8) & 0xF
        words = c[..., 0::2] | (c[..., 1::2] << 4)
    return np.ascontiguousarray(words), np.ascontiguousarray(byte.astype(np.uint8).reshape(k // 512, 16, n))


def unpack_weight(words, scales, fmt):
    g, p, n, _ = words.shape
    if fmt == "e4m3":
        vals = np.ascontiguousarray(words).view(ml_dtypes.float8_e4m3fn).astype(np.float64)
    else:
        nib = np.empty((g, p, n, 4), np.uint8)
        nib[..., 0::2] = words & 0xF
        nib[..., 1::2] = words >> 4
        vals = E2M1[nib]
    vals = vals * np.repeat(np.exp2(scales.astype(np.float64) - 127.0), 8, axis=1)[..., None]
    return vals.transpose(0, 1, 3, 2).reshape(g * 512, n)
def pack4(w):
    words, scales = pack_weight(w, "e2m1")
    return words.reshape(words.shape[0], 128, -1), scales


def unpack4(words, scales):
    return unpack_weight(words.reshape(words.shape[0], 128, -1, 2), scales, "e2m1")


H, C, G = 1536, 1024, 512


def setup_inputs():
    s, t = mx_kscale(H), mx_kscale(C)
    x = np.random.standard_normal((H, C)) * s[:, None] * t
    A = np.random.standard_normal((H, H)) / (3 * np.sqrt(H)) / s[:, None] * s
    R = np.random.standard_normal((C, C)) / (3 * np.sqrt(C)) / t[:, None] * t
    B = np.random.standard_normal((H, G)) / np.sqrt(H) / s[:, None]
    transfer_words, transfer_scales = pack4(A)
    reclass_words, reclass_scales = pack4(R)
    bracket_words, bracket_scales = pack4(B)
    return {"x": bf(x),
            "transfer_words": transfer_words, "transfer_scales": transfer_scales,
            "reclass_words": reclass_words, "reclass_scales": reclass_scales,
            "bracket_words": bracket_words, "bracket_scales": bracket_scales,
            "propensity": bf(np.random.uniform(0.5, 1.5, H)),
            "rate": bf(np.random.uniform(0.1, 0.5, (G, C)) / t)}


def reference(x, transfer_words, transfer_scales, reclass_words, reclass_scales, bracket_words, bracket_scales, propensity, rate):
    A = unpack4(transfer_words, transfer_scales)
    R = unpack4(reclass_words, reclass_scales)
    B = unpack4(bracket_words, bracket_scales)
    x0 = f64(x)
    x1 = x0 + (A.T @ mxq(x0, 0, "e4m3"))
    x2 = x1 + f64(propensity)[:, None] * (mxq(x1, 1, "e4m3") @ R)
    return f64(rate) * (B.T @ mxq(x2, 0, "e4m3"))

@@ -1,0 +1,448 @@
+from contextlib import ExitStack
+
+import concourse.mybir as mybir
+from concourse.masks import make_identity
+
+H, C, G = 1536, 1024, 512
+FLOPS = 2 * (H * H * C + H * C * C + H * G * C)
+
+F32 = mybir.dt.float32
+BF16 = mybir.dt.bfloat16
+I32 = mybir.dt.int32
+U32 = mybir.dt.uint32
+U8 = mybir.dt.uint8
+FP8X4 = mybir.dt.float8_e4m3fn_x4
+FP4X4 = mybir.dt.float4_e2m1fn_x4
+ADD = mybir.AluOpType.add
+MULT = mybir.AluOpType.mult
+
+P = 128
+PACK = 4
+K_PASS = P * PACK
+GROUPS = H // K_PASS
+HALVES = C // K_PASS
+HALF = K_PASS
+PART = HALF // 2
+OUT_TILES = G // P
+BANKS = 8
+E2M1_BYTES = 2
+
+
+def tile_household_bracket_response_t2_kernel(
+    tc,
+    x,
+    transfer_words,
+    transfer_scales,
+    reclass_words,
+    reclass_scales,
+    bracket_words,
+    bracket_scales,
+    propensity,
+    rate,
+    out,
+):
+    nc = tc.nc
+    with ExitStack() as ctx:
+        keep = ctx.enter_context(tc.tile_pool(name="keep", bufs=1))
+        work = ctx.enter_context(tc.tile_pool(name="work", bufs=3))
+        psum = ctx.enter_context(tc.psum_pool(name="psum", bufs=1))
+        ctx.enter_context(tc.manual_schedule())
+
+        def kept(shape, dtype, name):
+            return keep.tile(shape, dtype, name=name, align_bytes=64)
+
+        a_scales_in = [kept([P, GROUPS, K_PASS], U8, "a_scales_first"), kept([P, GROUPS, H - K_PASS], U8, "a_scales_rest")]
+        r_scales = kept([P, HALVES, C], U8, "r_scales")
+        b_scales = kept([P, GROUPS, G], U8, "b_scales")
+        nc.vector.memset(a_scales_in[0][:].bitcast(I32), 0)
+        nc.gpsimd.memset(a_scales_in[1][:].bitcast(I32), 0)
+        nc.gpsimd.memset(r_scales[:].bitcast(I32), 0)
+        nc.gpsimd.memset(b_scales[:].bitcast(I32), 0)
+        identity = kept([P, P], F32, "identity")
+        make_identity(nc, identity[:])
+
+        def load_scales(plane, scales):
+            words = plane[:].bitcast(I32)
+            for q in range(4):
+                nc.sync.dma_start(
+                    out=words[32 * q : 32 * q + 4, :, :],
+                    in_=scales[:, 4 * q : 4 * q + 4, :].rearrange("k r n -> r k n").bitcast(I32),
+                )
+
+        def load_words(tile, words):
+            nc.sync.dma_start(out=tile[:].bitcast(I32), in_=words.rearrange("k p n -> p k n").bitcast(I32))
+
+        x_in = [[kept([P, PACK, HALF], BF16, f"x_{g}_{half}") for half in range(HALVES)] for g in range(GROUPS)]
+        a_in = [kept([P, GROUPS, E2M1_BYTES * K_PASS], U8, f"a_in_{g}") for g in range(GROUPS)]
+        r_words = kept([P, HALVES, E2M1_BYTES * C], U8, "r_words")
+        b_words = kept([P, GROUPS, E2M1_BYTES * G], U8, "b_words")
+        prop = kept([P, GROUPS, PACK], BF16, "prop")
+        rates = kept([P, OUT_TILES, C], BF16, "rates")
+
+        def load_x(g, half):
+            nc.sync.dma_start(
+                out=x_in[g][half][:],
+                in_=x[K_PASS * g : K_PASS * (g + 1), HALF * half : HALF * (half + 1)].rearrange("(p t) c -> p t c", t=PACK),
+            )
+
+        def load_a(g):
+            width = E2M1_BYTES * K_PASS
+            load_words(a_in[g], transfer_words[:, :, width * g : width * (g + 1)])
+
+        load_a(0)
+        load_scales(a_scales_in[0], transfer_scales[:, :, :K_PASS])
+        load_x(0, 0)
+        load_x(1, 0)
+        load_x(2, 0)
+        load_x(0, 1)
+        load_scales(a_scales_in[1], transfer_scales[:, :, K_PASS:])
+        load_a(1)
+        load_x(1, 1)
+        load_x(2, 1)
+        load_a(2)
+        load_scales(r_scales, reclass_scales)
+        load_words(r_words, reclass_words)
+        nc.sync.dma_start(out=prop[:], in_=propensity.rearrange("(g p t) -> p g t", p=P, t=PACK))
+        load_scales(b_scales, bracket_scales)
+        load_words(b_words, bracket_words)
+        nc.sync.dma_start(out=rates[:], in_=rate.rearrange("(j p) c -> p j c", p=P))
+
+        closed_banks = list(range(BANKS))
+        open_banks = {}
+
+        def open_bank(key, shape):
+            bank = closed_banks.pop(0)
+            tile = psum.tile(shape, F32, name="acc", tag=f"bank_{bank}")
+            open_banks[key] = bank, tile
+            return tile
+
+        def close_bank(key):
+            bank, tile = open_banks.pop(key)
+            closed_banks.append(bank)
+            return tile
+
+        staged = {}
+
+        def stage(kind, key, shape, bufs):
+            if (kind, key) not in staged:
+                tile = work.tile(shape, BF16, name=kind, tag=kind, bufs=bufs, align_bytes=64)
+                staged[kind, key] = tile
+            return staged[kind, key]
+
+        def copy(engine, out_ap, in_ap):
+            if engine == "vector":
+                nc.vector.tensor_copy(out=out_ap, in_=in_ap)
+            else:
+                nc.scalar.copy(out=out_ap, in_=in_ap)
+
+        def flat(tile):
+            return tile[:].rearrange("p c t -> p (c t)")
+
+        a_words = [kept([P, GROUPS, E2M1_BYTES * K_PASS], U8, f"a_words_{g}") for g in range(GROUPS)]
+        a_scales = [kept([P, GROUPS, K_PASS], U8, f"a_scales_{g}") for g in range(GROUPS)]
+
+        def reorder_a_words(g, pair):
+            tiles = slice(2 * pair, 2 * pair + 2)
+            nc.vector.tensor_copy(
+                out=a_words[g][:].rearrange("p k (t m b) -> p t k m b", t=PACK, b=E2M1_BYTES)[:, tiles, :, :, :],
+                in_=a_in[g][:].rearrange("p k (m t b) -> p t k m b", t=PACK, b=E2M1_BYTES)[:, tiles, :, :, :],
+            )
+
+        def reorder_a_scales(g):
+            if g == 0:
+                scales_in = a_scales_in[0][:]
+            else:
+                scales_in = a_scales_in[1][:, :, K_PASS * (g - 1) : K_PASS * g]
+            nc.vector.tensor_copy(
+                out=a_scales[g][:].rearrange("p k (t m) -> p t k m", t=PACK),
+                in_=scales_in.rearrange("p k (m t) -> p t k m", t=PACK),
+            )
+
+        xq = [kept([P, C], U32, f"xq_{g}") for g in range(GROUPS)]
+        xq_scales = [kept([P, C], U8, f"xq_scales_{g}") for g in range(GROUPS)]
+
+        def interleave_x(engine, g, half, part):
+            grouped = stage("x_grouped", (g, half), [P, HALF, PACK], 3)
+            cols = slice(PART * part, PART * (part + 1))
+            copy(engine, grouped[:, cols, :], x_in[g][half][:, :, cols].rearrange("p t c -> p c t"))
+
+        def quantise_x(g, half):
+            cols = slice(HALF * half, HALF * (half + 1))
+            nc.vector.quantize_mx(
+                out=xq[g][:, cols].bitcast(FP8X4),
+                scales=xq_scales[g][:, cols],
+                in_=flat(staged["x_grouped", (g, half)]),
+            )
+
+        x1 = [kept([P, PACK, C], F32, f"x1_{g}") for g in range(GROUPS)]
+
+        def multiply_a_pass(g, half, t, k):
+            cols = slice(HALF * half, HALF * (half + 1))
+            if k == 0:
+                open_bank((1, g, half, t), [P, HALF])
+            nc.tensor.matmul_mx(
+                out=open_banks[1, g, half, t][1][:],
+                lhsT=a_words[g][:, k, E2M1_BYTES * P * t : E2M1_BYTES * P * (t + 1)].bitcast(FP4X4),
+                lhsT_scale=a_scales[g][:, k, P * t : P * (t + 1)],
+                rhs=xq[k][:, cols].bitcast(FP8X4),
+                rhs_scale=xq_scales[k][:, cols],
+                start=(k == 0),
+                stop=(k == GROUPS - 1),
+            )
+
+        def multiply_a(g, half, pair):
+            for t in (2 * pair, 2 * pair + 1):
+                for k in range(GROUPS):
+                    multiply_a_pass(g, half, t, k)
+
+        def add_x(g, half, pair):
+            for t in (2 * pair, 2 * pair + 1):
+                nc.vector.tensor_tensor(
+                    out=x1[g][:, t, HALF * half : HALF * (half + 1)],
+                    in0=close_bank((1, g, half, t))[:],
+                    in1=x_in[g][half][:, t, :],
+                    op=ADD,
+                )
+
+        x1q = [[kept([P, K_PASS], U32, f"x1q_{g}_{half}") for half in range(HALVES)] for g in range(GROUPS)]
+        x1q_scales = [[kept([P, K_PASS], U8, f"x1q_scales_{g}_{half}") for half in range(HALVES)] for g in range(GROUPS)]
+
+        def round_x1(g, half, pair):
+            rounded = stage("x1_rounded", (g, half), [P, PACK, 2, P, 2], 4)
+            for t in (2 * pair, 2 * pair + 1):
+                row = x1[g][:, t, HALF * half : HALF * (half + 1)]
+                nc.scalar.copy(out=rounded[:, t, :, :, :], in_=row.rearrange("p (w u e) -> p u w e", u=2, e=2))
+
+        def turn_x1(g, half, pair):
+            rounded = staged["x1_rounded", (g, half)]
+            turned = open_bank(("turn", g, half, pair), [P, 2, 2, P])
+            for i in range(2):
+                for u in range(2):
+                    words = rounded[:, 2 * pair + i, u, :, :].rearrange("p w e -> p (w e)").bitcast(F32)
+                    nc.tensor.transpose(turned[:, i, u, :], words, identity[:])
+
+        def regroup_x1(g, half, pair):
+            grouped = stage("x1_grouped", (g, half), [P, K_PASS, PACK], 3)
+            words = grouped[:, 2 * P * pair : 2 * P * (pair + 1), :].rearrange("p m v -> p (m v)").bitcast(F32)
+            nc.scalar.copy(
+                out=words.rearrange("p (i m u) -> p i m u", i=2, u=2),
+                in_=close_bank(("turn", g, half, pair))[:].rearrange("p i u m -> p i m u"),
+            )
+
+        def quantise_x1(g, half):
+            nc.vector.quantize_mx(
+                out=x1q[g][half][:].bitcast(FP8X4),
+                scales=x1q_scales[g][half][:],
+                in_=flat(staged["x1_grouped", (g, half)]),
+            )
+
+        def multiply_r(g, half, pair):
+            for t in (2 * pair, 2 * pair + 1):
+                acc = open_bank((2, g, half, t), [P, HALF])
+                for k in range(HALVES):
+                    nc.tensor.matmul_mx(
+                        out=acc[:],
+                        lhsT=x1q[g][k][:, P * t : P * (t + 1)].bitcast(FP8X4),
+                        lhsT_scale=x1q_scales[g][k][:, P * t : P * (t + 1)],
+                        rhs=r_words[:, k, E2M1_BYTES * HALF * half : E2M1_BYTES * HALF * (half + 1)].bitcast(FP4X4),
+                        rhs_scale=r_scales[:, k, HALF * half : HALF * (half + 1)],
+                        start=(k == 0),
+                        stop=(k == HALVES - 1),
+                    )
+
+        def add_x1(g, half, pair):
+            x2 = stage("x2", (g, half), [P, PACK, HALF], 3)
+            for t in (2 * pair, 2 * pair + 1):
+                nc.vector.scalar_tensor_tensor(
+                    out=x2[:, t, :],
+                    in0=close_bank((2, g, half, t))[:],
+                    scalar=prop[:, g, t : t + 1],
+                    in1=x1[g][:, t, HALF * half : HALF * (half + 1)],
+                    op0=MULT,
+                    op1=ADD,
+                )
+
+        x2q = [kept([P, C], U32, f"x2q_{g}") for g in range(GROUPS)]
+        x2q_scales = [kept([P, C], U8, f"x2q_scales_{g}") for g in range(GROUPS)]
+
+        def interleave_x2(engine, g, half, part):
+            grouped = stage("x2_grouped", (g, half), [P, HALF, PACK], 2)
+            cols = slice(PART * part, PART * (part + 1))
+            copy(engine, grouped[:, cols, :], staged["x2", (g, half)][:, :, cols].rearrange("p t c -> p c t"))
+
+        def quantise_x2(g, half):
+            cols = slice(HALF * half, HALF * (half + 1))
+            nc.vector.quantize_mx(
+                out=x2q[g][:, cols].bitcast(FP8X4),
+                scales=x2q_scales[g][:, cols],
+                in_=flat(staged["x2_grouped", (g, half)]),
+            )
+
+        def multiply_b(half, k):
+            cols = slice(HALF * half, HALF * (half + 1))
+            for j in range(OUT_TILES):
+                if k == 0:
+                    open_bank((3, half, j), [P, HALF])
+                nc.tensor.matmul_mx(
+                    out=open_banks[3, half, j][1][:],
+                    lhsT=b_words[:, k, E2M1_BYTES * P * j : E2M1_BYTES * P * (j + 1)].bitcast(FP4X4),
+                    lhsT_scale=b_scales[:, k, P * j : P * (j + 1)],
+                    rhs=x2q[k][:, cols].bitcast(FP8X4),
+                    rhs_scale=x2q_scales[k][:, cols],
+                    start=(k == 0),
+                    stop=(k == GROUPS - 1),
+                )
+
+        def finish(half, pair):
+            cols = slice(HALF * half, HALF * (half + 1))
+            for j in (2 * pair, 2 * pair + 1):
+                response = work.tile([P, HALF], F32, name="response", bufs=7)
+                nc.vector.tensor_tensor(out=response[:], in0=close_bank((3, half, j))[:], in1=rates[:, j, cols], op=MULT)
+                nc.sync.dma_start(out=out[P * j : P * (j + 1), cols], in_=response[:])
+
+        reorder_a_words(0, 0)
+        reorder_a_words(0, 1)
+        interleave_x("vector", 0, 0, 1)
+        reorder_a_scales(0)
+        interleave_x("vector", 1, 0, 1)
+        interleave_x("scalar", 0, 0, 0)
+        interleave_x("scalar", 1, 0, 0)
+        interleave_x("scalar", 2, 0, 1)
+        quantise_x(0, 0)
+        interleave_x("vector", 2, 0, 0)
+        quantise_x(1, 0)
+        interleave_x("vector", 0, 1, 0)
+        quantise_x(2, 0)
+        reorder_a_words(1, 0)
+        reorder_a_scales(1)
+        reorder_a_words(1, 1)
+        interleave_x("scalar", 0, 1, 1)
+        interleave_x("scalar", 1, 1, 0)
+        interleave_x("scalar", 1, 1, 1)
+        interleave_x("scalar", 2, 1, 0)
+        for k in range(GROUPS):
+            for t in range(PACK):
+                multiply_a_pass(0, 0, t, k)
+        add_x(0, 0, 1)
+        interleave_x("vector", 2, 1, 1)
+        quantise_x(0, 1)
+        quantise_x(1, 1)
+        quantise_x(2, 1)
+        multiply_a(1, 0, 0)
+        multiply_a(1, 0, 1)
+        add_x(1, 0, 1)
+        add_x(1, 0, 0)
+        add_x(0, 0, 0)
+        round_x1(1, 0, 1)
+        round_x1(1, 0, 0)
+        round_x1(0, 0, 0)
+        round_x1(0, 0, 1)
+        multiply_a(0, 1, 1)
+        multiply_a(0, 1, 0)
+        add_x(0, 1, 0)
+        reorder_a_words(2, 0)
+        reorder_a_scales(2)
+        add_x(0, 1, 1)
+        round_x1(0, 1, 0)
+        round_x1(0, 1, 1)
+        multiply_a(1, 1, 1)
+        multiply_a(1, 1, 0)
+        add_x(1, 1, 0)
+        add_x(1, 1, 1)
+        round_x1(1, 1, 0)
+        multiply_a(2, 0, 0)
+        add_x(2, 0, 0)
+        reorder_a_words(2, 1)
+        turn_x1(1, 0, 1)
+        turn_x1(0, 1, 0)
+        turn_x1(0, 0, 1)
+        regroup_x1(0, 0, 1)
+        regroup_x1(0, 1, 0)
+        turn_x1(0, 1, 1)
+        turn_x1(1, 0, 0)
+        turn_x1(0, 0, 0)
+        regroup_x1(0, 0, 0)
+        regroup_x1(1, 0, 0)
+        regroup_x1(1, 0, 1)
+        regroup_x1(0, 1, 1)
+        round_x1(1, 1, 1)
+        round_x1(2, 0, 0)
+        multiply_a(2, 1, 0)
+        quantise_x1(0, 0)
+        add_x(2, 1, 0)
+        quantise_x1(1, 0)
+        round_x1(2, 1, 0)
+        multiply_a(2, 1, 1)
+        add_x(2, 1, 1)
+        quantise_x1(0, 1)
+        turn_x1(1, 1, 0)
+        regroup_x1(1, 1, 0)
+        turn_x1(1, 1, 1)
+        regroup_x1(1, 1, 1)
+        multiply_a(2, 0, 1)
+        add_x(2, 0, 1)
+        round_x1(2, 0, 1)
+        round_x1(2, 1, 1)
+        multiply_r(0, 1, 1)
+        add_x1(0, 1, 1)
+        quantise_x1(1, 1)
+        multiply_r(0, 1, 0)
+        add_x1(0, 1, 0)
+        turn_x1(2, 0, 1)
+        regroup_x1(2, 0, 1)
+        interleave_x2("scalar", 0, 1, 0)
+        interleave_x2("scalar", 0, 1, 1)
+        turn_x1(2, 0, 0)
+        multiply_r(1, 0, 0)
+        add_x1(1, 0, 0)
+        multiply_r(1, 0, 1)
+        add_x1(1, 0, 1)
+        interleave_x2("scalar", 1, 0, 0)
+        interleave_x2("scalar", 1, 0, 1)
+        multiply_r(0, 0, 0)
+        add_x1(0, 0, 0)
+        quantise_x2(0, 1)
+        multiply_r(1, 1, 1)
+        add_x1(1, 1, 1)
+        multiply_r(0, 0, 1)
+        add_x1(0, 0, 1)
+        quantise_x2(1, 0)
+        turn_x1(2, 1, 1)
+        regroup_x1(2, 1, 1)
+        turn_x1(2, 1, 0)
+        regroup_x1(2, 1, 0)
+        regroup_x1(2, 0, 0)
+        interleave_x2("scalar", 0, 0, 0)
+        interleave_x2("scalar", 0, 0, 1)
+        multiply_r(1, 1, 0)
+        quantise_x1(2, 1)
+        quantise_x1(2, 0)
+        add_x1(1, 1, 0)
+        interleave_x2("scalar", 1, 1, 0)
+        interleave_x2("scalar", 1, 1, 1)
+        multiply_b(1, 0)
+        multiply_r(2, 1, 1)
+        add_x1(2, 1, 1)
+        quantise_x2(0, 0)
+        multiply_r(2, 1, 0)
+        add_x1(2, 1, 0)
+        quantise_x2(1, 1)
+        interleave_x2("scalar", 2, 1, 1)
+        interleave_x2("scalar", 2, 1, 0)
+        multiply_r(2, 0, 0)
+        multiply_r(2, 0, 1)
+        add_x1(2, 0, 1)
+        add_x1(2, 0, 0)
+        quantise_x2(2, 1)
+        interleave_x2("vector", 2, 0, 0)
+        interleave_x2("scalar", 2, 0, 1)
+        multiply_b(1, 1)
+        multiply_b(0, 0)
+        multiply_b(1, 2)
+        finish(1, 0)
+        quantise_x2(2, 0)
+        finish(1, 1)
+        multiply_b(0, 1)
+        multiply_b(0, 2)
+        finish(0, 0)
+        finish(0, 1)

@@ -10,6 +10,7 @@ F32 = mybir.dt.float32
 BF16 = mybir.dt.bfloat16
 I32 = mybir.dt.int32
 U32 = mybir.dt.uint32
+U16 = mybir.dt.uint16
 U8 = mybir.dt.uint8
 FP8X4 = mybir.dt.float8_e4m3fn_x4
 FP4X4 = mybir.dt.float4_e2m1fn_x4
@@ -89,14 +90,14 @@ def tile_household_bracket_response_t2_kernel(
             width = E2M1_BYTES * K_PASS
             load_words(a_in[g], transfer_words[:, :, width * g : width * (g + 1)])
 
+        load_x(0, 0)
         load_a(0)
         load_scales(a_scales_in[0], transfer_scales[:, :, :K_PASS])
-        load_x(0, 0)
         load_x(1, 0)
         load_x(2, 0)
         load_x(0, 1)
-        load_scales(a_scales_in[1], transfer_scales[:, :, K_PASS:])
         load_a(1)
+        load_scales(a_scales_in[1], transfer_scales[:, :, K_PASS:])
         load_x(1, 1)
         load_x(2, 1)
         load_a(2)
@@ -138,25 +139,20 @@ def tile_household_bracket_response_t2_kernel(
         def flat(tile):
             return tile[:].rearrange("p c t -> p (c t)")
 
-        a_words = [kept([P, GROUPS, E2M1_BYTES * K_PASS], U8, f"a_words_{g}") for g in range(GROUPS)]
-        a_scales = [kept([P, GROUPS, K_PASS], U8, f"a_scales_{g}") for g in range(GROUPS)]
+        a_words = [kept([P, PACK, GROUPS, E2M1_BYTES * P], U8, f"a_words_{g}") for g in range(GROUPS)]
+        a_scales = [kept([P, PACK, GROUPS, P], U8, f"a_scales_{g}") for g in range(GROUPS)]
 
-        def reorder_a_words(g, pair):
-            tiles = slice(2 * pair, 2 * pair + 2)
+        def reorder_a(g, first, passes):
+            ks = slice(first, first + passes)
             nc.vector.tensor_copy(
-                out=a_words[g][:].rearrange("p k (t m b) -> p t k m b", t=PACK, b=E2M1_BYTES)[:, tiles, :, :, :],
-                in_=a_in[g][:].rearrange("p k (m t b) -> p t k m b", t=PACK, b=E2M1_BYTES)[:, tiles, :, :, :],
+                out=a_words[g][:, :, ks, :].bitcast(U16),
+                in_=a_in[g][:, ks, :].bitcast(U16).rearrange("p k (m t) -> p t k m", t=PACK),
             )
-
-        def reorder_a_scales(g):
             if g == 0:
-                scales_in = a_scales_in[0][:]
+                scales_in = a_scales_in[0][:, ks, :]
             else:
-                scales_in = a_scales_in[1][:, :, K_PASS * (g - 1) : K_PASS * g]
-            nc.vector.tensor_copy(
-                out=a_scales[g][:].rearrange("p k (t m) -> p t k m", t=PACK),
-                in_=scales_in.rearrange("p k (m t) -> p t k m", t=PACK),
-            )
+                scales_in = a_scales_in[1][:, ks, K_PASS * (g - 1) : K_PASS * g]
+            nc.vector.tensor_copy(out=a_scales[g][:, :, ks, :], in_=scales_in.rearrange("p k (m t) -> p t k m", t=PACK))
 
         xq = [kept([P, C], U32, f"xq_{g}") for g in range(GROUPS)]
         xq_scales = [kept([P, C], U8, f"xq_scales_{g}") for g in range(GROUPS)]
@@ -182,8 +178,8 @@ def tile_household_bracket_response_t2_kernel(
                 open_bank((1, g, half, t), [P, HALF])
             nc.tensor.matmul_mx(
                 out=open_banks[1, g, half, t][1][:],
-                lhsT=a_words[g][:, k, E2M1_BYTES * P * t : E2M1_BYTES * P * (t + 1)].bitcast(FP4X4),
-                lhsT_scale=a_scales[g][:, k, P * t : P * (t + 1)],
+                lhsT=a_words[g][:, t, k, :].bitcast(FP4X4),
+                lhsT_scale=a_scales[g][:, t, k, :],
                 rhs=xq[k][:, cols].bitcast(FP8X4),
                 rhs_scale=xq_scales[k][:, cols],
                 start=(k == 0),
@@ -300,149 +296,107 @@ def tile_household_bracket_response_t2_kernel(
                 nc.vector.tensor_tensor(out=response[:], in0=close_bank((3, half, j))[:], in1=rates[:, j, cols], op=MULT)
                 nc.sync.dma_start(out=out[P * j : P * (j + 1), cols], in_=response[:])
 
-        reorder_a_words(0, 0)
-        reorder_a_words(0, 1)
-        interleave_x("vector", 0, 0, 1)
-        reorder_a_scales(0)
-        interleave_x("vector", 1, 0, 1)
-        interleave_x("scalar", 0, 0, 0)
-        interleave_x("scalar", 1, 0, 0)
-        interleave_x("scalar", 2, 0, 1)
-        quantise_x(0, 0)
-        interleave_x("vector", 2, 0, 0)
-        quantise_x(1, 0)
-        interleave_x("vector", 0, 1, 0)
-        quantise_x(2, 0)
-        reorder_a_words(1, 0)
-        reorder_a_scales(1)
-        reorder_a_words(1, 1)
-        interleave_x("scalar", 0, 1, 1)
-        interleave_x("scalar", 1, 1, 0)
-        interleave_x("scalar", 1, 1, 1)
-        interleave_x("scalar", 2, 1, 0)
-        for k in range(GROUPS):
+        def both(step, *unit):
+            for pair in range(PACK // 2):
+                step(*unit, pair)
+
+        def multiply_a_by_pass(g, half, k):
             for t in range(PACK):
-                multiply_a_pass(0, 0, t, k)
-        add_x(0, 0, 1)
-        interleave_x("vector", 2, 1, 1)
+                multiply_a_pass(g, half, t, k)
+
+        def multiply_r_and_add(g, half):
+            for pair in range(PACK // 2):
+                multiply_r(g, half, pair)
+                add_x1(g, half, pair)
+
+        def multiply_a_and_add(g, half):
+            for pair in range(PACK // 2):
+                multiply_a(g, half, pair)
+                add_x(g, half, pair)
+
+        for g in range(GROUPS):
+            interleave_x("scalar", g, 0, 0)
+            interleave_x("vector", g, 0, 1)
+            reorder_a(0, g, 1)
+            quantise_x(g, 0)
+            multiply_a_by_pass(0, 0, g)
+        reorder_a(1, 0, GROUPS)
+        for g in range(GROUPS):
+            both(interleave_x, "scalar", g, 1)
+        both(multiply_a, 1, 0)
+        both(add_x, 0, 0)
         quantise_x(0, 1)
         quantise_x(1, 1)
+        both(add_x, 1, 0)
         quantise_x(2, 1)
-        multiply_a(1, 0, 0)
-        multiply_a(1, 0, 1)
-        add_x(1, 0, 1)
-        add_x(1, 0, 0)
-        add_x(0, 0, 0)
-        round_x1(1, 0, 1)
-        round_x1(1, 0, 0)
-        round_x1(0, 0, 0)
-        round_x1(0, 0, 1)
-        multiply_a(0, 1, 1)
-        multiply_a(0, 1, 0)
-        add_x(0, 1, 0)
-        reorder_a_words(2, 0)
-        reorder_a_scales(2)
-        add_x(0, 1, 1)
-        round_x1(0, 1, 0)
-        round_x1(0, 1, 1)
-        multiply_a(1, 1, 1)
-        multiply_a(1, 1, 0)
-        add_x(1, 1, 0)
-        add_x(1, 1, 1)
-        round_x1(1, 1, 0)
+        for k in range(GROUPS):
+            multiply_a_by_pass(0, 1, k)
+        both(round_x1, 0, 0)
+        both(round_x1, 1, 0)
+        reorder_a(2, 0, GROUPS)
+        both(add_x, 0, 1)
+        both(turn_x1, 0, 0)
+        both(regroup_x1, 0, 0)
+        both(round_x1, 0, 1)
+        multiply_a_and_add(1, 1)
+        both(turn_x1, 0, 1)
+        both(turn_x1, 1, 0)
+        both(regroup_x1, 0, 1)
+        both(regroup_x1, 1, 0)
+        both(round_x1, 1, 1)
+        quantise_x1(0, 0)
         multiply_a(2, 0, 0)
         add_x(2, 0, 0)
-        reorder_a_words(2, 1)
-        turn_x1(1, 0, 1)
-        turn_x1(0, 1, 0)
-        turn_x1(0, 0, 1)
-        regroup_x1(0, 0, 1)
-        regroup_x1(0, 1, 0)
-        turn_x1(0, 1, 1)
-        turn_x1(1, 0, 0)
-        turn_x1(0, 0, 0)
-        regroup_x1(0, 0, 0)
-        regroup_x1(1, 0, 0)
-        regroup_x1(1, 0, 1)
-        regroup_x1(0, 1, 1)
-        round_x1(1, 1, 1)
-        round_x1(2, 0, 0)
-        multiply_a(2, 1, 0)
-        quantise_x1(0, 0)
-        add_x(2, 1, 0)
-        quantise_x1(1, 0)
-        round_x1(2, 1, 0)
-        multiply_a(2, 1, 1)
-        add_x(2, 1, 1)
         quantise_x1(0, 1)
-        turn_x1(1, 1, 0)
-        regroup_x1(1, 1, 0)
-        turn_x1(1, 1, 1)
-        regroup_x1(1, 1, 1)
         multiply_a(2, 0, 1)
         add_x(2, 0, 1)
-        round_x1(2, 0, 1)
-        round_x1(2, 1, 1)
-        multiply_r(0, 1, 1)
-        add_x1(0, 1, 1)
+        quantise_x1(1, 0)
+        multiply_r_and_add(0, 0)
+        both(turn_x1, 1, 1)
+        both(round_x1, 2, 0)
+        both(regroup_x1, 1, 1)
+        both(interleave_x2, "scalar", 0, 0)
+        multiply_a(2, 1, 0)
+        add_x(2, 1, 0)
         quantise_x1(1, 1)
-        multiply_r(0, 1, 0)
-        add_x1(0, 1, 0)
-        turn_x1(2, 0, 1)
-        regroup_x1(2, 0, 1)
-        interleave_x2("scalar", 0, 1, 0)
-        interleave_x2("scalar", 0, 1, 1)
-        turn_x1(2, 0, 0)
-        multiply_r(1, 0, 0)
-        add_x1(1, 0, 0)
-        multiply_r(1, 0, 1)
-        add_x1(1, 0, 1)
-        interleave_x2("scalar", 1, 0, 0)
-        interleave_x2("scalar", 1, 0, 1)
-        multiply_r(0, 0, 0)
-        add_x1(0, 0, 0)
-        quantise_x2(0, 1)
-        multiply_r(1, 1, 1)
-        add_x1(1, 1, 1)
-        multiply_r(0, 0, 1)
-        add_x1(0, 0, 1)
-        quantise_x2(1, 0)
-        turn_x1(2, 1, 1)
-        regroup_x1(2, 1, 1)
-        turn_x1(2, 1, 0)
-        regroup_x1(2, 1, 0)
-        regroup_x1(2, 0, 0)
-        interleave_x2("scalar", 0, 0, 0)
-        interleave_x2("scalar", 0, 0, 1)
-        multiply_r(1, 1, 0)
-        quantise_x1(2, 1)
-        quantise_x1(2, 0)
-        add_x1(1, 1, 0)
-        interleave_x2("scalar", 1, 1, 0)
-        interleave_x2("scalar", 1, 1, 1)
-        multiply_b(1, 0)
-        multiply_r(2, 1, 1)
-        add_x1(2, 1, 1)
+        multiply_a(2, 1, 1)
+        add_x(2, 1, 1)
+        both(round_x1, 2, 1)
+        multiply_r_and_add(1, 0)
         quantise_x2(0, 0)
-        multiply_r(2, 1, 0)
-        add_x1(2, 1, 0)
-        quantise_x2(1, 1)
-        interleave_x2("scalar", 2, 1, 1)
-        interleave_x2("scalar", 2, 1, 0)
+        both(turn_x1, 2, 0)
+        both(turn_x1, 2, 1)
+        both(regroup_x1, 2, 0)
+        both(regroup_x1, 2, 1)
+        both(interleave_x2, "scalar", 1, 0)
+        multiply_r_and_add(0, 1)
+        quantise_x1(2, 0)
+        quantise_x1(2, 1)
+        both(interleave_x2, "scalar", 0, 1)
+        multiply_b(0, 0)
         multiply_r(2, 0, 0)
+        add_x1(2, 0, 0)
+        quantise_x2(1, 0)
         multiply_r(2, 0, 1)
         add_x1(2, 0, 1)
-        add_x1(2, 0, 0)
-        quantise_x2(2, 1)
-        interleave_x2("vector", 2, 0, 0)
-        interleave_x2("scalar", 2, 0, 1)
-        multiply_b(1, 1)
-        multiply_b(0, 0)
-        multiply_b(1, 2)
-        finish(1, 0)
-        quantise_x2(2, 0)
-        finish(1, 1)
+        both(interleave_x2, "scalar", 2, 0)
+        multiply_r_and_add(1, 1)
+        quantise_x2(0, 1)
         multiply_b(0, 1)
+        both(interleave_x2, "scalar", 1, 1)
+        multiply_r(2, 1, 0)
+        add_x1(2, 1, 0)
+        quantise_x2(2, 0)
+        multiply_r(2, 1, 1)
+        add_x1(2, 1, 1)
         multiply_b(0, 2)
+        interleave_x2("scalar", 2, 1, 0)
+        quantise_x2(1, 1)
+        interleave_x2("vector", 2, 1, 1)
+        multiply_b(1, 0)
+        multiply_b(1, 1)
         finish(0, 0)
+        quantise_x2(2, 1)
         finish(0, 1)
+        multiply_b(1, 2)
+        both(finish, 1)

@@ -24,6 +24,7 @@ GROUPS = H // K_PASS
 HALVES = C // K_PASS
 HALF = K_PASS
 PART = HALF // 2
+RUN = 4
 OUT_TILES = G // P
 BANKS = 8
 E2M1_BYTES = 2
@@ -136,6 +137,13 @@ def tile_household_bracket_response_t2_kernel(
             else:
                 nc.scalar.copy(out=out_ap, in_=in_ap)
 
+        def interleave(engine, grouped, tiles):
+            copy(
+                engine,
+                grouped.rearrange("p (c i) t -> p c t i", i=RUN),
+                tiles.rearrange("p t (c i) -> p c t i", i=RUN),
+            )
+
         def flat(tile):
             return tile[:].rearrange("p c t -> p (c t)")
 
@@ -160,7 +168,7 @@ def tile_household_bracket_response_t2_kernel(
         def interleave_x(engine, g, half, part):
             grouped = stage("x_grouped", (g, half), [P, HALF, PACK], 3)
             cols = slice(PART * part, PART * (part + 1))
-            copy(engine, grouped[:, cols, :], x_in[g][half][:, :, cols].rearrange("p t c -> p c t"))
+            interleave(engine, grouped[:, cols, :], x_in[g][half][:, :, cols])
 
         def quantise_x(g, half):
             cols = slice(HALF * half, HALF * (half + 1))
@@ -264,7 +272,7 @@ def tile_household_bracket_response_t2_kernel(
         def interleave_x2(engine, g, half, part):
             grouped = stage("x2_grouped", (g, half), [P, HALF, PACK], 2)
             cols = slice(PART * part, PART * (part + 1))
-            copy(engine, grouped[:, cols, :], staged["x2", (g, half)][:, :, cols].rearrange("p t c -> p c t"))
+            interleave(engine, grouped[:, cols, :], staged["x2", (g, half)][:, :, cols])
 
         def quantise_x2(g, half):
             cols = slice(HALF * half, HALF * (half + 1))

@@ -57,9 +57,9 @@ def tile_household_bracket_response_t2_kernel(
         r_scales = kept([P, HALVES, C], U8, "r_scales")
         b_scales = kept([P, GROUPS, G], U8, "b_scales")
         nc.vector.memset(a_scales_in[0][:].bitcast(I32), 0)
-        nc.gpsimd.memset(a_scales_in[1][:].bitcast(I32), 0)
-        nc.gpsimd.memset(r_scales[:].bitcast(I32), 0)
-        nc.gpsimd.memset(b_scales[:].bitcast(I32), 0)
+        nc.vector.memset(a_scales_in[1][:].bitcast(I32), 0)
+        nc.vector.memset(r_scales[:].bitcast(I32), 0)
+        nc.vector.memset(b_scales[:].bitcast(I32), 0)
         identity = kept([P, P], F32, "identity")
         make_identity(nc, identity[:])
 
@@ -72,7 +72,7 @@ def tile_household_bracket_response_t2_kernel(
                 )
 
         def load_words(tile, words):
-            nc.sync.dma_start(out=tile[:].bitcast(I32), in_=words.rearrange("k p n -> p k n").bitcast(I32))
+            nc.sync.dma_start(out=tile.bitcast(I32), in_=words.rearrange("k p n -> p k n").bitcast(I32))
 
         x_in = [[kept([P, PACK, HALF], BF16, f"x_{g}_{half}") for half in range(HALVES)] for g in range(GROUPS)]
         a_in = [kept([P, GROUPS, E2M1_BYTES * K_PASS], U8, f"a_in_{g}") for g in range(GROUPS)]
@@ -87,26 +87,27 @@ def tile_household_bracket_response_t2_kernel(
                 in_=x[K_PASS * g : K_PASS * (g + 1), HALF * half : HALF * (half + 1)].rearrange("(p t) c -> p t c", t=PACK),
             )
 
-        def load_a(g):
+        def load_a(g, ks=slice(None)):
             width = E2M1_BYTES * K_PASS
-            load_words(a_in[g], transfer_words[:, :, width * g : width * (g + 1)])
+            load_words(a_in[g][:, ks, :], transfer_words[ks, :, width * g : width * (g + 1)])
 
-        load_x(0, 0)
-        load_a(0)
+        load_a(0, slice(0, 1))
         load_scales(a_scales_in[0], transfer_scales[:, :, :K_PASS])
+        load_x(0, 0)
         load_x(1, 0)
+        load_a(0, slice(1, GROUPS))
         load_x(2, 0)
-        load_x(0, 1)
         load_a(1)
         load_scales(a_scales_in[1], transfer_scales[:, :, K_PASS:])
+        load_x(0, 1)
+        load_a(2)
         load_x(1, 1)
         load_x(2, 1)
-        load_a(2)
         load_scales(r_scales, reclass_scales)
-        load_words(r_words, reclass_words)
+        load_words(r_words[:], reclass_words)
         nc.sync.dma_start(out=prop[:], in_=propensity.rearrange("(g p t) -> p g t", p=P, t=PACK))
         load_scales(b_scales, bracket_scales)
-        load_words(b_words, bracket_words)
+        load_words(b_words[:], bracket_words)
         nc.sync.dma_start(out=rates[:], in_=rate.rearrange("(j p) c -> p j c", p=P))
 
         closed_banks = list(range(BANKS))
@@ -150,17 +151,22 @@ def tile_household_bracket_response_t2_kernel(
         a_words = [kept([P, PACK, GROUPS, E2M1_BYTES * P], U8, f"a_words_{g}") for g in range(GROUPS)]
         a_scales = [kept([P, PACK, GROUPS, P], U8, f"a_scales_{g}") for g in range(GROUPS)]
 
-        def reorder_a(g, first, passes):
-            ks = slice(first, first + passes)
+        def reorder_a_words(g, ks=slice(None)):
             nc.vector.tensor_copy(
                 out=a_words[g][:, :, ks, :].bitcast(U16),
                 in_=a_in[g][:, ks, :].bitcast(U16).rearrange("p k (m t) -> p t k m", t=PACK),
             )
+
+        def reorder_a_scales(g, ks=slice(None)):
             if g == 0:
                 scales_in = a_scales_in[0][:, ks, :]
             else:
                 scales_in = a_scales_in[1][:, ks, K_PASS * (g - 1) : K_PASS * g]
             nc.vector.tensor_copy(out=a_scales[g][:, :, ks, :], in_=scales_in.rearrange("p k (m t) -> p t k m", t=PACK))
+
+        def reorder_a(g, first, passes):
+            reorder_a_words(g, slice(first, first + passes))
+            reorder_a_scales(g, slice(first, first + passes))
 
         xq = [kept([P, C], U32, f"xq_{g}") for g in range(GROUPS)]
         xq_scales = [kept([P, C], U8, f"xq_scales_{g}") for g in range(GROUPS)]
@@ -211,11 +217,15 @@ def tile_household_bracket_response_t2_kernel(
         x1q = [[kept([P, K_PASS], U32, f"x1q_{g}_{half}") for half in range(HALVES)] for g in range(GROUPS)]
         x1q_scales = [[kept([P, K_PASS], U8, f"x1q_scales_{g}_{half}") for half in range(HALVES)] for g in range(GROUPS)]
 
-        def round_x1(g, half, pair):
+        def round_x1(engine, g, half, pair):
             rounded = stage("x1_rounded", (g, half), [P, PACK, 2, P, 2], 4)
             for t in (2 * pair, 2 * pair + 1):
                 row = x1[g][:, t, HALF * half : HALF * (half + 1)]
-                nc.scalar.copy(out=rounded[:, t, :, :, :], in_=row.rearrange("p (w u e) -> p u w e", u=2, e=2))
+                source = row.rearrange("p (w u e) -> p u w e", u=2, e=2)
+                if engine == "gpsimd":
+                    nc.gpsimd.tensor_scalar(out=rounded[:, t, :, :, :], in0=source, scalar1=1.0, scalar2=0.0, op0=MULT, op1=ADD)
+                else:
+                    nc.scalar.copy(out=rounded[:, t, :, :, :], in_=source)
 
         def turn_x1(g, half, pair):
             rounded = staged["x1_rounded", (g, half)]
@@ -240,28 +250,35 @@ def tile_household_bracket_response_t2_kernel(
                 in_=flat(staged["x1_grouped", (g, half)]),
             )
 
-        def multiply_r(g, half, pair):
+        def multiply_r(g, span, pair):
+            first, width = span
             for t in (2 * pair, 2 * pair + 1):
-                acc = open_bank((2, g, half, t), [P, HALF])
+                slot = t % (HALF // width)
+                if slot == 0:
+                    acc = open_bank((2, g, span, t), [P, HALF // width, width])
                 for k in range(HALVES):
                     nc.tensor.matmul_mx(
-                        out=acc[:],
+                        out=acc[:, slot, :],
                         lhsT=x1q[g][k][:, P * t : P * (t + 1)].bitcast(FP8X4),
                         lhsT_scale=x1q_scales[g][k][:, P * t : P * (t + 1)],
-                        rhs=r_words[:, k, E2M1_BYTES * HALF * half : E2M1_BYTES * HALF * (half + 1)].bitcast(FP4X4),
-                        rhs_scale=r_scales[:, k, HALF * half : HALF * (half + 1)],
+                        rhs=r_words[:, k, E2M1_BYTES * first : E2M1_BYTES * (first + width)].bitcast(FP4X4),
+                        rhs_scale=r_scales[:, k, first : first + width],
                         start=(k == 0),
                         stop=(k == HALVES - 1),
                     )
 
-        def add_x1(g, half, pair):
-            x2 = stage("x2", (g, half), [P, PACK, HALF], 3)
+        def add_x1(g, span, pair):
+            first, width = span
+            x2 = stage("x2", (g, span), [P, PACK, width], 3)
             for t in (2 * pair, 2 * pair + 1):
+                slot = t % (HALF // width)
+                if slot == 0:
+                    acc = close_bank((2, g, span, t))
                 nc.vector.scalar_tensor_tensor(
                     out=x2[:, t, :],
-                    in0=close_bank((2, g, half, t))[:],
+                    in0=acc[:, slot, :],
                     scalar=prop[:, g, t : t + 1],
-                    in1=x1[g][:, t, HALF * half : HALF * (half + 1)],
+                    in1=x1[g][:, t, first : first + width],
                     op0=MULT,
                     op1=ADD,
                 )
@@ -269,142 +286,159 @@ def tile_household_bracket_response_t2_kernel(
         x2q = [kept([P, C], U32, f"x2q_{g}") for g in range(GROUPS)]
         x2q_scales = [kept([P, C], U8, f"x2q_scales_{g}") for g in range(GROUPS)]
 
-        def interleave_x2(engine, g, half, part):
-            grouped = stage("x2_grouped", (g, half), [P, HALF, PACK], 2)
-            cols = slice(PART * part, PART * (part + 1))
-            interleave(engine, grouped[:, cols, :], staged["x2", (g, half)][:, :, cols])
+        def interleave_x2(engine, g, span, cols):
+            grouped = stage("x2_grouped", (g, span), [P, span[1], PACK], 2)
+            interleave(engine, grouped[:, cols, :], staged["x2", (g, span)][:, :, cols])
 
-        def quantise_x2(g, half):
-            cols = slice(HALF * half, HALF * (half + 1))
+        def quantise_x2(g, span):
+            cols = slice(span[0], span[0] + span[1])
             nc.vector.quantize_mx(
                 out=x2q[g][:, cols].bitcast(FP8X4),
                 scales=x2q_scales[g][:, cols],
-                in_=flat(staged["x2_grouped", (g, half)]),
+                in_=flat(staged["x2_grouped", (g, span)]),
             )
 
-        def multiply_b(half, k):
-            cols = slice(HALF * half, HALF * (half + 1))
+        def multiply_b(span, k):
+            first, width = span
+            cols = slice(first, first + width)
+            shared = HALF // width
             for j in range(OUT_TILES):
-                if k == 0:
-                    open_bank((3, half, j), [P, HALF])
+                slot = j % shared
+                if k == 0 and slot == 0:
+                    open_bank((3, span, j), [P, shared, width])
                 nc.tensor.matmul_mx(
-                    out=open_banks[3, half, j][1][:],
+                    out=open_banks[3, span, j - slot][1][:, slot, :],
                     lhsT=b_words[:, k, E2M1_BYTES * P * j : E2M1_BYTES * P * (j + 1)].bitcast(FP4X4),
                     lhsT_scale=b_scales[:, k, P * j : P * (j + 1)],
                     rhs=x2q[k][:, cols].bitcast(FP8X4),
                     rhs_scale=x2q_scales[k][:, cols],
-                    start=(k == 0),
-                    stop=(k == GROUPS - 1),
+                    start=(k == 0 and slot == 0),
+                    stop=(k == GROUPS - 1 and slot == shared - 1),
                 )
 
-        def finish(half, pair):
-            cols = slice(HALF * half, HALF * (half + 1))
-            for j in (2 * pair, 2 * pair + 1):
-                response = work.tile([P, HALF], F32, name="response", bufs=7)
-                nc.vector.tensor_tensor(out=response[:], in0=close_bank((3, half, j))[:], in1=rates[:, j, cols], op=MULT)
-                nc.sync.dma_start(out=out[P * j : P * (j + 1), cols], in_=response[:])
+        def finish(span):
+            first, width = span
+            cols = slice(first, first + width)
+            shared = HALF // width
+            for j in range(0, OUT_TILES, shared):
+                response = work.tile([P, shared, width], F32, name="response", bufs=7)
+                nc.vector.tensor_tensor(
+                    out=response[:], in0=close_bank((3, span, j))[:], in1=rates[:, j : j + shared, cols], op=MULT
+                )
+                rows = out[P * j : P * (j + shared), cols].rearrange("(j p) c -> p j c", p=P)
+                nc.sync.dma_start(out=rows, in_=response[:])
 
         def both(step, *unit):
             for pair in range(PACK // 2):
                 step(*unit, pair)
 
+        def round_unit(g, half):
+            round_x1("gpsimd", g, half, 0)
+            round_x1("scalar", g, half, 1)
+
         def multiply_a_by_pass(g, half, k):
             for t in range(PACK):
                 multiply_a_pass(g, half, t, k)
 
-        def multiply_r_and_add(g, half):
+        def multiply_r_and_add(g, span):
             for pair in range(PACK // 2):
-                multiply_r(g, half, pair)
-                add_x1(g, half, pair)
+                multiply_r(g, span, pair)
+                add_x1(g, span, pair)
 
         def multiply_a_and_add(g, half):
             for pair in range(PACK // 2):
                 multiply_a(g, half, pair)
                 add_x(g, half, pair)
 
+        left, right = (0, HALF), (HALF, HALF)
+        third, fourth = (HALF, PART), (HALF + PART, PART)
+        whole = slice(None)
+
+        reorder_a_words(0, slice(0, 1))
+        reorder_a_scales(0)
         for g in range(GROUPS):
             interleave_x("scalar", g, 0, 0)
             interleave_x("vector", g, 0, 1)
-            reorder_a(0, g, 1)
+            if g == 1:
+                reorder_a_words(0, slice(1, GROUPS))
+            if g == 2:
+                reorder_a_words(1)
             quantise_x(g, 0)
             multiply_a_by_pass(0, 0, g)
-        reorder_a(1, 0, GROUPS)
+        reorder_a_scales(1)
         for g in range(GROUPS):
             both(interleave_x, "scalar", g, 1)
         both(multiply_a, 1, 0)
         both(add_x, 0, 0)
+        round_unit(0, 0)
+        reorder_a(2, 0, GROUPS)
+        both(multiply_a, 2, 0)
+        both(add_x, 1, 0)
+        round_unit(1, 0)
         quantise_x(0, 1)
         quantise_x(1, 1)
-        both(add_x, 1, 0)
+        add_x(2, 0, 0)
         quantise_x(2, 1)
+        add_x(2, 0, 1)
+        round_unit(2, 0)
         for k in range(GROUPS):
             multiply_a_by_pass(0, 1, k)
-        both(round_x1, 0, 0)
-        both(round_x1, 1, 0)
-        reorder_a(2, 0, GROUPS)
         both(add_x, 0, 1)
         both(turn_x1, 0, 0)
+        both(turn_x1, 1, 0)
         both(regroup_x1, 0, 0)
-        both(round_x1, 0, 1)
+        round_unit(0, 1)
+        both(regroup_x1, 1, 0)
         multiply_a_and_add(1, 1)
         both(turn_x1, 0, 1)
-        both(turn_x1, 1, 0)
+        both(turn_x1, 2, 0)
         both(regroup_x1, 0, 1)
-        both(regroup_x1, 1, 0)
-        both(round_x1, 1, 1)
+        round_unit(1, 1)
+        both(regroup_x1, 2, 0)
         quantise_x1(0, 0)
-        multiply_a(2, 0, 0)
-        add_x(2, 0, 0)
-        quantise_x1(0, 1)
-        multiply_a(2, 0, 1)
-        add_x(2, 0, 1)
         quantise_x1(1, 0)
-        multiply_r_and_add(0, 0)
-        both(turn_x1, 1, 1)
-        both(round_x1, 2, 0)
-        both(regroup_x1, 1, 1)
-        both(interleave_x2, "scalar", 0, 0)
         multiply_a(2, 1, 0)
         add_x(2, 1, 0)
-        quantise_x1(1, 1)
+        quantise_x1(0, 1)
         multiply_a(2, 1, 1)
         add_x(2, 1, 1)
-        both(round_x1, 2, 1)
-        multiply_r_and_add(1, 0)
-        quantise_x2(0, 0)
-        both(turn_x1, 2, 0)
-        both(turn_x1, 2, 1)
-        both(regroup_x1, 2, 0)
-        both(regroup_x1, 2, 1)
-        both(interleave_x2, "scalar", 1, 0)
-        multiply_r_and_add(0, 1)
+        both(turn_x1, 1, 1)
+        both(regroup_x1, 1, 1)
+        round_unit(2, 1)
         quantise_x1(2, 0)
+        multiply_r(0, left, 0)
+        add_x1(0, left, 0)
+        quantise_x1(1, 1)
+        multiply_r(0, left, 1)
+        add_x1(0, left, 1)
+        both(turn_x1, 2, 1)
+        both(regroup_x1, 2, 1)
+        interleave_x2("scalar", 0, left, whole)
+        multiply_r(1, left, 0)
+        add_x1(1, left, 0)
         quantise_x1(2, 1)
-        both(interleave_x2, "scalar", 0, 1)
-        multiply_b(0, 0)
-        multiply_r(2, 0, 0)
-        add_x1(2, 0, 0)
-        quantise_x2(1, 0)
-        multiply_r(2, 0, 1)
-        add_x1(2, 0, 1)
-        both(interleave_x2, "scalar", 2, 0)
-        multiply_r_and_add(1, 1)
-        quantise_x2(0, 1)
-        multiply_b(0, 1)
-        both(interleave_x2, "scalar", 1, 1)
-        multiply_r(2, 1, 0)
-        add_x1(2, 1, 0)
-        quantise_x2(2, 0)
-        multiply_r(2, 1, 1)
-        add_x1(2, 1, 1)
-        multiply_b(0, 2)
-        interleave_x2("scalar", 2, 1, 0)
-        quantise_x2(1, 1)
-        interleave_x2("vector", 2, 1, 1)
-        multiply_b(1, 0)
-        multiply_b(1, 1)
-        finish(0, 0)
-        quantise_x2(2, 1)
-        finish(0, 1)
-        multiply_b(1, 2)
-        both(finish, 1)
+        multiply_r(1, left, 1)
+        add_x1(1, left, 1)
+        interleave_x2("scalar", 1, left, whole)
+        quantise_x2(0, left)
+        multiply_r_and_add(2, left)
+        interleave_x2("scalar", 2, left, whole)
+        multiply_b(left, 0)
+        quantise_x2(1, left)
+        multiply_r_and_add(0, right)
+        interleave_x2("scalar", 0, right, whole)
+        multiply_b(left, 1)
+        quantise_x2(2, left)
+        multiply_r_and_add(1, right)
+        interleave_x2("scalar", 1, right, whole)
+        multiply_b(left, 2)
+        quantise_x2(0, right)
+        multiply_r_and_add(2, right)
+        interleave_x2("scalar", 2, right, whole)
+        quantise_x2(1, right)
+        multiply_b(right, 0)
+        multiply_b(right, 1)
+        finish(left)
+        quantise_x2(2, right)
+        multiply_b(right, 2)
+        finish(right)

@@ -24,6 +24,8 @@ GROUPS = H // K_PASS
 HALVES = C // K_PASS
 HALF = K_PASS
 PART = HALF // 2
+HEAD_SHARE = 192
+GPSIMD_SHARE = 224
 RUN = 4
 OUT_TILES = G // P
 BANKS = 8
@@ -135,6 +137,8 @@ def tile_household_bracket_response_t2_kernel(
         def copy(engine, out_ap, in_ap):
             if engine == "vector":
                 nc.vector.tensor_copy(out=out_ap, in_=in_ap)
+            elif engine == "gpsimd":
+                nc.gpsimd.tensor_scalar(out=out_ap, in0=in_ap, scalar1=1.0, scalar2=0.0, op0=MULT, op1=ADD)
             else:
                 nc.scalar.copy(out=out_ap, in_=in_ap)
 
@@ -171,9 +175,8 @@ def tile_household_bracket_response_t2_kernel(
         xq = [kept([P, C], U32, f"xq_{g}") for g in range(GROUPS)]
         xq_scales = [kept([P, C], U8, f"xq_scales_{g}") for g in range(GROUPS)]
 
-        def interleave_x(engine, g, half, part):
+        def interleave_x(engine, g, half, cols):
             grouped = stage("x_grouped", (g, half), [P, HALF, PACK], 3)
-            cols = slice(PART * part, PART * (part + 1))
             interleave(engine, grouped[:, cols, :], x_in[g][half][:, :, cols])
 
         def quantise_x(g, half):
@@ -221,11 +224,7 @@ def tile_household_bracket_response_t2_kernel(
             rounded = stage("x1_rounded", (g, half), [P, PACK, 2, P, 2], 4)
             for t in (2 * pair, 2 * pair + 1):
                 row = x1[g][:, t, HALF * half : HALF * (half + 1)]
-                source = row.rearrange("p (w u e) -> p u w e", u=2, e=2)
-                if engine == "gpsimd":
-                    nc.gpsimd.tensor_scalar(out=rounded[:, t, :, :, :], in0=source, scalar1=1.0, scalar2=0.0, op0=MULT, op1=ADD)
-                else:
-                    nc.scalar.copy(out=rounded[:, t, :, :, :], in_=source)
+                copy(engine, rounded[:, t, :, :, :], row.rearrange("p (w u e) -> p u w e", u=2, e=2))
 
         def turn_x1(g, half, pair):
             rounded = staged["x1_rounded", (g, half)]
@@ -267,10 +266,10 @@ def tile_household_bracket_response_t2_kernel(
                         stop=(k == HALVES - 1),
                     )
 
-        def add_x1(g, span, pair):
+        def add_x1(g, span, tiles):
             first, width = span
             x2 = stage("x2", (g, span), [P, PACK, width], 3)
-            for t in (2 * pair, 2 * pair + 1):
+            for t in tiles:
                 slot = t % (HALF // width)
                 if slot == 0:
                     acc = close_bank((2, g, span, t))
@@ -316,11 +315,11 @@ def tile_household_bracket_response_t2_kernel(
                     stop=(k == GROUPS - 1 and slot == shared - 1),
                 )
 
-        def finish(span):
+        def finish(span, banks):
             first, width = span
             cols = slice(first, first + width)
             shared = HALF // width
-            for j in range(0, OUT_TILES, shared):
+            for j in range(0, OUT_TILES, shared)[banks]:
                 response = work.tile([P, shared, width], F32, name="response", bufs=7)
                 nc.vector.tensor_tensor(
                     out=response[:], in0=close_bank((3, span, j))[:], in1=rates[:, j : j + shared, cols], op=MULT
@@ -336,14 +335,13 @@ def tile_household_bracket_response_t2_kernel(
             round_x1("gpsimd", g, half, 0)
             round_x1("scalar", g, half, 1)
 
+        def interleave_x2_unit(g, span):
+            interleave_x2("gpsimd", g, span, slice(0, GPSIMD_SHARE))
+            interleave_x2("scalar", g, span, slice(GPSIMD_SHARE, HALF))
+
         def multiply_a_by_pass(g, half, k):
             for t in range(PACK):
                 multiply_a_pass(g, half, t, k)
-
-        def multiply_r_and_add(g, span):
-            for pair in range(PACK // 2):
-                multiply_r(g, span, pair)
-                add_x1(g, span, pair)
 
         def multiply_a_and_add(g, half):
             for pair in range(PACK // 2):
@@ -353,25 +351,29 @@ def tile_household_bracket_response_t2_kernel(
         left, right = (0, HALF), (HALF, HALF)
         third, fourth = (HALF, PART), (HALF + PART, PART)
         whole = slice(None)
+        tiles = range(PACK)
 
         reorder_a_words(0, slice(0, 1))
         reorder_a_scales(0)
         for g in range(GROUPS):
-            interleave_x("scalar", g, 0, 0)
-            interleave_x("vector", g, 0, 1)
+            share = HEAD_SHARE if g == 0 else PART
+            interleave_x("scalar", g, 0, slice(0, share))
+            interleave_x("vector", g, 0, slice(share, HALF))
             if g == 1:
                 reorder_a_words(0, slice(1, GROUPS))
             if g == 2:
-                reorder_a_words(1)
+                reorder_a_words(1, slice(0, 1))
             quantise_x(g, 0)
             multiply_a_by_pass(0, 0, g)
+        reorder_a_words(1, slice(1, GROUPS))
         reorder_a_scales(1)
+        reorder_a_scales(2)
+        reorder_a_words(2)
         for g in range(GROUPS):
-            both(interleave_x, "scalar", g, 1)
+            interleave_x("scalar", g, 1, whole)
         both(multiply_a, 1, 0)
         both(add_x, 0, 0)
         round_unit(0, 0)
-        reorder_a(2, 0, GROUPS)
         both(multiply_a, 2, 0)
         both(add_x, 1, 0)
         round_unit(1, 0)
@@ -389,56 +391,63 @@ def tile_household_bracket_response_t2_kernel(
         both(regroup_x1, 0, 0)
         round_unit(0, 1)
         both(regroup_x1, 1, 0)
-        multiply_a_and_add(1, 1)
+        quantise_x1(0, 0)
+        multiply_a(1, 1, 0)
+        add_x(1, 1, 0)
+        round_x1("gpsimd", 1, 1, 0)
         both(turn_x1, 0, 1)
         both(turn_x1, 2, 0)
         both(regroup_x1, 0, 1)
-        round_unit(1, 1)
         both(regroup_x1, 2, 0)
-        quantise_x1(0, 0)
         quantise_x1(1, 0)
-        multiply_a(2, 1, 0)
-        add_x(2, 1, 0)
+        multiply_a(1, 1, 1)
         quantise_x1(0, 1)
-        multiply_a(2, 1, 1)
-        add_x(2, 1, 1)
+        add_x(1, 1, 1)
+        round_x1("scalar", 1, 1, 1)
+        both(multiply_r, 0, left)
+        add_x1(0, left, tiles)
         both(turn_x1, 1, 1)
         both(regroup_x1, 1, 1)
-        round_unit(2, 1)
+        interleave_x2("scalar", 0, left, whole)
         quantise_x1(2, 0)
-        multiply_r(0, left, 0)
-        add_x1(0, left, 0)
+        multiply_a(2, 1, 0)
+        add_x(2, 1, 0)
+        multiply_a(2, 1, 1)
         quantise_x1(1, 1)
-        multiply_r(0, left, 1)
-        add_x1(0, left, 1)
+        add_x(2, 1, 1)
+        round_unit(2, 1)
+        both(multiply_r, 1, left)
+        add_x1(1, left, tiles)
         both(turn_x1, 2, 1)
         both(regroup_x1, 2, 1)
-        interleave_x2("scalar", 0, left, whole)
-        multiply_r(1, left, 0)
-        add_x1(1, left, 0)
-        quantise_x1(2, 1)
-        multiply_r(1, left, 1)
-        add_x1(1, left, 1)
         interleave_x2("scalar", 1, left, whole)
         quantise_x2(0, left)
-        multiply_r_and_add(2, left)
-        interleave_x2("scalar", 2, left, whole)
-        multiply_b(left, 0)
-        quantise_x2(1, left)
-        multiply_r_and_add(0, right)
+        both(multiply_r, 0, right)
+        add_x1(0, right, tiles[:1])
+        quantise_x1(2, 1)
+        add_x1(0, right, tiles[1:])
         interleave_x2("scalar", 0, right, whole)
-        multiply_b(left, 1)
-        quantise_x2(2, left)
-        multiply_r_and_add(1, right)
+        both(multiply_r, 2, left)
+        quantise_x2(1, left)
+        add_x1(2, left, tiles)
+        interleave_x2("scalar", 2, left, whole)
+        both(multiply_r, 1, right)
+        add_x1(1, right, tiles)
         interleave_x2("scalar", 1, right, whole)
-        multiply_b(left, 2)
+        multiply_b(left, 0)
+        multiply_b(left, 1)
         quantise_x2(0, right)
-        multiply_r_and_add(2, right)
-        interleave_x2("scalar", 2, right, whole)
+        quantise_x2(2, left)
+        both(multiply_r, 2, right)
+        multiply_b(left, 2)
+        add_x1(2, right, tiles[:3])
         quantise_x2(1, right)
+        add_x1(2, right, tiles[3:])
+        interleave_x2_unit(2, right)
         multiply_b(right, 0)
         multiply_b(right, 1)
-        finish(left)
+        finish(left, slice(0, 3))
         quantise_x2(2, right)
+        finish(left, slice(3, 4))
         multiply_b(right, 2)
-        finish(right)
+        finish(right, whole)

@@ -157,8 +157,8 @@ def tile_household_bracket_response_t2_kernel(
 
         def reorder_a_words(g, ks=slice(None)):
             nc.vector.tensor_copy(
-                out=a_words[g][:, :, ks, :].bitcast(U16),
-                in_=a_in[g][:, ks, :].bitcast(U16).rearrange("p k (m t) -> p t k m", t=PACK),
+                out=a_words[g][:, :, ks, :].bitcast(U16).rearrange("p t k (m i) -> p k m t i", i=RUN),
+                in_=a_in[g][:, ks, :].bitcast(U16).rearrange("p k (m i t) -> p k m t i", i=RUN, t=PACK),
             )
 
         def reorder_a_scales(g, ks=slice(None)):

@@ -375,13 +375,12 @@ def tile_household_bracket_response_t2_kernel(
         both(add_x, 0, 0)
         round_unit(0, 0)
         both(multiply_a, 2, 0)
+        quantise_x(0, 1)
         both(add_x, 1, 0)
         round_unit(1, 0)
-        quantise_x(0, 1)
         quantise_x(1, 1)
-        add_x(2, 0, 0)
         quantise_x(2, 1)
-        add_x(2, 0, 1)
+        both(add_x, 2, 0)
         round_unit(2, 0)
         for k in range(GROUPS):
             multiply_a_by_pass(0, 1, k)
@@ -394,56 +393,53 @@ def tile_household_bracket_response_t2_kernel(
         quantise_x1(0, 0)
         multiply_a(1, 1, 0)
         add_x(1, 1, 0)
-        round_x1("gpsimd", 1, 1, 0)
         both(turn_x1, 0, 1)
         both(turn_x1, 2, 0)
         both(regroup_x1, 0, 1)
         both(regroup_x1, 2, 0)
+        round_x1("scalar", 1, 1, 0)
         quantise_x1(1, 0)
         multiply_a(1, 1, 1)
         quantise_x1(0, 1)
         add_x(1, 1, 1)
-        round_x1("scalar", 1, 1, 1)
+        round_x1("gpsimd", 1, 1, 1)
         both(multiply_r, 0, left)
         add_x1(0, left, tiles)
         both(turn_x1, 1, 1)
         both(regroup_x1, 1, 1)
         interleave_x2("scalar", 0, left, whole)
         quantise_x1(2, 0)
-        multiply_a(2, 1, 0)
-        add_x(2, 1, 0)
-        multiply_a(2, 1, 1)
+        both(multiply_r, 0, right)
+        add_x1(0, right, tiles)
+        interleave_x2("scalar", 0, right, whole)
         quantise_x1(1, 1)
-        add_x(2, 1, 1)
+        quantise_x2(0, left)
+        multiply_a_and_add(2, 1)
         round_unit(2, 1)
         both(multiply_r, 1, left)
         add_x1(1, left, tiles)
         both(turn_x1, 2, 1)
         both(regroup_x1, 2, 1)
         interleave_x2("scalar", 1, left, whole)
-        quantise_x2(0, left)
-        both(multiply_r, 0, right)
-        add_x1(0, right, tiles[:1])
+        quantise_x2(0, right)
+        both(multiply_r, 1, right)
+        add_x1(1, right, tiles[:1])
         quantise_x1(2, 1)
-        add_x1(0, right, tiles[1:])
-        interleave_x2("scalar", 0, right, whole)
+        add_x1(1, right, tiles[1:])
+        interleave_x2("scalar", 1, right, whole)
         both(multiply_r, 2, left)
         quantise_x2(1, left)
         add_x1(2, left, tiles)
-        interleave_x2("scalar", 2, left, whole)
-        both(multiply_r, 1, right)
-        add_x1(1, right, tiles)
-        interleave_x2("scalar", 1, right, whole)
+        interleave_x2_unit(2, left)
         multiply_b(left, 0)
         multiply_b(left, 1)
-        quantise_x2(0, right)
-        quantise_x2(2, left)
         both(multiply_r, 2, right)
-        multiply_b(left, 2)
-        add_x1(2, right, tiles[:3])
         quantise_x2(1, right)
-        add_x1(2, right, tiles[3:])
+        add_x1(2, right, tiles[:2])
+        quantise_x2(2, left)
+        add_x1(2, right, tiles[2:])
         interleave_x2_unit(2, right)
+        multiply_b(left, 2)
         multiply_b(right, 0)
         multiply_b(right, 1)
         finish(left, slice(0, 3))

@@ -26,6 +26,7 @@ HALF = K_PASS
 PART = HALF // 2
 HEAD_SHARE = 192
 GPSIMD_SHARE = 224
+EARLY = 2
 RUN = 4
 OUT_TILES = G // P
 BANKS = 8
@@ -55,7 +56,7 @@ def tile_household_bracket_response_t2_kernel(
         def kept(shape, dtype, name):
             return keep.tile(shape, dtype, name=name, align_bytes=64)
 
-        a_scales_in = [kept([P, GROUPS, K_PASS], U8, "a_scales_first"), kept([P, GROUPS, H - K_PASS], U8, "a_scales_rest")]
+        a_scales_in = [kept([P, GROUPS, EARLY * K_PASS], U8, "a_scales_early"), kept([P, GROUPS, K_PASS], U8, "a_scales_last")]
         r_scales = kept([P, HALVES, C], U8, "r_scales")
         b_scales = kept([P, GROUPS, G], U8, "b_scales")
         nc.vector.memset(a_scales_in[0][:].bitcast(I32), 0)
@@ -77,7 +78,8 @@ def tile_household_bracket_response_t2_kernel(
             nc.sync.dma_start(out=tile.bitcast(I32), in_=words.rearrange("k p n -> p k n").bitcast(I32))
 
         x_in = [[kept([P, PACK, HALF], BF16, f"x_{g}_{half}") for half in range(HALVES)] for g in range(GROUPS)]
-        a_in = [kept([P, GROUPS, E2M1_BYTES * K_PASS], U8, f"a_in_{g}") for g in range(GROUPS)]
+        a_early = [kept([P, EARLY, E2M1_BYTES * K_PASS], U8, f"a_early_{k}") for k in range(GROUPS)]
+        a_last = kept([P, GROUPS, E2M1_BYTES * K_PASS], U8, "a_last")
         r_words = kept([P, HALVES, E2M1_BYTES * C], U8, "r_words")
         b_words = kept([P, GROUPS, E2M1_BYTES * G], U8, "b_words")
         prop = kept([P, GROUPS, PACK], BF16, "prop")
@@ -89,20 +91,21 @@ def tile_household_bracket_response_t2_kernel(
                 in_=x[K_PASS * g : K_PASS * (g + 1), HALF * half : HALF * (half + 1)].rearrange("(p t) c -> p t c", t=PACK),
             )
 
-        def load_a(g, ks=slice(None)):
-            width = E2M1_BYTES * K_PASS
-            load_words(a_in[g][:, ks, :], transfer_words[ks, :, width * g : width * (g + 1)])
+        def load_a_early(k):
+            width = E2M1_BYTES * EARLY * K_PASS
+            words = transfer_words[k, :, :width].rearrange("p (g n) -> p g n", g=EARLY)
+            nc.sync.dma_start(out=a_early[k][:].bitcast(I32), in_=words.bitcast(I32))
 
-        load_a(0, slice(0, 1))
-        load_scales(a_scales_in[0], transfer_scales[:, :, :K_PASS])
         load_x(0, 0)
+        load_a_early(0)
+        load_scales(a_scales_in[0], transfer_scales[:, :, : EARLY * K_PASS])
         load_x(1, 0)
-        load_a(0, slice(1, GROUPS))
+        load_a_early(1)
         load_x(2, 0)
-        load_a(1)
-        load_scales(a_scales_in[1], transfer_scales[:, :, K_PASS:])
+        load_a_early(2)
+        load_scales(a_scales_in[1], transfer_scales[:, :, EARLY * K_PASS :])
+        load_words(a_last[:], transfer_words[:, :, E2M1_BYTES * EARLY * K_PASS :])
         load_x(0, 1)
-        load_a(2)
         load_x(1, 1)
         load_x(2, 1)
         load_scales(r_scales, reclass_scales)
@@ -155,22 +158,24 @@ def tile_household_bracket_response_t2_kernel(
         a_words = [kept([P, PACK, GROUPS, E2M1_BYTES * P], U8, f"a_words_{g}") for g in range(GROUPS)]
         a_scales = [kept([P, PACK, GROUPS, P], U8, f"a_scales_{g}") for g in range(GROUPS)]
 
-        def reorder_a_words(g, ks=slice(None)):
+        def reorder_words(target, source):
             nc.vector.tensor_copy(
-                out=a_words[g][:, :, ks, :].bitcast(U16).rearrange("p t k (m i) -> p k m t i", i=RUN),
-                in_=a_in[g][:, ks, :].bitcast(U16).rearrange("p k (m i t) -> p k m t i", i=RUN, t=PACK),
+                out=target.bitcast(U16).rearrange("p t k (m i) -> p k m t i", i=RUN),
+                in_=source.bitcast(U16).rearrange("p k (m i t) -> p k m t i", i=RUN, t=PACK),
             )
 
-        def reorder_a_scales(g, ks=slice(None)):
-            if g == 0:
-                scales_in = a_scales_in[0][:, ks, :]
-            else:
-                scales_in = a_scales_in[1][:, ks, K_PASS * (g - 1) : K_PASS * g]
-            nc.vector.tensor_copy(out=a_scales[g][:, :, ks, :], in_=scales_in.rearrange("p k (m t) -> p t k m", t=PACK))
+        def reorder_early_words(k):
+            for g in range(EARLY):
+                reorder_words(a_words[g][:, :, k : k + 1, :], a_early[k][:, g : g + 1, :])
 
-        def reorder_a(g, first, passes):
-            reorder_a_words(g, slice(first, first + passes))
-            reorder_a_scales(g, slice(first, first + passes))
+        def reorder_a_scales(g, passes):
+            if g < EARLY:
+                scales_in = a_scales_in[0][:, passes, K_PASS * g : K_PASS * (g + 1)]
+            else:
+                scales_in = a_scales_in[1][:, passes, :]
+            nc.vector.tensor_copy(
+                out=a_scales[g][:, :, passes, :], in_=scales_in.rearrange("p k (m t) -> p t k m", t=PACK)
+            )
 
         xq = [kept([P, C], U32, f"xq_{g}") for g in range(GROUPS)]
         xq_scales = [kept([P, C], U8, f"xq_scales_{g}") for g in range(GROUPS)]
@@ -203,13 +208,13 @@ def tile_household_bracket_response_t2_kernel(
                 stop=(k == GROUPS - 1),
             )
 
-        def multiply_a(g, half, pair):
-            for t in (2 * pair, 2 * pair + 1):
+        def multiply_a(g, half, tiles):
+            for t in tiles:
                 for k in range(GROUPS):
                     multiply_a_pass(g, half, t, k)
 
-        def add_x(g, half, pair):
-            for t in (2 * pair, 2 * pair + 1):
+        def add_x(g, half, tiles):
+            for t in tiles:
                 nc.vector.tensor_tensor(
                     out=x1[g][:, t, HALF * half : HALF * (half + 1)],
                     in0=close_bank((1, g, half, t))[:],
@@ -220,9 +225,9 @@ def tile_household_bracket_response_t2_kernel(
         x1q = [[kept([P, K_PASS], U32, f"x1q_{g}_{half}") for half in range(HALVES)] for g in range(GROUPS)]
         x1q_scales = [[kept([P, K_PASS], U8, f"x1q_scales_{g}_{half}") for half in range(HALVES)] for g in range(GROUPS)]
 
-        def round_x1(engine, g, half, pair):
+        def round_x1(engine, g, half, tiles):
             rounded = stage("x1_rounded", (g, half), [P, PACK, 2, P, 2], 4)
-            for t in (2 * pair, 2 * pair + 1):
+            for t in tiles:
                 row = x1[g][:, t, HALF * half : HALF * (half + 1)]
                 copy(engine, rounded[:, t, :, :, :], row.rearrange("p (w u e) -> p u w e", u=2, e=2))
 
@@ -286,7 +291,7 @@ def tile_household_bracket_response_t2_kernel(
         x2q_scales = [kept([P, C], U8, f"x2q_scales_{g}") for g in range(GROUPS)]
 
         def interleave_x2(engine, g, span, cols):
-            grouped = stage("x2_grouped", (g, span), [P, span[1], PACK], 2)
+            grouped = stage("x2_grouped", (g, span), [P, span[1], PACK], 3)
             interleave(engine, grouped[:, cols, :], staged["x2", (g, span)][:, :, cols])
 
         def quantise_x2(g, span):
@@ -315,107 +320,119 @@ def tile_household_bracket_response_t2_kernel(
                     stop=(k == GROUPS - 1 and slot == shared - 1),
                 )
 
+        responses = {}
+
         def finish(span, banks):
             first, width = span
             cols = slice(first, first + width)
             shared = HALF // width
             for j in range(0, OUT_TILES, shared)[banks]:
-                response = work.tile([P, shared, width], F32, name="response", bufs=7)
+                if j % 2 == 0:
+                    pair = work.tile([P, 2, HALF], F32, name="response", tag="x1_rounded", bufs=4, align_bytes=64)
+                    responses[span[0] // HALF * 2 + j // 2] = pair
+                response = responses[span[0] // HALF * 2 + j // 2][:, j % 2 : j % 2 + shared, :]
                 nc.vector.tensor_tensor(
-                    out=response[:], in0=close_bank((3, span, j))[:], in1=rates[:, j : j + shared, cols], op=MULT
+                    out=response, in0=close_bank((3, span, j))[:], in1=rates[:, j : j + shared, cols], op=MULT
                 )
                 rows = out[P * j : P * (j + shared), cols].rearrange("(j p) c -> p j c", p=P)
-                nc.sync.dma_start(out=rows, in_=response[:])
+                nc.sync.dma_start(out=rows, in_=response)
 
         def both(step, *unit):
             for pair in range(PACK // 2):
                 step(*unit, pair)
 
         def round_unit(g, half):
-            round_x1("gpsimd", g, half, 0)
-            round_x1("scalar", g, half, 1)
+            round_x1("gpsimd", g, half, front)
+            round_x1("scalar", g, half, back)
 
         def interleave_x2_unit(g, span):
             interleave_x2("gpsimd", g, span, slice(0, GPSIMD_SHARE))
             interleave_x2("scalar", g, span, slice(GPSIMD_SHARE, HALF))
 
+        def interleave_x_unit(g, half):
+            interleave_x("gpsimd", g, half, slice(0, GPSIMD_SHARE))
+            interleave_x("scalar", g, half, slice(GPSIMD_SHARE, HALF))
+
         def multiply_a_by_pass(g, half, k):
             for t in range(PACK):
                 multiply_a_pass(g, half, t, k)
-
-        def multiply_a_and_add(g, half):
-            for pair in range(PACK // 2):
-                multiply_a(g, half, pair)
-                add_x(g, half, pair)
 
         left, right = (0, HALF), (HALF, HALF)
         third, fourth = (HALF, PART), (HALF + PART, PART)
         whole = slice(None)
         tiles = range(PACK)
+        front, back = tiles[:2], tiles[2:]
 
-        reorder_a_words(0, slice(0, 1))
-        reorder_a_scales(0)
-        for g in range(GROUPS):
-            share = HEAD_SHARE if g == 0 else PART
-            interleave_x("scalar", g, 0, slice(0, share))
-            interleave_x("vector", g, 0, slice(share, HALF))
-            if g == 1:
-                reorder_a_words(0, slice(1, GROUPS))
-            if g == 2:
-                reorder_a_words(1, slice(0, 1))
-            quantise_x(g, 0)
-            multiply_a_by_pass(0, 0, g)
-        reorder_a_words(1, slice(1, GROUPS))
-        reorder_a_scales(1)
-        reorder_a_scales(2)
-        reorder_a_words(2)
-        for g in range(GROUPS):
-            interleave_x("scalar", g, 1, whole)
-        both(multiply_a, 1, 0)
-        both(add_x, 0, 0)
-        round_unit(0, 0)
-        both(multiply_a, 2, 0)
-        quantise_x(0, 1)
-        both(add_x, 1, 0)
-        round_unit(1, 0)
-        quantise_x(1, 1)
-        quantise_x(2, 1)
-        both(add_x, 2, 0)
-        round_unit(2, 0)
         for k in range(GROUPS):
-            multiply_a_by_pass(0, 1, k)
-        both(add_x, 0, 1)
+            share = HEAD_SHARE if k == 0 else PART
+            interleave_x("scalar", k, 0, slice(0, share))
+            interleave_x("vector", k, 0, slice(share, HALF))
+            reorder_early_words(k)
+            quantise_x(k, 0)
+            for g in range(EARLY):
+                if k == 0:
+                    reorder_a_scales(g, slice(0, 1))
+                multiply_a_by_pass(g, 0, k)
+            if k == 0:
+                for g in range(EARLY):
+                    reorder_a_scales(g, slice(1, GROUPS))
+        reorder_a_scales(2, whole)
+        reorder_words(a_words[2][:], a_last[:])
+        interleave_x("scalar", 0, 1, whole)
+        interleave_x_unit(1, 1)
+        interleave_x_unit(2, 1)
+        add_x(0, 0, tiles)
+        multiply_a(2, 0, tiles)
+        add_x(1, 0, front)
+        for g in range(GROUPS):
+            quantise_x(g, 1)
+        add_x(1, 0, back)
+        round_x1("scalar", 0, 0, tiles)
+        round_x1("scalar", 1, 0, tiles)
+        add_x(2, 0, front)
+        for k in range(GROUPS):
+            for t in front:
+                multiply_a_pass(0, 1, t, k)
+        multiply_a(0, 1, back)
         both(turn_x1, 0, 0)
-        both(turn_x1, 1, 0)
-        both(regroup_x1, 0, 0)
+        add_x(0, 1, tiles)
+        regroup_x1(0, 0, 0)
         round_unit(0, 1)
-        both(regroup_x1, 1, 0)
-        quantise_x1(0, 0)
-        multiply_a(1, 1, 0)
-        add_x(1, 1, 0)
+        round_x1("gpsimd", 2, 0, front)
+        regroup_x1(0, 0, 1)
+        multiply_a(1, 1, front)
+        add_x(1, 1, front)
         both(turn_x1, 0, 1)
-        both(turn_x1, 2, 0)
+        both(turn_x1, 1, 0)
         both(regroup_x1, 0, 1)
-        both(regroup_x1, 2, 0)
-        round_x1("scalar", 1, 1, 0)
-        quantise_x1(1, 0)
-        multiply_a(1, 1, 1)
+        both(regroup_x1, 1, 0)
+        round_x1("scalar", 1, 1, front)
+        multiply_a(1, 1, back)
+        add_x(2, 0, back)
+        round_x1("scalar", 2, 0, back)
+        quantise_x1(0, 0)
         quantise_x1(0, 1)
-        add_x(1, 1, 1)
-        round_x1("gpsimd", 1, 1, 1)
+        add_x(1, 1, back)
+        round_x1("gpsimd", 1, 1, back)
         both(multiply_r, 0, left)
         add_x1(0, left, tiles)
         both(turn_x1, 1, 1)
         both(regroup_x1, 1, 1)
         interleave_x2("scalar", 0, left, whole)
-        quantise_x1(2, 0)
+        quantise_x1(1, 0)
         both(multiply_r, 0, right)
         add_x1(0, right, tiles)
+        both(turn_x1, 2, 0)
+        both(regroup_x1, 2, 0)
         interleave_x2("scalar", 0, right, whole)
         quantise_x1(1, 1)
         quantise_x2(0, left)
-        multiply_a_and_add(2, 1)
-        round_unit(2, 1)
+        multiply_a(2, 1, tiles)
+        add_x(2, 1, tiles[:1])
+        quantise_x1(2, 0)
+        add_x(2, 1, tiles[1:])
+        round_x1("scalar", 2, 1, front)
+        round_x1("gpsimd", 2, 1, back)
         both(multiply_r, 1, left)
         add_x1(1, left, tiles)
         both(turn_x1, 2, 1)

@@ -25,7 +25,7 @@ HALVES = C // K_PASS
 HALF = K_PASS
 PART = HALF // 2
 HEAD_SHARE = 192
-GPSIMD_SHARE = 224
+GPSIMD_SHARE = 208
 EARLY = 2
 RUN = 4
 OUT_TILES = G // P
@@ -302,11 +302,11 @@ def tile_household_bracket_response_t2_kernel(
                 in_=flat(staged["x2_grouped", (g, span)]),
             )
 
-        def multiply_b(span, k):
+        def multiply_b(span, k, out_tiles=range(OUT_TILES)):
             first, width = span
             cols = slice(first, first + width)
             shared = HALF // width
-            for j in range(OUT_TILES):
+            for j in out_tiles:
                 slot = j % shared
                 if k == 0 and slot == 0:
                     open_bank((3, span, j), [P, shared, width])
@@ -388,7 +388,8 @@ def tile_household_bracket_response_t2_kernel(
             quantise_x(g, 1)
         add_x(1, 0, back)
         round_x1("scalar", 0, 0, tiles)
-        round_x1("scalar", 1, 0, tiles)
+        round_x1("scalar", 1, 0, front)
+        round_x1("gpsimd", 1, 0, back)
         add_x(2, 0, front)
         for k in range(GROUPS):
             for t in front:
@@ -416,22 +417,23 @@ def tile_household_bracket_response_t2_kernel(
         round_x1("gpsimd", 1, 1, back)
         both(multiply_r, 0, left)
         add_x1(0, left, tiles)
-        both(turn_x1, 1, 1)
-        both(regroup_x1, 1, 1)
         interleave_x2("scalar", 0, left, whole)
         quantise_x1(1, 0)
         both(multiply_r, 0, right)
         add_x1(0, right, tiles)
+        both(turn_x1, 1, 1)
         both(turn_x1, 2, 0)
+        both(regroup_x1, 1, 1)
         both(regroup_x1, 2, 0)
-        interleave_x2("scalar", 0, right, whole)
-        quantise_x1(1, 1)
         quantise_x2(0, left)
         multiply_a(2, 1, tiles)
         add_x(2, 1, tiles[:1])
+        quantise_x1(1, 1)
+        add_x(2, 1, tiles[1:2])
         quantise_x1(2, 0)
-        add_x(2, 1, tiles[1:])
+        add_x(2, 1, tiles[2:])
         round_x1("scalar", 2, 1, front)
+        interleave_x2("scalar", 0, right, whole)
         round_x1("gpsimd", 2, 1, back)
         both(multiply_r, 1, left)
         add_x1(1, left, tiles)
@@ -449,18 +451,19 @@ def tile_household_bracket_response_t2_kernel(
         add_x1(2, left, tiles)
         interleave_x2_unit(2, left)
         multiply_b(left, 0)
-        multiply_b(left, 1)
         both(multiply_r, 2, right)
         quantise_x2(1, right)
-        add_x1(2, right, tiles[:2])
+        add_x1(2, right, tiles[:3])
         quantise_x2(2, left)
-        add_x1(2, right, tiles[2:])
+        add_x1(2, right, tiles[3:])
         interleave_x2_unit(2, right)
+        multiply_b(left, 1)
+        multiply_b(right, 0, tiles[:3])
         multiply_b(left, 2)
-        multiply_b(right, 0)
+        multiply_b(right, 0, tiles[3:])
         multiply_b(right, 1)
-        finish(left, slice(0, 3))
+        finish(left, slice(0, 2))
         quantise_x2(2, right)
-        finish(left, slice(3, 4))
+        finish(left, slice(2, 4))
         multiply_b(right, 2)
         finish(right, whole)

@@ -16,6 +16,7 @@ FP8X4 = mybir.dt.float8_e4m3fn_x4
 FP4X4 = mybir.dt.float4_e2m1fn_x4
 ADD = mybir.AluOpType.add
 MULT = mybir.AluOpType.mult
+COPY = mybir.ActivationFunctionType.Copy
 
 P = 128
 PACK = 4
@@ -23,14 +24,14 @@ K_PASS = P * PACK
 GROUPS = H // K_PASS
 HALVES = C // K_PASS
 HALF = K_PASS
-PART = HALF // 2
-HEAD_SHARE = 192
-GPSIMD_SHARE = 208
-EARLY = 2
-RUN = 4
+LEFT, RIGHT = range(HALVES)
 OUT_TILES = G // P
 BANKS = 8
 E2M1_BYTES = 2
+EARLY = BANKS // PACK
+RUN = 4
+SCALAR_SHARES = (192, 320, 256)
+GPSIMD_SHARE = 208
 
 
 def tile_household_bracket_response_t2_kernel(
@@ -56,15 +57,25 @@ def tile_household_bracket_response_t2_kernel(
         def kept(shape, dtype, name):
             return keep.tile(shape, dtype, name=name, align_bytes=64)
 
-        a_scales_in = [kept([P, GROUPS, EARLY * K_PASS], U8, "a_scales_early"), kept([P, GROUPS, K_PASS], U8, "a_scales_last")]
+        def columns(half):
+            return slice(HALF * half, HALF * (half + 1))
+
+        a_scales_early = kept([P, GROUPS, EARLY * K_PASS], U8, "a_scales_early")
+        a_scales_last = kept([P, GROUPS, K_PASS], U8, "a_scales_last")
         r_scales = kept([P, HALVES, C], U8, "r_scales")
         b_scales = kept([P, GROUPS, G], U8, "b_scales")
-        nc.vector.memset(a_scales_in[0][:].bitcast(I32), 0)
-        nc.vector.memset(a_scales_in[1][:].bitcast(I32), 0)
-        nc.vector.memset(r_scales[:].bitcast(I32), 0)
-        nc.vector.memset(b_scales[:].bitcast(I32), 0)
+        for plane in (a_scales_early, a_scales_last, r_scales, b_scales):
+            nc.vector.memset(plane[:].bitcast(I32), 0)
         identity = kept([P, P], F32, "identity")
         make_identity(nc, identity[:])
+
+        x_in = [[kept([P, PACK, HALF], BF16, f"x_{g}_{half}") for half in range(HALVES)] for g in range(GROUPS)]
+        a_early = [kept([P, EARLY, E2M1_BYTES * K_PASS], U8, f"a_early_{k}") for k in range(GROUPS)]
+        a_last = kept([P, GROUPS, E2M1_BYTES * K_PASS], U8, "a_last")
+        r_words = kept([P, HALVES, E2M1_BYTES * C], U8, "r_words")
+        b_words = kept([P, GROUPS, E2M1_BYTES * G], U8, "b_words")
+        prop = kept([P, GROUPS, PACK], BF16, "prop")
+        rates = kept([P, OUT_TILES, C], BF16, "rates")
 
         def load_scales(plane, scales):
             words = plane[:].bitcast(I32)
@@ -75,44 +86,30 @@ def tile_household_bracket_response_t2_kernel(
                 )
 
         def load_words(tile, words):
-            nc.sync.dma_start(out=tile.bitcast(I32), in_=words.rearrange("k p n -> p k n").bitcast(I32))
-
-        x_in = [[kept([P, PACK, HALF], BF16, f"x_{g}_{half}") for half in range(HALVES)] for g in range(GROUPS)]
-        a_early = [kept([P, EARLY, E2M1_BYTES * K_PASS], U8, f"a_early_{k}") for k in range(GROUPS)]
-        a_last = kept([P, GROUPS, E2M1_BYTES * K_PASS], U8, "a_last")
-        r_words = kept([P, HALVES, E2M1_BYTES * C], U8, "r_words")
-        b_words = kept([P, GROUPS, E2M1_BYTES * G], U8, "b_words")
-        prop = kept([P, GROUPS, PACK], BF16, "prop")
-        rates = kept([P, OUT_TILES, C], BF16, "rates")
+            nc.sync.dma_start(out=tile[:].bitcast(I32), in_=words.rearrange("k p n -> p k n").bitcast(I32))
 
         def load_x(g, half):
-            nc.sync.dma_start(
-                out=x_in[g][half][:],
-                in_=x[K_PASS * g : K_PASS * (g + 1), HALF * half : HALF * (half + 1)].rearrange("(p t) c -> p t c", t=PACK),
-            )
+            rows = x[K_PASS * g : K_PASS * (g + 1), columns(half)]
+            nc.sync.dma_start(out=x_in[g][half][:], in_=rows.rearrange("(p t) c -> p t c", t=PACK))
 
         def load_a_early(k):
-            width = E2M1_BYTES * EARLY * K_PASS
-            words = transfer_words[k, :, :width].rearrange("p (g n) -> p g n", g=EARLY)
+            words = transfer_words[k, :, : E2M1_BYTES * EARLY * K_PASS].rearrange("p (g n) -> p g n", g=EARLY)
             nc.sync.dma_start(out=a_early[k][:].bitcast(I32), in_=words.bitcast(I32))
 
-        load_x(0, 0)
-        load_a_early(0)
-        load_scales(a_scales_in[0], transfer_scales[:, :, : EARLY * K_PASS])
-        load_x(1, 0)
-        load_a_early(1)
-        load_x(2, 0)
-        load_a_early(2)
-        load_scales(a_scales_in[1], transfer_scales[:, :, EARLY * K_PASS :])
-        load_words(a_last[:], transfer_words[:, :, E2M1_BYTES * EARLY * K_PASS :])
-        load_x(0, 1)
-        load_x(1, 1)
-        load_x(2, 1)
+        for k in range(GROUPS):
+            load_x(k, LEFT)
+            load_a_early(k)
+            if k == 0:
+                load_scales(a_scales_early, transfer_scales[:, :, : EARLY * K_PASS])
+        load_scales(a_scales_last, transfer_scales[:, :, EARLY * K_PASS :])
+        load_words(a_last, transfer_words[:, :, E2M1_BYTES * EARLY * K_PASS :])
+        for g in range(GROUPS):
+            load_x(g, RIGHT)
         load_scales(r_scales, reclass_scales)
-        load_words(r_words[:], reclass_words)
+        load_words(r_words, reclass_words)
         nc.sync.dma_start(out=prop[:], in_=propensity.rearrange("(g p t) -> p g t", p=P, t=PACK))
         load_scales(b_scales, bracket_scales)
-        load_words(b_words[:], bracket_words)
+        load_words(b_words, bracket_words)
         nc.sync.dma_start(out=rates[:], in_=rate.rearrange("(j p) c -> p j c", p=P))
 
         closed_banks = list(range(BANKS))
@@ -130,12 +127,13 @@ def tile_household_bracket_response_t2_kernel(
             return tile
 
         staged = {}
+        ROUNDED_BUFS = 4
 
-        def stage(kind, key, shape, bufs):
-            if (kind, key) not in staged:
+        def stage(kind, g, half, shape, bufs=3):
+            if (kind, g, half) not in staged:
                 tile = work.tile(shape, BF16, name=kind, tag=kind, bufs=bufs, align_bytes=64)
-                staged[kind, key] = tile
-            return staged[kind, key]
+                staged[kind, g, half] = tile
+            return staged[kind, g, half]
 
         def copy(engine, out_ap, in_ap):
             if engine == "vector":
@@ -145,78 +143,74 @@ def tile_household_bracket_response_t2_kernel(
             else:
                 nc.scalar.copy(out=out_ap, in_=in_ap)
 
-        def interleave(engine, grouped, tiles):
+        def interleave(engine, grouped, unit):
             copy(
                 engine,
                 grouped.rearrange("p (c i) t -> p c t i", i=RUN),
-                tiles.rearrange("p t (c i) -> p c t i", i=RUN),
+                unit.rearrange("p t (c i) -> p c t i", i=RUN),
             )
 
-        def flat(tile):
-            return tile[:].rearrange("p c t -> p (c t)")
+        def quantise(codes, scales, grouped):
+            nc.vector.quantize_mx(out=codes.bitcast(FP8X4), scales=scales, in_=grouped[:].rearrange("p c t -> p (c t)"))
 
-        a_words = [kept([P, PACK, GROUPS, E2M1_BYTES * P], U8, f"a_words_{g}") for g in range(GROUPS)]
-        a_scales = [kept([P, PACK, GROUPS, P], U8, f"a_scales_{g}") for g in range(GROUPS)]
-
-        def reorder_words(target, source):
-            nc.vector.tensor_copy(
-                out=target.bitcast(U16).rearrange("p t k (m i) -> p k m t i", i=RUN),
-                in_=source.bitcast(U16).rearrange("p k (m i t) -> p k m t i", i=RUN, t=PACK),
-            )
+        a_words = kept([P, GROUPS, PACK, GROUPS, E2M1_BYTES * P], U8, "a_words")
+        a_scales = kept([P, GROUPS, PACK, GROUPS, P], U8, "a_scales")
 
         def reorder_early_words(k):
-            for g in range(EARLY):
-                reorder_words(a_words[g][:, :, k : k + 1, :], a_early[k][:, g : g + 1, :])
-
-        def reorder_a_scales(g, passes):
-            if g < EARLY:
-                scales_in = a_scales_in[0][:, passes, K_PASS * g : K_PASS * (g + 1)]
-            else:
-                scales_in = a_scales_in[1][:, passes, :]
             nc.vector.tensor_copy(
-                out=a_scales[g][:, :, passes, :], in_=scales_in.rearrange("p k (m t) -> p t k m", t=PACK)
+                out=a_words[:, :EARLY, :, k, :].bitcast(U16).rearrange("p g t (m i) -> p g m t i", i=RUN),
+                in_=a_early[k][:].bitcast(U16).rearrange("p g (m i t) -> p g m t i", i=RUN, t=PACK),
+            )
+
+        def reorder_last_words():
+            nc.vector.tensor_copy(
+                out=a_words[:, EARLY, :, :, :].bitcast(U16).rearrange("p t k (m i) -> p k m t i", i=RUN),
+                in_=a_last[:].bitcast(U16).rearrange("p k (m i t) -> p k m t i", i=RUN, t=PACK),
+            )
+
+        def reorder_early_scales(groups, passes):
+            scales_in = a_scales_early[:, passes, :].rearrange("p k (g m t) -> p g t k m", g=EARLY, t=PACK)
+            nc.vector.tensor_copy(out=a_scales[:, groups, :, passes, :], in_=scales_in[:, groups, :, :, :])
+
+        def reorder_last_scales():
+            nc.vector.tensor_copy(
+                out=a_scales[:, EARLY, :, :, :], in_=a_scales_last[:].rearrange("p k (m t) -> p t k m", t=PACK)
             )
 
         xq = [kept([P, C], U32, f"xq_{g}") for g in range(GROUPS)]
         xq_scales = [kept([P, C], U8, f"xq_scales_{g}") for g in range(GROUPS)]
 
-        def interleave_x(engine, g, half, cols):
-            grouped = stage("x_grouped", (g, half), [P, HALF, PACK], 3)
-            interleave(engine, grouped[:, cols, :], x_in[g][half][:, :, cols])
+        def interleave_x(engine, g, half, part):
+            grouped = stage("x_grouped", g, half, [P, HALF, PACK])
+            interleave(engine, grouped[:, part, :], x_in[g][half][:, :, part])
 
         def quantise_x(g, half):
-            cols = slice(HALF * half, HALF * (half + 1))
-            nc.vector.quantize_mx(
-                out=xq[g][:, cols].bitcast(FP8X4),
-                scales=xq_scales[g][:, cols],
-                in_=flat(staged["x_grouped", (g, half)]),
-            )
+            quantise(xq[g][:, columns(half)], xq_scales[g][:, columns(half)], staged["x_grouped", g, half])
 
         x1 = [kept([P, PACK, C], F32, f"x1_{g}") for g in range(GROUPS)]
 
-        def multiply_a_pass(g, half, t, k):
-            cols = slice(HALF * half, HALF * (half + 1))
+        def multiply_a(g, half, t, k):
             if k == 0:
                 open_bank((1, g, half, t), [P, HALF])
             nc.tensor.matmul_mx(
                 out=open_banks[1, g, half, t][1][:],
-                lhsT=a_words[g][:, t, k, :].bitcast(FP4X4),
-                lhsT_scale=a_scales[g][:, t, k, :],
-                rhs=xq[k][:, cols].bitcast(FP8X4),
-                rhs_scale=xq_scales[k][:, cols],
+                lhsT=a_words[:, g, t, k, :].bitcast(FP4X4),
+                lhsT_scale=a_scales[:, g, t, k, :],
+                rhs=xq[k][:, columns(half)].bitcast(FP8X4),
+                rhs_scale=xq_scales[k][:, columns(half)],
                 start=(k == 0),
                 stop=(k == GROUPS - 1),
             )
 
-        def multiply_a(g, half, tiles):
+        def multiply_a_tiles(g, half, tiles):
             for t in tiles:
                 for k in range(GROUPS):
-                    multiply_a_pass(g, half, t, k)
+                    multiply_a(g, half, t, k)
 
         def add_x(g, half, tiles):
             for t in tiles:
                 nc.vector.tensor_tensor(
-                    out=x1[g][:, t, HALF * half : HALF * (half + 1)],
+                    out=x1[g][:, t, columns(half)],
                     in0=close_bank((1, g, half, t))[:],
                     in1=x_in[g][half][:, t, :],
                     op=ADD,
@@ -226,244 +220,218 @@ def tile_household_bracket_response_t2_kernel(
         x1q_scales = [[kept([P, K_PASS], U8, f"x1q_scales_{g}_{half}") for half in range(HALVES)] for g in range(GROUPS)]
 
         def round_x1(engine, g, half, tiles):
-            rounded = stage("x1_rounded", (g, half), [P, PACK, 2, P, 2], 4)
+            rounded = stage("x1_rounded", g, half, [P, PACK, 2, P, 2], ROUNDED_BUFS)
             for t in tiles:
-                row = x1[g][:, t, HALF * half : HALF * (half + 1)]
+                row = x1[g][:, t, columns(half)]
                 copy(engine, rounded[:, t, :, :, :], row.rearrange("p (w u e) -> p u w e", u=2, e=2))
 
-        def turn_x1(g, half, pair):
-            rounded = staged["x1_rounded", (g, half)]
-            turned = open_bank(("turn", g, half, pair), [P, 2, 2, P])
-            for i in range(2):
-                for u in range(2):
-                    words = rounded[:, 2 * pair + i, u, :, :].rearrange("p w e -> p (w e)").bitcast(F32)
-                    nc.tensor.transpose(turned[:, i, u, :], words, identity[:])
+        def turn_x1(g, half):
+            rounded = staged["x1_rounded", g, half]
+            for pair in range(PACK // 2):
+                turned = open_bank(("turn", g, half, pair), [P, 2, 2, P])
+                for i in range(2):
+                    for u in range(2):
+                        words = rounded[:, 2 * pair + i, u, :, :].rearrange("p w e -> p (w e)").bitcast(F32)
+                        nc.tensor.transpose(turned[:, i, u, :], words, identity[:])
 
-        def regroup_x1(g, half, pair):
-            grouped = stage("x1_grouped", (g, half), [P, K_PASS, PACK], 3)
-            words = grouped[:, 2 * P * pair : 2 * P * (pair + 1), :].rearrange("p m v -> p (m v)").bitcast(F32)
-            nc.scalar.copy(
-                out=words.rearrange("p (i m u) -> p i m u", i=2, u=2),
-                in_=close_bank(("turn", g, half, pair))[:].rearrange("p i u m -> p i m u"),
-            )
+        def regroup_x1(g, half, pairs):
+            grouped = stage("x1_grouped", g, half, [P, K_PASS, PACK])
+            for pair in pairs:
+                words = grouped[:, 2 * P * pair : 2 * P * (pair + 1), :].rearrange("p m v -> p (m v)").bitcast(F32)
+                nc.scalar.copy(
+                    out=words.rearrange("p (i m u) -> p i m u", i=2, u=2),
+                    in_=close_bank(("turn", g, half, pair))[:].rearrange("p i u m -> p i m u"),
+                )
 
         def quantise_x1(g, half):
-            nc.vector.quantize_mx(
-                out=x1q[g][half][:].bitcast(FP8X4),
-                scales=x1q_scales[g][half][:],
-                in_=flat(staged["x1_grouped", (g, half)]),
-            )
+            quantise(x1q[g][half][:], x1q_scales[g][half][:], staged["x1_grouped", g, half])
 
-        def multiply_r(g, span, pair):
-            first, width = span
-            for t in (2 * pair, 2 * pair + 1):
-                slot = t % (HALF // width)
-                if slot == 0:
-                    acc = open_bank((2, g, span, t), [P, HALF // width, width])
+        def multiply_r(g, half):
+            for t in range(PACK):
+                acc = open_bank((2, g, half, t), [P, HALF])
                 for k in range(HALVES):
                     nc.tensor.matmul_mx(
-                        out=acc[:, slot, :],
+                        out=acc[:],
                         lhsT=x1q[g][k][:, P * t : P * (t + 1)].bitcast(FP8X4),
                         lhsT_scale=x1q_scales[g][k][:, P * t : P * (t + 1)],
-                        rhs=r_words[:, k, E2M1_BYTES * first : E2M1_BYTES * (first + width)].bitcast(FP4X4),
-                        rhs_scale=r_scales[:, k, first : first + width],
+                        rhs=r_words[:, k, E2M1_BYTES * HALF * half : E2M1_BYTES * HALF * (half + 1)].bitcast(FP4X4),
+                        rhs_scale=r_scales[:, k, columns(half)],
                         start=(k == 0),
                         stop=(k == HALVES - 1),
                     )
 
-        def add_x1(g, span, tiles):
-            first, width = span
-            x2 = stage("x2", (g, span), [P, PACK, width], 3)
+        def add_x1(g, half, tiles):
+            x2 = stage("x2", g, half, [P, PACK, HALF])
             for t in tiles:
-                slot = t % (HALF // width)
-                if slot == 0:
-                    acc = close_bank((2, g, span, t))
                 nc.vector.scalar_tensor_tensor(
                     out=x2[:, t, :],
-                    in0=acc[:, slot, :],
+                    in0=close_bank((2, g, half, t))[:],
                     scalar=prop[:, g, t : t + 1],
-                    in1=x1[g][:, t, first : first + width],
+                    in1=x1[g][:, t, columns(half)],
                     op0=MULT,
                     op1=ADD,
                 )
 
+        def add_x1_aside(g, half, t, factor):
+            x2 = stage("x2", g, half, [P, PACK, HALF])
+            scaled = work.tile([P, HALF], F32, name="scaled", bufs=1)
+            nc.scalar.activation(out=scaled[:], in_=close_bank((2, g, half, t))[:], func=COPY, scale=factor)
+            nc.gpsimd.tensor_tensor(out=x2[:, t, :], in0=scaled[:], in1=x1[g][:, t, columns(half)], op=ADD)
+
         x2q = [kept([P, C], U32, f"x2q_{g}") for g in range(GROUPS)]
         x2q_scales = [kept([P, C], U8, f"x2q_scales_{g}") for g in range(GROUPS)]
 
-        def interleave_x2(engine, g, span, cols):
-            grouped = stage("x2_grouped", (g, span), [P, span[1], PACK], 3)
-            interleave(engine, grouped[:, cols, :], staged["x2", (g, span)][:, :, cols])
+        def interleave_x2(engine, g, half, part):
+            grouped = stage("x2_grouped", g, half, [P, HALF, PACK])
+            interleave(engine, grouped[:, part, :], staged["x2", g, half][:, :, part])
 
-        def quantise_x2(g, span):
-            cols = slice(span[0], span[0] + span[1])
-            nc.vector.quantize_mx(
-                out=x2q[g][:, cols].bitcast(FP8X4),
-                scales=x2q_scales[g][:, cols],
-                in_=flat(staged["x2_grouped", (g, span)]),
-            )
+        def quantise_x2(g, half):
+            quantise(x2q[g][:, columns(half)], x2q_scales[g][:, columns(half)], staged["x2_grouped", g, half])
 
-        def multiply_b(span, k, out_tiles=range(OUT_TILES)):
-            first, width = span
-            cols = slice(first, first + width)
-            shared = HALF // width
+        def multiply_b(half, k, out_tiles):
             for j in out_tiles:
-                slot = j % shared
-                if k == 0 and slot == 0:
-                    open_bank((3, span, j), [P, shared, width])
+                if k == 0:
+                    open_bank((3, half, j), [P, HALF])
                 nc.tensor.matmul_mx(
-                    out=open_banks[3, span, j - slot][1][:, slot, :],
+                    out=open_banks[3, half, j][1][:],
                     lhsT=b_words[:, k, E2M1_BYTES * P * j : E2M1_BYTES * P * (j + 1)].bitcast(FP4X4),
                     lhsT_scale=b_scales[:, k, P * j : P * (j + 1)],
-                    rhs=x2q[k][:, cols].bitcast(FP8X4),
-                    rhs_scale=x2q_scales[k][:, cols],
-                    start=(k == 0 and slot == 0),
-                    stop=(k == GROUPS - 1 and slot == shared - 1),
+                    rhs=x2q[k][:, columns(half)].bitcast(FP8X4),
+                    rhs_scale=x2q_scales[k][:, columns(half)],
+                    start=(k == 0),
+                    stop=(k == GROUPS - 1),
                 )
 
-        responses = {}
-
-        def finish(span, banks):
-            first, width = span
-            cols = slice(first, first + width)
-            shared = HALF // width
-            for j in range(0, OUT_TILES, shared)[banks]:
+        def finish(half, out_tiles):
+            for j in out_tiles:
                 if j % 2 == 0:
-                    pair = work.tile([P, 2, HALF], F32, name="response", tag="x1_rounded", bufs=4, align_bytes=64)
-                    responses[span[0] // HALF * 2 + j // 2] = pair
-                response = responses[span[0] // HALF * 2 + j // 2][:, j % 2 : j % 2 + shared, :]
+                    pair = work.tile([P, 2, HALF], F32, name="response", tag="x1_rounded", bufs=ROUNDED_BUFS, align_bytes=64)
+                response = pair[:, j % 2, :]
                 nc.vector.tensor_tensor(
-                    out=response, in0=close_bank((3, span, j))[:], in1=rates[:, j : j + shared, cols], op=MULT
+                    out=response, in0=close_bank((3, half, j))[:], in1=rates[:, j, columns(half)], op=MULT
                 )
-                rows = out[P * j : P * (j + shared), cols].rearrange("(j p) c -> p j c", p=P)
-                nc.sync.dma_start(out=rows, in_=response)
+                nc.sync.dma_start(out=out[P * j : P * (j + 1), columns(half)], in_=response)
 
-        def both(step, *unit):
-            for pair in range(PACK // 2):
-                step(*unit, pair)
+        def shared(interleave_step, g, half):
+            interleave_step("gpsimd", g, half, slice(0, GPSIMD_SHARE))
+            interleave_step("scalar", g, half, slice(GPSIMD_SHARE, HALF))
 
-        def round_unit(g, half):
-            round_x1("gpsimd", g, half, front)
-            round_x1("scalar", g, half, back)
-
-        def interleave_x2_unit(g, span):
-            interleave_x2("gpsimd", g, span, slice(0, GPSIMD_SHARE))
-            interleave_x2("scalar", g, span, slice(GPSIMD_SHARE, HALF))
-
-        def interleave_x_unit(g, half):
-            interleave_x("gpsimd", g, half, slice(0, GPSIMD_SHARE))
-            interleave_x("scalar", g, half, slice(GPSIMD_SHARE, HALF))
-
-        def multiply_a_by_pass(g, half, k):
-            for t in range(PACK):
-                multiply_a_pass(g, half, t, k)
-
-        left, right = (0, HALF), (HALF, HALF)
-        third, fourth = (HALF, PART), (HALF + PART, PART)
-        whole = slice(None)
+        whole = slice(0, HALF)
         tiles = range(PACK)
         front, back = tiles[:2], tiles[2:]
+        pairs = range(PACK // 2)
 
         for k in range(GROUPS):
-            share = HEAD_SHARE if k == 0 else PART
-            interleave_x("scalar", k, 0, slice(0, share))
-            interleave_x("vector", k, 0, slice(share, HALF))
+            interleave_x("scalar", k, LEFT, slice(0, SCALAR_SHARES[k]))
+            interleave_x("vector", k, LEFT, slice(SCALAR_SHARES[k], HALF))
             reorder_early_words(k)
-            quantise_x(k, 0)
+            quantise_x(k, LEFT)
             for g in range(EARLY):
                 if k == 0:
-                    reorder_a_scales(g, slice(0, 1))
-                multiply_a_by_pass(g, 0, k)
+                    reorder_early_scales(slice(g, g + 1), slice(0, 1))
+                for t in tiles:
+                    multiply_a(g, LEFT, t, k)
             if k == 0:
-                for g in range(EARLY):
-                    reorder_a_scales(g, slice(1, GROUPS))
-        reorder_a_scales(2, whole)
-        reorder_words(a_words[2][:], a_last[:])
-        interleave_x("scalar", 0, 1, whole)
-        interleave_x_unit(1, 1)
-        interleave_x_unit(2, 1)
-        add_x(0, 0, tiles)
-        multiply_a(2, 0, tiles)
-        add_x(1, 0, front)
+                reorder_early_scales(slice(0, EARLY), slice(1, GROUPS))
+        reorder_last_scales()
+        reorder_last_words()
+
+        interleave_x("scalar", 0, RIGHT, whole)
+        shared(interleave_x, 1, RIGHT)
+        shared(interleave_x, 2, RIGHT)
+        add_x(0, LEFT, tiles)
+        multiply_a_tiles(2, LEFT, tiles)
+        add_x(1, LEFT, front)
         for g in range(GROUPS):
-            quantise_x(g, 1)
-        add_x(1, 0, back)
-        round_x1("scalar", 0, 0, tiles)
-        round_x1("scalar", 1, 0, front)
-        round_x1("gpsimd", 1, 0, back)
-        add_x(2, 0, front)
+            quantise_x(g, RIGHT)
+        add_x(1, LEFT, back)
+        round_x1("scalar", 0, LEFT, tiles)
+        round_x1("scalar", 1, LEFT, front)
+        round_x1("gpsimd", 1, LEFT, back)
+
+        add_x(2, LEFT, front)
         for k in range(GROUPS):
             for t in front:
-                multiply_a_pass(0, 1, t, k)
-        multiply_a(0, 1, back)
-        both(turn_x1, 0, 0)
-        add_x(0, 1, tiles)
-        regroup_x1(0, 0, 0)
-        round_unit(0, 1)
-        round_x1("gpsimd", 2, 0, front)
-        regroup_x1(0, 0, 1)
-        multiply_a(1, 1, front)
-        add_x(1, 1, front)
-        both(turn_x1, 0, 1)
-        both(turn_x1, 1, 0)
-        both(regroup_x1, 0, 1)
-        both(regroup_x1, 1, 0)
-        round_x1("scalar", 1, 1, front)
-        multiply_a(1, 1, back)
-        add_x(2, 0, back)
-        round_x1("scalar", 2, 0, back)
-        quantise_x1(0, 0)
-        quantise_x1(0, 1)
-        add_x(1, 1, back)
-        round_x1("gpsimd", 1, 1, back)
-        both(multiply_r, 0, left)
-        add_x1(0, left, tiles)
-        interleave_x2("scalar", 0, left, whole)
-        quantise_x1(1, 0)
-        both(multiply_r, 0, right)
-        add_x1(0, right, tiles)
-        both(turn_x1, 1, 1)
-        both(turn_x1, 2, 0)
-        both(regroup_x1, 1, 1)
-        both(regroup_x1, 2, 0)
-        quantise_x2(0, left)
-        multiply_a(2, 1, tiles)
-        add_x(2, 1, tiles[:1])
-        quantise_x1(1, 1)
-        add_x(2, 1, tiles[1:2])
-        quantise_x1(2, 0)
-        add_x(2, 1, tiles[2:])
-        round_x1("scalar", 2, 1, front)
-        interleave_x2("scalar", 0, right, whole)
-        round_x1("gpsimd", 2, 1, back)
-        both(multiply_r, 1, left)
-        add_x1(1, left, tiles)
-        both(turn_x1, 2, 1)
-        both(regroup_x1, 2, 1)
-        interleave_x2("scalar", 1, left, whole)
-        quantise_x2(0, right)
-        both(multiply_r, 1, right)
-        add_x1(1, right, tiles[:1])
-        quantise_x1(2, 1)
-        add_x1(1, right, tiles[1:])
-        interleave_x2("scalar", 1, right, whole)
-        both(multiply_r, 2, left)
-        quantise_x2(1, left)
-        add_x1(2, left, tiles)
-        interleave_x2_unit(2, left)
-        multiply_b(left, 0)
-        both(multiply_r, 2, right)
-        quantise_x2(1, right)
-        add_x1(2, right, tiles[:3])
-        quantise_x2(2, left)
-        add_x1(2, right, tiles[3:])
-        interleave_x2_unit(2, right)
-        multiply_b(left, 1)
-        multiply_b(right, 0, tiles[:3])
-        multiply_b(left, 2)
-        multiply_b(right, 0, tiles[3:])
-        multiply_b(right, 1)
-        finish(left, slice(0, 2))
-        quantise_x2(2, right)
-        finish(left, slice(2, 4))
-        multiply_b(right, 2)
-        finish(right, whole)
+                multiply_a(0, RIGHT, t, k)
+        multiply_a_tiles(0, RIGHT, back)
+        turn_x1(0, LEFT)
+        add_x(0, RIGHT, tiles)
+        regroup_x1(0, LEFT, pairs[:1])
+        round_x1("gpsimd", 0, RIGHT, front)
+        round_x1("scalar", 0, RIGHT, back)
+        round_x1("gpsimd", 2, LEFT, front)
+        regroup_x1(0, LEFT, pairs[1:])
+
+        multiply_a_tiles(1, RIGHT, front)
+        add_x(1, RIGHT, front)
+        turn_x1(0, RIGHT)
+        turn_x1(1, LEFT)
+        regroup_x1(0, RIGHT, pairs)
+        regroup_x1(1, LEFT, pairs)
+        round_x1("scalar", 1, RIGHT, front)
+        multiply_a_tiles(1, RIGHT, back)
+        add_x(2, LEFT, back)
+        round_x1("scalar", 2, LEFT, back)
+        factor = kept([P, 1], F32, "factor")
+        nc.scalar.copy(out=factor[:], in_=prop[:, 1, 0:1])
+        quantise_x1(0, LEFT)
+        quantise_x1(0, RIGHT)
+        add_x(1, RIGHT, back)
+        round_x1("gpsimd", 1, RIGHT, back)
+
+        multiply_r(0, LEFT)
+        add_x1(0, LEFT, tiles)
+        interleave_x2("scalar", 0, LEFT, whole)
+        quantise_x1(1, LEFT)
+        multiply_r(0, RIGHT)
+        add_x1(0, RIGHT, tiles)
+        turn_x1(1, RIGHT)
+        turn_x1(2, LEFT)
+        regroup_x1(1, RIGHT, pairs)
+        regroup_x1(2, LEFT, pairs)
+        quantise_x2(0, LEFT)
+
+        multiply_a_tiles(2, RIGHT, tiles)
+        add_x(2, RIGHT, tiles[:1])
+        quantise_x1(1, RIGHT)
+        add_x(2, RIGHT, tiles[1:2])
+        quantise_x1(2, LEFT)
+        add_x(2, RIGHT, back)
+        round_x1("scalar", 2, RIGHT, front)
+        interleave_x2("scalar", 0, RIGHT, whole)
+        round_x1("gpsimd", 2, RIGHT, back)
+
+        multiply_r(1, LEFT)
+        add_x1(1, LEFT, tiles)
+        turn_x1(2, RIGHT)
+        regroup_x1(2, RIGHT, pairs)
+        quantise_x2(0, RIGHT)
+        multiply_r(1, RIGHT)
+        quantise_x1(2, RIGHT)
+        add_x1_aside(1, RIGHT, 0, factor[:])
+        interleave_x2("scalar", 1, LEFT, whole)
+        add_x1(1, RIGHT, tiles[1:])
+        interleave_x2("scalar", 1, RIGHT, whole)
+
+        multiply_r(2, LEFT)
+        add_x1(2, LEFT, tiles[:1])
+        quantise_x2(1, LEFT)
+        add_x1(2, LEFT, tiles[1:])
+        shared(interleave_x2, 2, LEFT)
+        multiply_b(LEFT, 0, tiles)
+        multiply_r(2, RIGHT)
+        add_x1(2, RIGHT, tiles)
+        interleave_x2("scalar", 2, RIGHT, whole)
+        quantise_x2(2, LEFT)
+        quantise_x2(1, RIGHT)
+
+        multiply_b(LEFT, 1, tiles)
+        multiply_b(RIGHT, 0, tiles[:3])
+        multiply_b(LEFT, 2, tiles)
+        multiply_b(RIGHT, 0, tiles[3:])
+        multiply_b(RIGHT, 1, tiles)
+        finish(LEFT, front)
+        quantise_x2(2, RIGHT)
+        finish(LEFT, back)
+        multiply_b(RIGHT, 2, tiles)
+        finish(RIGHT, tiles)

@@ -302,7 +302,7 @@ def tile_household_bracket_response_t2_kernel(
                     stop=(k == GROUPS - 1),
                 )
 
-        def finish(half, out_tiles):
+        def finish(half, out_tiles, queues):
             for j in out_tiles:
                 if j % 2 == 0:
                     pair = work.tile([P, 2, HALF], F32, name="response", tag="x1_rounded", bufs=ROUNDED_BUFS, align_bytes=64)
@@ -310,7 +310,7 @@ def tile_household_bracket_response_t2_kernel(
                 nc.vector.tensor_tensor(
                     out=response, in0=close_bank((3, half, j))[:], in1=rates[:, j, columns(half)], op=MULT
                 )
-                nc.sync.dma_start(out=out[P * j : P * (j + 1), columns(half)], in_=response)
+                queues[j % len(queues)].dma_start(out=out[P * j : P * (j + 1), columns(half)], in_=response)
 
         def shared(interleave_step, g, half):
             interleave_step("gpsimd", g, half, slice(0, GPSIMD_SHARE))
@@ -430,8 +430,8 @@ def tile_household_bracket_response_t2_kernel(
         multiply_b(LEFT, 2, tiles)
         multiply_b(RIGHT, 0, tiles[3:])
         multiply_b(RIGHT, 1, tiles)
-        finish(LEFT, front)
+        finish(LEFT, front, [nc.sync])
         quantise_x2(2, RIGHT)
-        finish(LEFT, back)
+        finish(LEFT, back, [nc.scalar, nc.sync])
         multiply_b(RIGHT, 2, tiles)
-        finish(RIGHT, tiles)
+        finish(RIGHT, tiles, [nc.scalar, nc.sync])

@@ -30,8 +30,9 @@ BANKS = 8
 E2M1_BYTES = 2
 EARLY = BANKS // PACK
 RUN = 4
-SCALAR_SHARES = (192, 320, 256)
-GPSIMD_SHARE = 208
+SCALAR_SHARE = 176
+GPSIMD_SHARES = (224, 96)
+LAST_SHARE = 352
 
 
 def tile_household_bracket_response_t2_kernel(
@@ -60,11 +61,12 @@ def tile_household_bracket_response_t2_kernel(
         def columns(half):
             return slice(HALF * half, HALF * (half + 1))
 
-        a_scales_early = kept([P, GROUPS, EARLY * K_PASS], U8, "a_scales_early")
+        a_scales_first = kept([P, 1, EARLY * K_PASS], U8, "a_scales_first")
+        a_scales_early = kept([P, GROUPS - 1, EARLY * K_PASS], U8, "a_scales_early")
         a_scales_last = kept([P, GROUPS, K_PASS], U8, "a_scales_last")
         r_scales = kept([P, HALVES, C], U8, "r_scales")
         b_scales = kept([P, GROUPS, G], U8, "b_scales")
-        for plane in (a_scales_early, a_scales_last, r_scales, b_scales):
+        for plane in (a_scales_first, a_scales_early, a_scales_last, r_scales, b_scales):
             nc.vector.memset(plane[:].bitcast(I32), 0)
         identity = kept([P, P], F32, "identity")
         make_identity(nc, identity[:])
@@ -98,9 +100,11 @@ def tile_household_bracket_response_t2_kernel(
 
         for k in range(GROUPS):
             load_x(k, LEFT)
-            load_a_early(k)
             if k == 0:
-                load_scales(a_scales_early, transfer_scales[:, :, : EARLY * K_PASS])
+                load_scales(a_scales_first, transfer_scales[:1, :, : EARLY * K_PASS])
+            if k == 1:
+                load_scales(a_scales_early, transfer_scales[1:, :, : EARLY * K_PASS])
+            load_a_early(k)
         load_scales(a_scales_last, transfer_scales[:, :, EARLY * K_PASS :])
         load_words(a_last, transfer_words[:, :, E2M1_BYTES * EARLY * K_PASS :])
         for g in range(GROUPS):
@@ -129,9 +133,9 @@ def tile_household_bracket_response_t2_kernel(
         staged = {}
         ROUNDED_BUFS = 4
 
-        def stage(kind, g, half, shape, bufs=3):
+        def stage(kind, g, half, shape, bufs=3, tag=None, dtype=BF16):
             if (kind, g, half) not in staged:
-                tile = work.tile(shape, BF16, name=kind, tag=kind, bufs=bufs, align_bytes=64)
+                tile = work.tile(shape, dtype, name=kind, tag=tag or kind, bufs=bufs, align_bytes=64)
                 staged[kind, g, half] = tile
             return staged[kind, g, half]
 
@@ -151,25 +155,27 @@ def tile_household_bracket_response_t2_kernel(
             )
 
         def quantise(codes, scales, grouped):
-            nc.vector.quantize_mx(out=codes.bitcast(FP8X4), scales=scales, in_=grouped[:].rearrange("p c t -> p (c t)"))
+            nc.vector.quantize_mx(out=codes.bitcast(FP8X4), scales=scales, in_=grouped.rearrange("p c t -> p (c t)"))
 
         a_words = kept([P, GROUPS, PACK, GROUPS, E2M1_BYTES * P], U8, "a_words")
         a_scales = kept([P, GROUPS, PACK, GROUPS, P], U8, "a_scales")
 
-        def reorder_early_words(k):
-            nc.vector.tensor_copy(
-                out=a_words[:, :EARLY, :, k, :].bitcast(U16).rearrange("p g t (m i) -> p g m t i", i=RUN),
-                in_=a_early[k][:].bitcast(U16).rearrange("p g (m i t) -> p g m t i", i=RUN, t=PACK),
+        def reorder_early_words(engine, groups, k):
+            copy(
+                engine,
+                a_words[:, groups, :, k, :].bitcast(U16).rearrange("p g t (m i) -> p g m t i", i=RUN),
+                a_early[k][:, groups, :].bitcast(U16).rearrange("p g (m i t) -> p g m t i", i=RUN, t=PACK),
             )
 
-        def reorder_last_words():
-            nc.vector.tensor_copy(
-                out=a_words[:, EARLY, :, :, :].bitcast(U16).rearrange("p t k (m i) -> p k m t i", i=RUN),
-                in_=a_last[:].bitcast(U16).rearrange("p k (m i t) -> p k m t i", i=RUN, t=PACK),
+        def reorder_last_words(engine):
+            copy(
+                engine,
+                a_words[:, EARLY, :, :, :].bitcast(U16).rearrange("p t k (m i) -> p k m t i", i=RUN),
+                a_last[:].bitcast(U16).rearrange("p k (m i t) -> p k m t i", i=RUN, t=PACK),
             )
 
-        def reorder_early_scales(groups, passes):
-            scales_in = a_scales_early[:, passes, :].rearrange("p k (g m t) -> p g t k m", g=EARLY, t=PACK)
+        def reorder_early_scales(plane, groups, passes):
+            scales_in = plane[:].rearrange("p k (g m t) -> p g t k m", g=EARLY, t=PACK)
             nc.vector.tensor_copy(out=a_scales[:, groups, :, passes, :], in_=scales_in[:, groups, :, :, :])
 
         def reorder_last_scales():
@@ -181,11 +187,11 @@ def tile_household_bracket_response_t2_kernel(
         xq_scales = [kept([P, C], U8, f"xq_scales_{g}") for g in range(GROUPS)]
 
         def interleave_x(engine, g, half, part):
-            grouped = stage("x_grouped", g, half, [P, HALF, PACK])
+            grouped = stage("x_grouped", g, half, [P, HALF, PACK], tag="grouped")
             interleave(engine, grouped[:, part, :], x_in[g][half][:, :, part])
 
         def quantise_x(g, half):
-            quantise(xq[g][:, columns(half)], xq_scales[g][:, columns(half)], staged["x_grouped", g, half])
+            quantise(xq[g][:, columns(half)], xq_scales[g][:, columns(half)], staged["x_grouped", g, half][:])
 
         x1 = [kept([P, PACK, C], F32, f"x1_{g}") for g in range(GROUPS)]
 
@@ -234,20 +240,21 @@ def tile_household_bracket_response_t2_kernel(
                         words = rounded[:, 2 * pair + i, u, :, :].rearrange("p w e -> p (w e)").bitcast(F32)
                         nc.tensor.transpose(turned[:, i, u, :], words, identity[:])
 
-        def regroup_x1(g, half, pairs):
+        def regroup_x1(engine, g, half, pairs):
             grouped = stage("x1_grouped", g, half, [P, K_PASS, PACK])
             for pair in pairs:
                 words = grouped[:, 2 * P * pair : 2 * P * (pair + 1), :].rearrange("p m v -> p (m v)").bitcast(F32)
-                nc.scalar.copy(
-                    out=words.rearrange("p (i m u) -> p i m u", i=2, u=2),
-                    in_=close_bank(("turn", g, half, pair))[:].rearrange("p i u m -> p i m u"),
+                copy(
+                    engine,
+                    words.rearrange("p (i m u) -> p i m u", i=2, u=2),
+                    close_bank(("turn", g, half, pair))[:].rearrange("p i u m -> p i m u"),
                 )
 
         def quantise_x1(g, half):
-            quantise(x1q[g][half][:], x1q_scales[g][half][:], staged["x1_grouped", g, half])
+            quantise(x1q[g][half][:], x1q_scales[g][half][:], staged["x1_grouped", g, half][:])
 
-        def multiply_r(g, half):
-            for t in range(PACK):
+        def multiply_r(g, half, tiles):
+            for t in tiles:
                 acc = open_bank((2, g, half, t), [P, HALF])
                 for k in range(HALVES):
                     nc.tensor.matmul_mx(
@@ -272,21 +279,31 @@ def tile_household_bracket_response_t2_kernel(
                     op1=ADD,
                 )
 
-        def add_x1_aside(g, half, t, factor):
-            x2 = stage("x2", g, half, [P, PACK, HALF])
-            scaled = work.tile([P, HALF], F32, name="scaled", bufs=1)
-            nc.scalar.activation(out=scaled[:], in_=close_bank((2, g, half, t))[:], func=COPY, scale=factor)
-            nc.gpsimd.tensor_tensor(out=x2[:, t, :], in0=scaled[:], in1=x1[g][:, t, columns(half)], op=ADD)
+        def scale_aside(g, half, tiles):
+            scaled = stage("scaled", g, half, [P, PACK, HALF], bufs=1, dtype=F32)
+            for t in tiles:
+                nc.scalar.activation(
+                    out=scaled[:, t, :], in_=close_bank((2, g, half, t))[:], func=COPY, scale=factors[:, g, t : t + 1]
+                )
+
+        def add_aside(g, half, part):
+            grouped = stage("x2_grouped", g, half, [P, HALF, PACK], tag="grouped")
+            nc.gpsimd.tensor_tensor(
+                out=grouped[:, part, :].rearrange("p (c i) t -> p c t i", i=RUN),
+                in0=staged["scaled", g, half][:, :, part].rearrange("p t (c i) -> p c t i", i=RUN),
+                in1=x1[g][:, :, columns(half)][:, :, part].rearrange("p t (c i) -> p c t i", i=RUN),
+                op=ADD,
+            )
 
         x2q = [kept([P, C], U32, f"x2q_{g}") for g in range(GROUPS)]
         x2q_scales = [kept([P, C], U8, f"x2q_scales_{g}") for g in range(GROUPS)]
 
         def interleave_x2(engine, g, half, part):
-            grouped = stage("x2_grouped", g, half, [P, HALF, PACK])
+            grouped = stage("x2_grouped", g, half, [P, HALF, PACK], tag="grouped")
             interleave(engine, grouped[:, part, :], staged["x2", g, half][:, :, part])
 
         def quantise_x2(g, half):
-            quantise(x2q[g][:, columns(half)], x2q_scales[g][:, columns(half)], staged["x2_grouped", g, half])
+            quantise(x2q[g][:, columns(half)], x2q_scales[g][:, columns(half)], staged["x2_grouped", g, half][:])
 
         def multiply_b(half, k, out_tiles):
             for j in out_tiles:
@@ -304,134 +321,135 @@ def tile_household_bracket_response_t2_kernel(
 
         def finish(half, out_tiles, queues):
             for j in out_tiles:
-                if j % 2 == 0:
-                    pair = work.tile([P, 2, HALF], F32, name="response", tag="x1_rounded", bufs=ROUNDED_BUFS, align_bytes=64)
+                pair = stage("response", j // 2, half, [P, 2, HALF], ROUNDED_BUFS, tag="x1_rounded", dtype=F32)
                 response = pair[:, j % 2, :]
                 nc.vector.tensor_tensor(
                     out=response, in0=close_bank((3, half, j))[:], in1=rates[:, j, columns(half)], op=MULT
                 )
                 queues[j % len(queues)].dma_start(out=out[P * j : P * (j + 1), columns(half)], in_=response)
 
-        def shared(interleave_step, g, half):
-            interleave_step("gpsimd", g, half, slice(0, GPSIMD_SHARE))
-            interleave_step("scalar", g, half, slice(GPSIMD_SHARE, HALF))
-
         whole = slice(0, HALF)
         tiles = range(PACK)
         front, back = tiles[:2], tiles[2:]
         pairs = range(PACK // 2)
 
+        factors = kept([P, GROUPS, PACK], F32, "factors")
+        quarters = [slice(P * q, P * (q + 1)) for q in range(PACK)]
+        early = slice(0, EARLY)
         for k in range(GROUPS):
-            interleave_x("scalar", k, LEFT, slice(0, SCALAR_SHARES[k]))
-            interleave_x("vector", k, LEFT, slice(SCALAR_SHARES[k], HALF))
-            reorder_early_words(k)
-            quantise_x(k, LEFT)
+            interleave_x("scalar", k, LEFT, slice(0, SCALAR_SHARE))
+            interleave_x("vector", k, LEFT, slice(SCALAR_SHARE, HALF))
+            if k == 0:
+                reorder_early_scales(a_scales_first, slice(0, 1), slice(0, 1))
+                reorder_early_words("scalar", slice(0, 1), k)
+                quantise_x(k, LEFT)
+                reorder_early_scales(a_scales_first, slice(1, 2), slice(0, 1))
+                reorder_early_words("vector", slice(1, 2), k)
+            elif k == 1:
+                quantise_x(k, LEFT)
+                reorder_early_scales(a_scales_early, early, slice(1, GROUPS))
+                reorder_early_words("scalar", early, k)
+            else:
+                reorder_early_words("scalar", early, k)
+                quantise_x(k, LEFT)
             for g in range(EARLY):
-                if k == 0:
-                    reorder_early_scales(slice(g, g + 1), slice(0, 1))
                 for t in tiles:
                     multiply_a(g, LEFT, t, k)
-            if k == 0:
-                reorder_early_scales(slice(0, EARLY), slice(1, GROUPS))
         reorder_last_scales()
-        reorder_last_words()
+        reorder_last_words("scalar")
 
         interleave_x("scalar", 0, RIGHT, whole)
-        shared(interleave_x, 1, RIGHT)
-        shared(interleave_x, 2, RIGHT)
         add_x(0, LEFT, tiles)
         multiply_a_tiles(2, LEFT, tiles)
-        add_x(1, LEFT, front)
-        for g in range(GROUPS):
-            quantise_x(g, RIGHT)
-        add_x(1, LEFT, back)
-        round_x1("scalar", 0, LEFT, tiles)
-        round_x1("scalar", 1, LEFT, front)
-        round_x1("gpsimd", 1, LEFT, back)
-
-        add_x(2, LEFT, front)
+        interleave_x("gpsimd", 1, RIGHT, slice(0, GPSIMD_SHARES[0]))
+        interleave_x("scalar", 1, RIGHT, slice(GPSIMD_SHARES[0], HALF))
+        interleave_x("gpsimd", 2, RIGHT, slice(0, GPSIMD_SHARES[1]))
+        interleave_x("scalar", 2, RIGHT, slice(GPSIMD_SHARES[1], HALF))
+        add_x(1, LEFT, tiles[:3])
+        quantise_x(0, RIGHT)
+        add_x(1, LEFT, tiles[3:])
+        quantise_x(1, RIGHT)
+        add_x(2, LEFT, tiles[:1])
+        quantise_x(2, RIGHT)
         for k in range(GROUPS):
-            for t in front:
+            for t in tiles:
                 multiply_a(0, RIGHT, t, k)
-        multiply_a_tiles(0, RIGHT, back)
+        round_x1("scalar", 0, LEFT, tiles)
+        add_x(2, LEFT, tiles[1:])
+        round_x1("scalar", 1, LEFT, front)
+        round_x1("gpsimd", 2, LEFT, front)
+        round_x1("gpsimd", 1, LEFT, back)
         turn_x1(0, LEFT)
         add_x(0, RIGHT, tiles)
-        regroup_x1(0, LEFT, pairs[:1])
+        regroup_x1("scalar", 0, LEFT, pairs)
         round_x1("gpsimd", 0, RIGHT, front)
         round_x1("scalar", 0, RIGHT, back)
-        round_x1("gpsimd", 2, LEFT, front)
-        regroup_x1(0, LEFT, pairs[1:])
-
+        round_x1("gpsimd", 2, LEFT, back)
         multiply_a_tiles(1, RIGHT, front)
         add_x(1, RIGHT, front)
-        turn_x1(0, RIGHT)
         turn_x1(1, LEFT)
-        regroup_x1(0, RIGHT, pairs)
-        regroup_x1(1, LEFT, pairs)
-        round_x1("scalar", 1, RIGHT, front)
+        turn_x1(0, RIGHT)
+        regroup_x1("scalar", 0, RIGHT, pairs)
+        regroup_x1("scalar", 1, LEFT, pairs)
         multiply_a_tiles(1, RIGHT, back)
-        add_x(2, LEFT, back)
-        round_x1("scalar", 2, LEFT, back)
-        factor = kept([P, 1], F32, "factor")
-        nc.scalar.copy(out=factor[:], in_=prop[:, 1, 0:1])
+        nc.scalar.copy(out=factors[:], in_=prop[:])
         quantise_x1(0, LEFT)
         quantise_x1(0, RIGHT)
         add_x(1, RIGHT, back)
+        round_x1("scalar", 1, RIGHT, front)
         round_x1("gpsimd", 1, RIGHT, back)
 
-        multiply_r(0, LEFT)
+        multiply_r(0, LEFT, tiles)
         add_x1(0, LEFT, tiles)
         interleave_x2("scalar", 0, LEFT, whole)
         quantise_x1(1, LEFT)
-        multiply_r(0, RIGHT)
+        multiply_r(0, RIGHT, tiles)
         add_x1(0, RIGHT, tiles)
         turn_x1(1, RIGHT)
         turn_x1(2, LEFT)
-        regroup_x1(1, RIGHT, pairs)
-        regroup_x1(2, LEFT, pairs)
+        regroup_x1("scalar", 1, RIGHT, pairs)
+        regroup_x1("scalar", 2, LEFT, pairs)
         quantise_x2(0, LEFT)
-
         multiply_a_tiles(2, RIGHT, tiles)
         add_x(2, RIGHT, tiles[:1])
         quantise_x1(1, RIGHT)
         add_x(2, RIGHT, tiles[1:2])
         quantise_x1(2, LEFT)
         add_x(2, RIGHT, back)
-        round_x1("scalar", 2, RIGHT, front)
         interleave_x2("scalar", 0, RIGHT, whole)
+        round_x1("scalar", 2, RIGHT, front)
         round_x1("gpsimd", 2, RIGHT, back)
 
-        multiply_r(1, LEFT)
+        multiply_r(1, LEFT, tiles)
         add_x1(1, LEFT, tiles)
         turn_x1(2, RIGHT)
-        regroup_x1(2, RIGHT, pairs)
-        quantise_x2(0, RIGHT)
-        multiply_r(1, RIGHT)
+        regroup_x1("scalar", 2, RIGHT, pairs)
+        interleave_x2("vector", 1, LEFT, slice(0, HALF // 2))
+        multiply_r(1, RIGHT, tiles)
         quantise_x1(2, RIGHT)
-        add_x1_aside(1, RIGHT, 0, factor[:])
-        interleave_x2("scalar", 1, LEFT, whole)
-        add_x1(1, RIGHT, tiles[1:])
-        interleave_x2("scalar", 1, RIGHT, whole)
-
-        multiply_r(2, LEFT)
-        add_x1(2, LEFT, tiles[:1])
+        interleave_x2("vector", 1, LEFT, slice(HALF // 2, HALF))
+        quantise_x2(0, RIGHT)
         quantise_x2(1, LEFT)
-        add_x1(2, LEFT, tiles[1:])
-        shared(interleave_x2, 2, LEFT)
-        multiply_b(LEFT, 0, tiles)
-        multiply_r(2, RIGHT)
+        scale_aside(1, RIGHT, tiles)
+        multiply_r(2, LEFT, tiles)
+        add_x1(2, LEFT, tiles)
+        for q in quarters:
+            add_aside(1, RIGHT, q)
+        interleave_x2("scalar", 2, LEFT, whole)
+        multiply_r(2, RIGHT, tiles)
         add_x1(2, RIGHT, tiles)
-        interleave_x2("scalar", 2, RIGHT, whole)
+        interleave_x2("scalar", 2, RIGHT, slice(0, LAST_SHARE))
         quantise_x2(2, LEFT)
         quantise_x2(1, RIGHT)
-
-        multiply_b(LEFT, 1, tiles)
-        multiply_b(RIGHT, 0, tiles[:3])
-        multiply_b(LEFT, 2, tiles)
-        multiply_b(RIGHT, 0, tiles[3:])
-        multiply_b(RIGHT, 1, tiles)
-        finish(LEFT, front, [nc.sync])
+        interleave_x2("vector", 2, RIGHT, slice(LAST_SHARE, HALF))
+        for k in range(GROUPS):
+            multiply_b(LEFT, k, tiles)
+        finish(LEFT, tiles[:1], [nc.sync])
         quantise_x2(2, RIGHT)
-        finish(LEFT, back, [nc.scalar, nc.sync])
-        multiply_b(RIGHT, 2, tiles)
-        finish(RIGHT, tiles, [nc.scalar, nc.sync])
+        finish(LEFT, tiles[1:], [nc.sync, nc.scalar])
+        for k in range(GROUPS):
+            multiply_b(RIGHT, k, front)
+        for j in back:
+            for k in range(GROUPS):
+                multiply_b(RIGHT, k, [j])
+        finish(RIGHT, tiles, [nc.sync, nc.scalar])

@@ -32,7 +32,7 @@ EARLY = BANKS // PACK
 RUN = 4
 SCALAR_SHARE = 176
 GPSIMD_SHARES = (224, 96)
-LAST_SHARE = 352
+GPSIMD_SHARE = 208
 
 
 def tile_household_bracket_response_t2_kernel(
@@ -279,21 +279,13 @@ def tile_household_bracket_response_t2_kernel(
                     op1=ADD,
                 )
 
-        def scale_aside(g, half, tiles):
-            scaled = stage("scaled", g, half, [P, PACK, HALF], bufs=1, dtype=F32)
-            for t in tiles:
-                nc.scalar.activation(
-                    out=scaled[:, t, :], in_=close_bank((2, g, half, t))[:], func=COPY, scale=factors[:, g, t : t + 1]
-                )
-
-        def add_aside(g, half, part):
-            grouped = stage("x2_grouped", g, half, [P, HALF, PACK], tag="grouped")
-            nc.gpsimd.tensor_tensor(
-                out=grouped[:, part, :].rearrange("p (c i) t -> p c t i", i=RUN),
-                in0=staged["scaled", g, half][:, :, part].rearrange("p t (c i) -> p c t i", i=RUN),
-                in1=x1[g][:, :, columns(half)][:, :, part].rearrange("p t (c i) -> p c t i", i=RUN),
-                op=ADD,
+        def add_x1_aside(g, half, t):
+            x2 = stage("x2", g, half, [P, PACK, HALF])
+            scaled = work.tile([P, HALF], F32, name="scaled", bufs=2)
+            nc.scalar.activation(
+                out=scaled[:], in_=close_bank((2, g, half, t))[:], func=COPY, scale=factors[:, g, t : t + 1]
             )
+            nc.gpsimd.tensor_tensor(out=x2[:, t, :], in0=scaled[:], in1=x1[g][:, t, columns(half)], op=ADD)
 
         x2q = [kept([P, C], U32, f"x2q_{g}") for g in range(GROUPS)]
         x2q_scales = [kept([P, C], U8, f"x2q_scales_{g}") for g in range(GROUPS)]
@@ -328,13 +320,16 @@ def tile_household_bracket_response_t2_kernel(
                 )
                 queues[j % len(queues)].dma_start(out=out[P * j : P * (j + 1), columns(half)], in_=response)
 
+        def shared(g, half):
+            interleave_x2("gpsimd", g, half, slice(0, GPSIMD_SHARE))
+            interleave_x2("scalar", g, half, slice(GPSIMD_SHARE, HALF))
+
         whole = slice(0, HALF)
         tiles = range(PACK)
         front, back = tiles[:2], tiles[2:]
         pairs = range(PACK // 2)
 
         factors = kept([P, GROUPS, PACK], F32, "factors")
-        quarters = [slice(P * q, P * (q + 1)) for q in range(PACK)]
         early = slice(0, EARLY)
         for k in range(GROUPS):
             interleave_x("scalar", k, LEFT, slice(0, SCALAR_SHARE))
@@ -410,46 +405,48 @@ def tile_household_bracket_response_t2_kernel(
         regroup_x1("scalar", 1, RIGHT, pairs)
         regroup_x1("scalar", 2, LEFT, pairs)
         quantise_x2(0, LEFT)
+
         multiply_a_tiles(2, RIGHT, tiles)
         add_x(2, RIGHT, tiles[:1])
         quantise_x1(1, RIGHT)
         add_x(2, RIGHT, tiles[1:2])
         quantise_x1(2, LEFT)
         add_x(2, RIGHT, back)
-        interleave_x2("scalar", 0, RIGHT, whole)
         round_x1("scalar", 2, RIGHT, front)
+        interleave_x2("scalar", 0, RIGHT, whole)
         round_x1("gpsimd", 2, RIGHT, back)
 
         multiply_r(1, LEFT, tiles)
         add_x1(1, LEFT, tiles)
         turn_x1(2, RIGHT)
         regroup_x1("scalar", 2, RIGHT, pairs)
-        interleave_x2("vector", 1, LEFT, slice(0, HALF // 2))
+        quantise_x2(0, RIGHT)
         multiply_r(1, RIGHT, tiles)
         quantise_x1(2, RIGHT)
-        interleave_x2("vector", 1, LEFT, slice(HALF // 2, HALF))
-        quantise_x2(0, RIGHT)
-        quantise_x2(1, LEFT)
-        scale_aside(1, RIGHT, tiles)
+        add_x1_aside(1, RIGHT, 0)
+        interleave_x2("scalar", 1, LEFT, whole)
+        add_x1(1, RIGHT, tiles[1:])
+        interleave_x2("scalar", 1, RIGHT, whole)
+
         multiply_r(2, LEFT, tiles)
-        add_x1(2, LEFT, tiles)
-        for q in quarters:
-            add_aside(1, RIGHT, q)
-        interleave_x2("scalar", 2, LEFT, whole)
+        add_x1(2, LEFT, tiles[:1])
+        quantise_x2(1, LEFT)
+        add_x1(2, LEFT, tiles[1:])
+        shared(2, LEFT)
+        multiply_b(LEFT, 0, tiles)
         multiply_r(2, RIGHT, tiles)
         add_x1(2, RIGHT, tiles)
-        interleave_x2("scalar", 2, RIGHT, slice(0, LAST_SHARE))
+        interleave_x2("scalar", 2, RIGHT, whole)
         quantise_x2(2, LEFT)
         quantise_x2(1, RIGHT)
-        interleave_x2("vector", 2, RIGHT, slice(LAST_SHARE, HALF))
-        for k in range(GROUPS):
-            multiply_b(LEFT, k, tiles)
-        finish(LEFT, tiles[:1], [nc.sync])
+
+        multiply_b(LEFT, 1, tiles)
+        multiply_b(RIGHT, 0, tiles[:3])
+        multiply_b(LEFT, 2, tiles)
+        multiply_b(RIGHT, 0, tiles[3:])
+        multiply_b(RIGHT, 1, tiles)
+        finish(LEFT, front, [nc.sync])
         quantise_x2(2, RIGHT)
-        finish(LEFT, tiles[1:], [nc.sync, nc.scalar])
-        for k in range(GROUPS):
-            multiply_b(RIGHT, k, front)
-        for j in back:
-            for k in range(GROUPS):
-                multiply_b(RIGHT, k, [j])
-        finish(RIGHT, tiles, [nc.sync, nc.scalar])
+        finish(LEFT, back, [nc.scalar, nc.sync])
+        multiply_b(RIGHT, 2, tiles)
+        finish(RIGHT, tiles, [nc.scalar, nc.sync])

@@ -29,6 +29,8 @@ OUT_TILES = G // P
 BANKS = 8
 E2M1_BYTES = 2
 EARLY = BANKS // PACK
+PLAIN = EARLY
+B_ORDER = (PLAIN, 0, 1)
 RUN = 4
 SCALAR_SHARE = 176
 GPSIMD_SHARES = (224, 96)
@@ -76,7 +78,9 @@ def tile_household_bracket_response_t2_kernel(
         a_last = kept([P, GROUPS, E2M1_BYTES * K_PASS], U8, "a_last")
         r_words = kept([P, HALVES, E2M1_BYTES * C], U8, "r_words")
         b_words = kept([P, GROUPS, E2M1_BYTES * G], U8, "b_words")
-        prop = kept([P, GROUPS, PACK], BF16, "prop")
+        x_plain = [kept([P, PACK, HALF], BF16, f"x_plain_{half}") for half in range(HALVES)]
+        prop = kept([P, EARLY, PACK], BF16, "prop")
+        prop_plain = kept([P, PACK, 2], BF16, "prop_plain")
         rates = kept([P, OUT_TILES, C], BF16, "rates")
 
         def load_scales(plane, scales):
@@ -105,13 +109,22 @@ def tile_household_bracket_response_t2_kernel(
             if k == 1:
                 load_scales(a_scales_early, transfer_scales[1:, :, : EARLY * K_PASS])
             load_a_early(k)
+        load_x(0, RIGHT)
         load_scales(a_scales_last, transfer_scales[:, :, EARLY * K_PASS :])
         load_words(a_last, transfer_words[:, :, E2M1_BYTES * EARLY * K_PASS :])
-        for g in range(GROUPS):
+        for g in range(1, GROUPS):
             load_x(g, RIGHT)
+        for half in range(HALVES):
+            rows = x[K_PASS * PLAIN :, columns(half)]
+            nc.sync.dma_start(out=x_plain[half][:], in_=rows.rearrange("(t p) c -> p t c", p=P))
         load_scales(r_scales, reclass_scales)
         load_words(r_words, reclass_words)
-        nc.sync.dma_start(out=prop[:], in_=propensity.rearrange("(g p t) -> p g t", p=P, t=PACK))
+        nc.sync.dma_start(out=prop[:], in_=propensity[: K_PASS * PLAIN].rearrange("(g p t) -> p g t", p=P, t=PACK))
+        nc.sync.dma_start(
+            out=prop_plain[:, :, 0:1],
+            in_=propensity[K_PASS * PLAIN :].rearrange("(t p o) -> p t o", p=P, o=1),
+            allow_slow_non_contiguous=True,
+        )
         load_scales(b_scales, bracket_scales)
         load_words(b_words, bracket_words)
         nc.sync.dma_start(out=rates[:], in_=rate.rearrange("(j p) c -> p j c", p=P))
@@ -157,8 +170,8 @@ def tile_household_bracket_response_t2_kernel(
         def quantise(codes, scales, grouped):
             nc.vector.quantize_mx(out=codes.bitcast(FP8X4), scales=scales, in_=grouped.rearrange("p c t -> p (c t)"))
 
-        a_words = kept([P, GROUPS, PACK, GROUPS, E2M1_BYTES * P], U8, "a_words")
-        a_scales = kept([P, GROUPS, PACK, GROUPS, P], U8, "a_scales")
+        a_words = kept([P, EARLY, PACK, GROUPS, E2M1_BYTES * P], U8, "a_words")
+        a_scales = kept([P, EARLY, PACK, GROUPS, P], U8, "a_scales")
 
         def reorder_early_words(engine, groups, k):
             copy(
@@ -167,21 +180,9 @@ def tile_household_bracket_response_t2_kernel(
                 a_early[k][:, groups, :].bitcast(U16).rearrange("p g (m i t) -> p g m t i", i=RUN, t=PACK),
             )
 
-        def reorder_last_words(engine):
-            copy(
-                engine,
-                a_words[:, EARLY, :, :, :].bitcast(U16).rearrange("p t k (m i) -> p k m t i", i=RUN),
-                a_last[:].bitcast(U16).rearrange("p k (m i t) -> p k m t i", i=RUN, t=PACK),
-            )
-
         def reorder_early_scales(plane, groups, passes):
-            scales_in = plane[:].rearrange("p k (g m t) -> p g t k m", g=EARLY, t=PACK)
+            scales_in = plane.rearrange("p k (g m t) -> p g t k m", g=EARLY, t=PACK)
             nc.vector.tensor_copy(out=a_scales[:, groups, :, passes, :], in_=scales_in[:, groups, :, :, :])
-
-        def reorder_last_scales():
-            nc.vector.tensor_copy(
-                out=a_scales[:, EARLY, :, :, :], in_=a_scales_last[:].rearrange("p k (m t) -> p t k m", t=PACK)
-            )
 
         xq = [kept([P, C], U32, f"xq_{g}") for g in range(GROUPS)]
         xq_scales = [kept([P, C], U8, f"xq_scales_{g}") for g in range(GROUPS)]
@@ -198,10 +199,15 @@ def tile_household_bracket_response_t2_kernel(
         def multiply_a(g, half, t, k):
             if k == 0:
                 open_bank((1, g, half, t), [P, HALF])
+            if g == PLAIN:
+                words = a_last[:, k, E2M1_BYTES * P * t : E2M1_BYTES * P * (t + 1)]
+                scales = a_scales_last[:, k, P * t : P * (t + 1)]
+            else:
+                words, scales = a_words[:, g, t, k, :], a_scales[:, g, t, k, :]
             nc.tensor.matmul_mx(
                 out=open_banks[1, g, half, t][1][:],
-                lhsT=a_words[:, g, t, k, :].bitcast(FP4X4),
-                lhsT_scale=a_scales[:, g, t, k, :],
+                lhsT=words.bitcast(FP4X4),
+                lhsT_scale=scales,
                 rhs=xq[k][:, columns(half)].bitcast(FP8X4),
                 rhs_scale=xq_scales[k][:, columns(half)],
                 start=(k == 0),
@@ -218,7 +224,7 @@ def tile_household_bracket_response_t2_kernel(
                 nc.vector.tensor_tensor(
                     out=x1[g][:, t, columns(half)],
                     in0=close_bank((1, g, half, t))[:],
-                    in1=x_in[g][half][:, t, :],
+                    in1=(x_plain[half] if g == PLAIN else x_in[g][half])[:, t, :],
                     op=ADD,
                 )
 
@@ -273,11 +279,16 @@ def tile_household_bracket_response_t2_kernel(
                 nc.vector.scalar_tensor_tensor(
                     out=x2[:, t, :],
                     in0=close_bank((2, g, half, t))[:],
-                    scalar=prop[:, g, t : t + 1],
+                    scalar=prop_plain[:, t, 0:1] if g == PLAIN else prop[:, g, t : t + 1],
                     in1=x1[g][:, t, columns(half)],
                     op0=MULT,
                     op1=ADD,
                 )
+
+        def move_x2(half, tiles):
+            moved = stage("x2_moved", PLAIN, half, [P, PACK, HALF], bufs=2)
+            for t in tiles:
+                nc.sync.dma_start(out=moved[32 * t : 32 * (t + 1), :, :], in_=staged["x2", PLAIN, half][:, t, :])
 
         def add_x1_aside(g, half, t):
             x2 = stage("x2", g, half, [P, PACK, HALF])
@@ -292,14 +303,14 @@ def tile_household_bracket_response_t2_kernel(
 
         def interleave_x2(engine, g, half, part):
             grouped = stage("x2_grouped", g, half, [P, HALF, PACK], tag="grouped")
-            interleave(engine, grouped[:, part, :], staged["x2", g, half][:, :, part])
+            interleave(engine, grouped[:, part, :], staged["x2_moved" if g == PLAIN else "x2", g, half][:, :, part])
 
         def quantise_x2(g, half):
             quantise(x2q[g][:, columns(half)], x2q_scales[g][:, columns(half)], staged["x2_grouped", g, half][:])
 
         def multiply_b(half, k, out_tiles):
             for j in out_tiles:
-                if k == 0:
+                if k == B_ORDER[0]:
                     open_bank((3, half, j), [P, HALF])
                 nc.tensor.matmul_mx(
                     out=open_banks[3, half, j][1][:],
@@ -307,8 +318,8 @@ def tile_household_bracket_response_t2_kernel(
                     lhsT_scale=b_scales[:, k, P * j : P * (j + 1)],
                     rhs=x2q[k][:, columns(half)].bitcast(FP8X4),
                     rhs_scale=x2q_scales[k][:, columns(half)],
-                    start=(k == 0),
-                    stop=(k == GROUPS - 1),
+                    start=(k == B_ORDER[0]),
+                    stop=(k == B_ORDER[-1]),
                 )
 
         def finish(half, out_tiles, queues):
@@ -329,124 +340,124 @@ def tile_household_bracket_response_t2_kernel(
         front, back = tiles[:2], tiles[2:]
         pairs = range(PACK // 2)
 
-        factors = kept([P, GROUPS, PACK], F32, "factors")
+        factors = kept([P, EARLY, PACK], F32, "factors")
         early = slice(0, EARLY)
         for k in range(GROUPS):
             interleave_x("scalar", k, LEFT, slice(0, SCALAR_SHARE))
             interleave_x("vector", k, LEFT, slice(SCALAR_SHARE, HALF))
             if k == 0:
-                reorder_early_scales(a_scales_first, slice(0, 1), slice(0, 1))
+                reorder_early_scales(a_scales_first[:], slice(0, 1), slice(0, 1))
                 reorder_early_words("scalar", slice(0, 1), k)
                 quantise_x(k, LEFT)
-                reorder_early_scales(a_scales_first, slice(1, 2), slice(0, 1))
+                reorder_early_scales(a_scales_first[:], slice(1, 2), slice(0, 1))
                 reorder_early_words("vector", slice(1, 2), k)
             elif k == 1:
+                reorder_early_scales(a_scales_early[:, :1, :], early, slice(1, 2))
                 quantise_x(k, LEFT)
-                reorder_early_scales(a_scales_early, early, slice(1, GROUPS))
-                reorder_early_words("scalar", early, k)
+                reorder_early_scales(a_scales_early[:, 1:, :], early, slice(2, GROUPS))
+                for g in range(EARLY):
+                    reorder_early_words("scalar", slice(g, g + 1), k)
             else:
-                reorder_early_words("scalar", early, k)
+                reorder_early_words("vector", early, k)
                 quantise_x(k, LEFT)
             for g in range(EARLY):
                 for t in tiles:
                     multiply_a(g, LEFT, t, k)
-        reorder_last_scales()
-        reorder_last_words("scalar")
 
-        interleave_x("scalar", 0, RIGHT, whole)
-        add_x(0, LEFT, tiles)
+        interleave_x("scalar", 0, RIGHT, slice(0, HALF - SCALAR_SHARE))
+        interleave_x("vector", 0, RIGHT, slice(HALF - SCALAR_SHARE, HALF))
+        add_x(0, LEFT, front)
+        quantise_x(0, RIGHT)
+        add_x(0, LEFT, back)
         multiply_a_tiles(2, LEFT, tiles)
         interleave_x("gpsimd", 1, RIGHT, slice(0, GPSIMD_SHARES[0]))
         interleave_x("scalar", 1, RIGHT, slice(GPSIMD_SHARES[0], HALF))
         interleave_x("gpsimd", 2, RIGHT, slice(0, GPSIMD_SHARES[1]))
         interleave_x("scalar", 2, RIGHT, slice(GPSIMD_SHARES[1], HALF))
-        add_x(1, LEFT, tiles[:3])
-        quantise_x(0, RIGHT)
-        add_x(1, LEFT, tiles[3:])
+        add_x(1, LEFT, tiles)
         quantise_x(1, RIGHT)
         add_x(2, LEFT, tiles[:1])
         quantise_x(2, RIGHT)
         for k in range(GROUPS):
             for t in tiles:
-                multiply_a(0, RIGHT, t, k)
+                multiply_a(2, RIGHT, t, k)
         round_x1("scalar", 0, LEFT, tiles)
         add_x(2, LEFT, tiles[1:])
-        round_x1("scalar", 1, LEFT, front)
-        round_x1("gpsimd", 2, LEFT, front)
-        round_x1("gpsimd", 1, LEFT, back)
+        round_x1("gpsimd", 2, LEFT, tiles)
         turn_x1(0, LEFT)
-        add_x(0, RIGHT, tiles)
+        add_x(2, RIGHT, tiles)
+        round_x1("scalar", 1, LEFT, front)
         regroup_x1("scalar", 0, LEFT, pairs)
-        round_x1("gpsimd", 0, RIGHT, front)
-        round_x1("scalar", 0, RIGHT, back)
-        round_x1("gpsimd", 2, LEFT, back)
-        multiply_a_tiles(1, RIGHT, front)
-        add_x(1, RIGHT, front)
-        turn_x1(1, LEFT)
+        round_x1("gpsimd", 2, RIGHT, tiles[:3])
+        round_x1("scalar", 2, RIGHT, tiles[3:])
+        multiply_a_tiles(0, RIGHT, front)
+        add_x(0, RIGHT, front)
+        turn_x1(2, LEFT)
+        turn_x1(2, RIGHT)
+        regroup_x1("scalar", 2, LEFT, pairs)
+        quantise_x1(0, LEFT)
+        regroup_x1("vector", 2, RIGHT, pairs[:1])
+        regroup_x1("scalar", 2, RIGHT, pairs[1:])
+        round_x1("scalar", 1, LEFT, back)
+        multiply_a_tiles(0, RIGHT, back)
+        nc.scalar.copy(out=factors[:], in_=prop[:])
+        quantise_x1(2, LEFT)
+        quantise_x1(2, RIGHT)
+        add_x(0, RIGHT, back)
+        round_x1("scalar", 0, RIGHT, front)
+        round_x1("gpsimd", 0, RIGHT, back)
+
+        for half in range(HALVES):
+            multiply_r(2, half, tiles)
+            for t in tiles:
+                add_x1(2, half, [t])
+                move_x2(half, [t])
         turn_x1(0, RIGHT)
+        turn_x1(1, LEFT)
         regroup_x1("scalar", 0, RIGHT, pairs)
         regroup_x1("scalar", 1, LEFT, pairs)
-        multiply_a_tiles(1, RIGHT, back)
-        nc.scalar.copy(out=factors[:], in_=prop[:])
-        quantise_x1(0, LEFT)
         quantise_x1(0, RIGHT)
-        add_x(1, RIGHT, back)
-        round_x1("scalar", 1, RIGHT, front)
-        round_x1("gpsimd", 1, RIGHT, back)
+
+        multiply_a_tiles(1, RIGHT, tiles)
+        add_x(1, RIGHT, tiles[:1])
+        quantise_x1(1, LEFT)
+        add_x(1, RIGHT, tiles[1:])
+        round_x1("gpsimd", 1, RIGHT, tiles)
+        interleave_x2("scalar", 2, LEFT, whole)
+        interleave_x2("scalar", 2, RIGHT, whole)
+        quantise_x2(2, LEFT)
 
         multiply_r(0, LEFT, tiles)
         add_x1(0, LEFT, tiles)
-        interleave_x2("scalar", 0, LEFT, whole)
-        quantise_x1(1, LEFT)
-        multiply_r(0, RIGHT, tiles)
-        add_x1(0, RIGHT, tiles)
         turn_x1(1, RIGHT)
-        turn_x1(2, LEFT)
         regroup_x1("scalar", 1, RIGHT, pairs)
-        regroup_x1("scalar", 2, LEFT, pairs)
-        quantise_x2(0, LEFT)
-
-        multiply_a_tiles(2, RIGHT, tiles)
-        add_x(2, RIGHT, tiles[:1])
+        quantise_x2(2, RIGHT)
+        multiply_r(0, RIGHT, tiles)
         quantise_x1(1, RIGHT)
-        add_x(2, RIGHT, tiles[1:2])
-        quantise_x1(2, LEFT)
-        add_x(2, RIGHT, back)
-        round_x1("scalar", 2, RIGHT, front)
+        add_x1_aside(0, RIGHT, 0)
+        interleave_x2("scalar", 0, LEFT, whole)
+        add_x1(0, RIGHT, tiles[1:])
         interleave_x2("scalar", 0, RIGHT, whole)
-        round_x1("gpsimd", 2, RIGHT, back)
 
         multiply_r(1, LEFT, tiles)
-        add_x1(1, LEFT, tiles)
-        turn_x1(2, RIGHT)
-        regroup_x1("scalar", 2, RIGHT, pairs)
-        quantise_x2(0, RIGHT)
-        multiply_r(1, RIGHT, tiles)
-        quantise_x1(2, RIGHT)
-        add_x1_aside(1, RIGHT, 0)
-        interleave_x2("scalar", 1, LEFT, whole)
-        add_x1(1, RIGHT, tiles[1:])
-        interleave_x2("scalar", 1, RIGHT, whole)
-
-        multiply_r(2, LEFT, tiles)
-        add_x1(2, LEFT, tiles[:1])
-        quantise_x2(1, LEFT)
-        add_x1(2, LEFT, tiles[1:])
-        shared(2, LEFT)
-        multiply_b(LEFT, 0, tiles)
-        multiply_r(2, RIGHT, tiles)
-        add_x1(2, RIGHT, tiles)
-        interleave_x2("scalar", 2, RIGHT, whole)
-        quantise_x2(2, LEFT)
-        quantise_x2(1, RIGHT)
-
-        multiply_b(LEFT, 1, tiles)
-        multiply_b(RIGHT, 0, tiles[:3])
+        add_x1(1, LEFT, tiles[:1])
+        quantise_x2(0, LEFT)
+        add_x1(1, LEFT, tiles[1:])
+        shared(1, LEFT)
         multiply_b(LEFT, 2, tiles)
-        multiply_b(RIGHT, 0, tiles[3:])
-        multiply_b(RIGHT, 1, tiles)
+        multiply_r(1, RIGHT, tiles)
+        add_x1(1, RIGHT, tiles)
+        interleave_x2("scalar", 1, RIGHT, whole)
+        quantise_x2(1, LEFT)
+        quantise_x2(0, RIGHT)
+
+        multiply_b(LEFT, 0, tiles)
+        multiply_b(RIGHT, 2, tiles[:3])
+        multiply_b(LEFT, 1, tiles)
+        multiply_b(RIGHT, 2, tiles[3:])
+        multiply_b(RIGHT, 0, tiles)
         finish(LEFT, front, [nc.sync])
-        quantise_x2(2, RIGHT)
+        quantise_x2(1, RIGHT)
         finish(LEFT, back, [nc.scalar, nc.sync])
-        multiply_b(RIGHT, 2, tiles)
+        multiply_b(RIGHT, 1, tiles)
         finish(RIGHT, tiles, [nc.scalar, nc.sync])

@@ -367,6 +367,7 @@ def tile_household_bracket_response_t2_kernel(
         interleave_x("scalar", 0, RIGHT, slice(0, HALF - SCALAR_SHARE))
         interleave_x("vector", 0, RIGHT, slice(HALF - SCALAR_SHARE, HALF))
         add_x(0, LEFT, front)
+        round_x1("scalar", 0, LEFT, front)
         quantise_x(0, RIGHT)
         add_x(0, LEFT, back)
         multiply_a_tiles(2, LEFT, tiles)
@@ -381,15 +382,15 @@ def tile_household_bracket_response_t2_kernel(
         for k in range(GROUPS):
             for t in tiles:
                 multiply_a(2, RIGHT, t, k)
-        round_x1("scalar", 0, LEFT, tiles)
+        round_x1("scalar", 0, LEFT, back)
         add_x(2, LEFT, tiles[1:])
-        round_x1("gpsimd", 2, LEFT, tiles)
+        round_x1("scalar", 2, LEFT, tiles[:3])
+        round_x1("gpsimd", 2, LEFT, tiles[3:])
         turn_x1(0, LEFT)
         add_x(2, RIGHT, tiles)
-        round_x1("scalar", 1, LEFT, front)
         regroup_x1("scalar", 0, LEFT, pairs)
-        round_x1("gpsimd", 2, RIGHT, tiles[:3])
-        round_x1("scalar", 2, RIGHT, tiles[3:])
+        round_x1("gpsimd", 2, RIGHT, front)
+        round_x1("scalar", 2, RIGHT, back)
         multiply_a_tiles(0, RIGHT, front)
         add_x(0, RIGHT, front)
         turn_x1(2, LEFT)
@@ -398,7 +399,6 @@ def tile_household_bracket_response_t2_kernel(
         quantise_x1(0, LEFT)
         regroup_x1("vector", 2, RIGHT, pairs[:1])
         regroup_x1("scalar", 2, RIGHT, pairs[1:])
-        round_x1("scalar", 1, LEFT, back)
         multiply_a_tiles(0, RIGHT, back)
         nc.scalar.copy(out=factors[:], in_=prop[:])
         quantise_x1(2, LEFT)
@@ -406,6 +406,7 @@ def tile_household_bracket_response_t2_kernel(
         add_x(0, RIGHT, back)
         round_x1("scalar", 0, RIGHT, front)
         round_x1("gpsimd", 0, RIGHT, back)
+        round_x1("scalar", 1, LEFT, tiles)
 
         for half in range(HALVES):
             multiply_r(2, half, tiles)
@@ -425,12 +426,12 @@ def tile_household_bracket_response_t2_kernel(
         round_x1("gpsimd", 1, RIGHT, tiles)
         interleave_x2("scalar", 2, LEFT, whole)
         interleave_x2("scalar", 2, RIGHT, whole)
-        quantise_x2(2, LEFT)
 
         multiply_r(0, LEFT, tiles)
         add_x1(0, LEFT, tiles)
         turn_x1(1, RIGHT)
         regroup_x1("scalar", 1, RIGHT, pairs)
+        quantise_x2(2, LEFT)
         quantise_x2(2, RIGHT)
         multiply_r(0, RIGHT, tiles)
         quantise_x1(1, RIGHT)
@@ -452,9 +453,9 @@ def tile_household_bracket_response_t2_kernel(
         quantise_x2(0, RIGHT)
 
         multiply_b(LEFT, 0, tiles)
-        multiply_b(RIGHT, 2, tiles[:3])
+        multiply_b(RIGHT, 2, front)
         multiply_b(LEFT, 1, tiles)
-        multiply_b(RIGHT, 2, tiles[3:])
+        multiply_b(RIGHT, 2, back)
         multiply_b(RIGHT, 0, tiles)
         finish(LEFT, front, [nc.sync])
         quantise_x2(1, RIGHT)

@@ -31,10 +31,12 @@ E2M1_BYTES = 2
 EARLY = BANKS // PACK
 PLAIN = EARLY
 B_ORDER = (PLAIN, 0, 1)
+WARM_UP_PASSES = 3
 RUN = 4
 SCALAR_SHARE = 176
 GPSIMD_SHARES = (224, 96)
 GPSIMD_SHARE = 208
+MOVED_SHARE = 208
 
 
 def tile_household_bracket_response_t2_kernel(
@@ -342,6 +344,25 @@ def tile_household_bracket_response_t2_kernel(
 
         factors = kept([P, EARLY, PACK], F32, "factors")
         early = slice(0, EARLY)
+
+        zeros = kept([P, P, PACK], BF16, "zeros")
+        zero_codes = kept([P, P], U32, "zero_codes")
+        zero_scales = kept([P, P], U8, "zero_scales")
+        nc.vector.memset(zeros[:].rearrange("p c t -> p (c t)").bitcast(I32), 0)
+        quantise(zero_codes[:], zero_scales[:], zeros[:])
+        unread = open_bank("warm-up", [P, HALF])
+        for repeat in range(WARM_UP_PASSES):
+            nc.tensor.matmul_mx(
+                out=unread[:],
+                lhsT=zero_codes[:].bitcast(FP8X4),
+                lhsT_scale=zero_scales[:],
+                rhs=a_scales_first[:, 0, :].bitcast(FP4X4),
+                rhs_scale=a_scales_first[:, 0, :HALF],
+                start=True,
+                stop=True,
+            )
+        close_bank("warm-up")
+
         for k in range(GROUPS):
             interleave_x("scalar", k, LEFT, slice(0, SCALAR_SHARE))
             interleave_x("vector", k, LEFT, slice(SCALAR_SHARE, HALF))
@@ -358,8 +379,9 @@ def tile_household_bracket_response_t2_kernel(
                 for g in range(EARLY):
                     reorder_early_words("scalar", slice(g, g + 1), k)
             else:
-                reorder_early_words("vector", early, k)
+                reorder_early_words("scalar", slice(0, 1), k)
                 quantise_x(k, LEFT)
+                reorder_early_words("vector", slice(1, 2), k)
             for g in range(EARLY):
                 for t in tiles:
                     multiply_a(g, LEFT, t, k)
@@ -423,9 +445,12 @@ def tile_household_bracket_response_t2_kernel(
         add_x(1, RIGHT, tiles[:1])
         quantise_x1(1, LEFT)
         add_x(1, RIGHT, tiles[1:])
-        round_x1("gpsimd", 1, RIGHT, tiles)
+        round_x1("scalar", 1, RIGHT, tiles[:1])
+        round_x1("gpsimd", 1, RIGHT, tiles[1:3])
         interleave_x2("scalar", 2, LEFT, whole)
-        interleave_x2("scalar", 2, RIGHT, whole)
+        round_x1("scalar", 1, RIGHT, tiles[3:])
+        interleave_x2("gpsimd", 2, RIGHT, slice(MOVED_SHARE, HALF))
+        interleave_x2("scalar", 2, RIGHT, slice(0, MOVED_SHARE))
 
         multiply_r(0, LEFT, tiles)
         add_x1(0, LEFT, tiles)

@@ -111,22 +111,23 @@ def tile_household_bracket_response_t2_kernel(
             if k == 1:
                 load_scales(a_scales_early, transfer_scales[1:, :, : EARLY * K_PASS])
             load_a_early(k)
-        load_x(0, RIGHT)
         load_scales(a_scales_last, transfer_scales[:, :, EARLY * K_PASS :])
         load_words(a_last, transfer_words[:, :, E2M1_BYTES * EARLY * K_PASS :])
-        for g in range(1, GROUPS):
+        for g in range(GROUPS):
             load_x(g, RIGHT)
         for half in range(HALVES):
-            rows = x[K_PASS * PLAIN :, columns(half)]
-            nc.sync.dma_start(out=x_plain[half][:], in_=rows.rearrange("(t p) c -> p t c", p=P))
+            rows = x[K_PASS * PLAIN :, columns(half)].rearrange("(a t e) c -> e a t c", t=PACK, e=2)
+            for e in range(2):
+                nc.sync.dma_start(out=x_plain[half][e:P:2, :, :], in_=rows[e, :, :, :])
         load_scales(r_scales, reclass_scales)
         load_words(r_words, reclass_words)
         nc.sync.dma_start(out=prop[:], in_=propensity[: K_PASS * PLAIN].rearrange("(g p t) -> p g t", p=P, t=PACK))
-        nc.sync.dma_start(
-            out=prop_plain[:, :, 0:1],
-            in_=propensity[K_PASS * PLAIN :].rearrange("(t p o) -> p t o", p=P, o=1),
-            allow_slow_non_contiguous=True,
-        )
+        for e in range(2):
+            nc.sync.dma_start(
+                out=prop_plain[e:P:2, :, 0:1],
+                in_=propensity[K_PASS * PLAIN :].rearrange("(a t e) -> a t e", t=PACK, e=2)[:, :, e : e + 1],
+                allow_slow_non_contiguous=True,
+            )
         load_scales(b_scales, bracket_scales)
         load_words(b_words, bracket_words)
         nc.sync.dma_start(out=rates[:], in_=rate.rearrange("(j p) c -> p j c", p=P))
@@ -172,14 +173,20 @@ def tile_household_bracket_response_t2_kernel(
         def quantise(codes, scales, grouped):
             nc.vector.quantize_mx(out=codes.bitcast(FP8X4), scales=scales, in_=grouped.rearrange("p c t -> p (c t)"))
 
-        a_words = kept([P, EARLY, PACK, GROUPS, E2M1_BYTES * P], U8, "a_words")
-        a_scales = kept([P, EARLY, PACK, GROUPS, P], U8, "a_scales")
+        a_words = kept([P, GROUPS, PACK, GROUPS, E2M1_BYTES * P], U8, "a_words")
+        a_scales = kept([P, GROUPS, PACK, GROUPS, P], U8, "a_scales")
 
         def reorder_early_words(engine, groups, k):
             copy(
                 engine,
                 a_words[:, groups, :, k, :].bitcast(U16).rearrange("p g t (m i) -> p g m t i", i=RUN),
                 a_early[k][:, groups, :].bitcast(U16).rearrange("p g (m i t) -> p g m t i", i=RUN, t=PACK),
+            )
+
+        def reorder_pairs(reordered, arrived, pair):
+            nc.scalar.copy(
+                out=reordered[:, PLAIN, :, :, :].bitcast(pair).rearrange("p t k (a i) -> p k a t i", i=RUN),
+                in_=arrived[:].bitcast(pair).rearrange("p k (a i t) -> p k a t i", i=RUN, t=PACK),
             )
 
         def reorder_early_scales(plane, groups, passes):
@@ -201,15 +208,10 @@ def tile_household_bracket_response_t2_kernel(
         def multiply_a(g, half, t, k):
             if k == 0:
                 open_bank((1, g, half, t), [P, HALF])
-            if g == PLAIN:
-                words = a_last[:, k, E2M1_BYTES * P * t : E2M1_BYTES * P * (t + 1)]
-                scales = a_scales_last[:, k, P * t : P * (t + 1)]
-            else:
-                words, scales = a_words[:, g, t, k, :], a_scales[:, g, t, k, :]
             nc.tensor.matmul_mx(
                 out=open_banks[1, g, half, t][1][:],
-                lhsT=words.bitcast(FP4X4),
-                lhsT_scale=scales,
+                lhsT=a_words[:, g, t, k, :].bitcast(FP4X4),
+                lhsT_scale=a_scales[:, g, t, k, :],
                 rhs=xq[k][:, columns(half)].bitcast(FP8X4),
                 rhs_scale=xq_scales[k][:, columns(half)],
                 start=(k == 0),
@@ -290,7 +292,8 @@ def tile_household_bracket_response_t2_kernel(
         def move_x2(half, tiles):
             moved = stage("x2_moved", PLAIN, half, [P, PACK, HALF], bufs=2)
             for t in tiles:
-                nc.sync.dma_start(out=moved[32 * t : 32 * (t + 1), :, :], in_=staged["x2", PLAIN, half][:, t, :])
+                u, v = divmod(t, 2)
+                nc.sync.dma_start(out=moved[u:P:2, 2 * v : 2 * v + 2, :], in_=staged["x2", PLAIN, half][:, t, :])
 
         def add_x1_aside(g, half, t):
             x2 = stage("x2", g, half, [P, PACK, HALF])
@@ -386,28 +389,29 @@ def tile_household_bracket_response_t2_kernel(
                 for t in tiles:
                     multiply_a(g, LEFT, t, k)
 
-        interleave_x("scalar", 0, RIGHT, slice(0, HALF - SCALAR_SHARE))
-        interleave_x("vector", 0, RIGHT, slice(HALF - SCALAR_SHARE, HALF))
-        add_x(0, LEFT, front)
-        round_x1("scalar", 0, LEFT, front)
-        quantise_x(0, RIGHT)
-        add_x(0, LEFT, back)
+        reorder_pairs(a_scales, a_scales_last, U16)
+        reorder_pairs(a_words, a_last, U32)
+        interleave_x("scalar", 0, RIGHT, whole)
+        add_x(0, LEFT, tiles)
         multiply_a_tiles(2, LEFT, tiles)
         interleave_x("gpsimd", 1, RIGHT, slice(0, GPSIMD_SHARES[0]))
         interleave_x("scalar", 1, RIGHT, slice(GPSIMD_SHARES[0], HALF))
         interleave_x("gpsimd", 2, RIGHT, slice(0, GPSIMD_SHARES[1]))
-        interleave_x("scalar", 2, RIGHT, slice(GPSIMD_SHARES[1], HALF))
-        add_x(1, LEFT, tiles)
+        interleave_x("scalar", 2, RIGHT, slice(2 * GPSIMD_SHARES[1], HALF))
+        add_x(1, LEFT, tiles[:3])
+        quantise_x(0, RIGHT)
+        add_x(1, LEFT, tiles[3:])
         quantise_x(1, RIGHT)
+        interleave_x("vector", 2, RIGHT, slice(GPSIMD_SHARES[1], 2 * GPSIMD_SHARES[1]))
         add_x(2, LEFT, tiles[:1])
         quantise_x(2, RIGHT)
         for k in range(GROUPS):
             for t in tiles:
                 multiply_a(2, RIGHT, t, k)
-        round_x1("scalar", 0, LEFT, back)
+        round_x1("scalar", 0, LEFT, tiles)
         add_x(2, LEFT, tiles[1:])
-        round_x1("scalar", 2, LEFT, tiles[:3])
-        round_x1("gpsimd", 2, LEFT, tiles[3:])
+        round_x1("scalar", 2, LEFT, front)
+        round_x1("gpsimd", 2, LEFT, back)
         turn_x1(0, LEFT)
         add_x(2, RIGHT, tiles)
         regroup_x1("scalar", 0, LEFT, pairs)
@@ -418,7 +422,6 @@ def tile_household_bracket_response_t2_kernel(
         turn_x1(2, LEFT)
         turn_x1(2, RIGHT)
         regroup_x1("scalar", 2, LEFT, pairs)
-        quantise_x1(0, LEFT)
         regroup_x1("vector", 2, RIGHT, pairs[:1])
         regroup_x1("scalar", 2, RIGHT, pairs[1:])
         multiply_a_tiles(0, RIGHT, back)
@@ -439,6 +442,7 @@ def tile_household_bracket_response_t2_kernel(
         turn_x1(1, LEFT)
         regroup_x1("scalar", 0, RIGHT, pairs)
         regroup_x1("scalar", 1, LEFT, pairs)
+        quantise_x1(0, LEFT)
         quantise_x1(0, RIGHT)
 
         multiply_a_tiles(1, RIGHT, tiles)

@@ -34,8 +34,8 @@ B_ORDER = (PLAIN, 0, 1)
 WARM_UP_PASSES = 3
 RUN = 4
 SCALAR_SHARE = 176
-GPSIMD_SHARES = (224, 96)
-GPSIMD_SHARE = 208
+GPSIMD_SHARES = (208, 208, 96)
+GPSIMD_SHARE = 288
 MOVED_SHARE = 208
 
 
@@ -391,18 +391,15 @@ def tile_household_bracket_response_t2_kernel(
 
         reorder_pairs(a_scales, a_scales_last, U16)
         reorder_pairs(a_words, a_last, U32)
-        interleave_x("scalar", 0, RIGHT, whole)
+        for g in range(GROUPS):
+            interleave_x("gpsimd", g, RIGHT, slice(0, GPSIMD_SHARES[g]))
+            interleave_x("scalar", g, RIGHT, slice(GPSIMD_SHARES[g], HALF))
         add_x(0, LEFT, tiles)
         multiply_a_tiles(2, LEFT, tiles)
-        interleave_x("gpsimd", 1, RIGHT, slice(0, GPSIMD_SHARES[0]))
-        interleave_x("scalar", 1, RIGHT, slice(GPSIMD_SHARES[0], HALF))
-        interleave_x("gpsimd", 2, RIGHT, slice(0, GPSIMD_SHARES[1]))
-        interleave_x("scalar", 2, RIGHT, slice(2 * GPSIMD_SHARES[1], HALF))
         add_x(1, LEFT, tiles[:3])
         quantise_x(0, RIGHT)
         add_x(1, LEFT, tiles[3:])
         quantise_x(1, RIGHT)
-        interleave_x("vector", 2, RIGHT, slice(GPSIMD_SHARES[1], 2 * GPSIMD_SHARES[1]))
         add_x(2, LEFT, tiles[:1])
         quantise_x(2, RIGHT)
         for k in range(GROUPS):
@@ -465,29 +462,28 @@ def tile_household_bracket_response_t2_kernel(
         multiply_r(0, RIGHT, tiles)
         quantise_x1(1, RIGHT)
         add_x1_aside(0, RIGHT, 0)
+        add_x1_aside(0, RIGHT, 1)
         interleave_x2("scalar", 0, LEFT, whole)
-        add_x1(0, RIGHT, tiles[1:])
+        add_x1(0, RIGHT, back)
         interleave_x2("scalar", 0, RIGHT, whole)
 
         multiply_r(1, LEFT, tiles)
-        add_x1(1, LEFT, tiles[:1])
+        add_x1(1, LEFT, tiles)
         quantise_x2(0, LEFT)
-        add_x1(1, LEFT, tiles[1:])
         shared(1, LEFT)
-        multiply_b(LEFT, 2, tiles)
         multiply_r(1, RIGHT, tiles)
         add_x1(1, RIGHT, tiles)
         interleave_x2("scalar", 1, RIGHT, whole)
         quantise_x2(1, LEFT)
         quantise_x2(0, RIGHT)
 
-        multiply_b(LEFT, 0, tiles)
-        multiply_b(RIGHT, 2, front)
-        multiply_b(LEFT, 1, tiles)
-        multiply_b(RIGHT, 2, back)
-        multiply_b(RIGHT, 0, tiles)
+        for k in B_ORDER:
+            multiply_b(LEFT, k, tiles)
+        multiply_b(RIGHT, 2, tiles)
         finish(LEFT, front, [nc.sync])
         quantise_x2(1, RIGHT)
         finish(LEFT, back, [nc.scalar, nc.sync])
-        multiply_b(RIGHT, 1, tiles)
+        for j in tiles:
+            multiply_b(RIGHT, 0, [j])
+            multiply_b(RIGHT, 1, [j])
         finish(RIGHT, tiles, [nc.scalar, nc.sync])

@@ -34,8 +34,9 @@ B_ORDER = (PLAIN, 0, 1)
 WARM_UP_PASSES = 3
 RUN = 4
 SCALAR_SHARE = 176
-GPSIMD_SHARES = (208, 208, 96)
-GPSIMD_SHARE = 288
+GPSIMD_SHARE = 208
+VECTOR_SHARE = 64
+LAST_SHARES = (224, 128)
 MOVED_SHARE = 208
 
 
@@ -336,9 +337,9 @@ def tile_household_bracket_response_t2_kernel(
                 )
                 queues[j % len(queues)].dma_start(out=out[P * j : P * (j + 1), columns(half)], in_=response)
 
-        def shared(g, half):
-            interleave_x2("gpsimd", g, half, slice(0, GPSIMD_SHARE))
-            interleave_x2("scalar", g, half, slice(GPSIMD_SHARE, HALF))
+        def shared(g, half, gpsimd_share):
+            interleave_x2("gpsimd", g, half, slice(0, gpsimd_share))
+            interleave_x2("scalar", g, half, slice(gpsimd_share, HALF))
 
         whole = slice(0, HALF)
         tiles = range(PACK)
@@ -391,15 +392,17 @@ def tile_household_bracket_response_t2_kernel(
 
         reorder_pairs(a_scales, a_scales_last, U16)
         reorder_pairs(a_words, a_last, U32)
-        for g in range(GROUPS):
-            interleave_x("gpsimd", g, RIGHT, slice(0, GPSIMD_SHARES[g]))
-            interleave_x("scalar", g, RIGHT, slice(GPSIMD_SHARES[g], HALF))
+        for g in range(EARLY):
+            interleave_x("gpsimd", g, RIGHT, slice(0, GPSIMD_SHARE))
+            interleave_x("scalar", g, RIGHT, slice(GPSIMD_SHARE, HALF))
+        interleave_x("scalar", 2, RIGHT, slice(VECTOR_SHARE, HALF))
         add_x(0, LEFT, tiles)
         multiply_a_tiles(2, LEFT, tiles)
         add_x(1, LEFT, tiles[:3])
         quantise_x(0, RIGHT)
         add_x(1, LEFT, tiles[3:])
         quantise_x(1, RIGHT)
+        interleave_x("vector", 2, RIGHT, slice(0, VECTOR_SHARE))
         add_x(2, LEFT, tiles[:1])
         quantise_x(2, RIGHT)
         for k in range(GROUPS):
@@ -465,12 +468,12 @@ def tile_household_bracket_response_t2_kernel(
         add_x1_aside(0, RIGHT, 1)
         interleave_x2("scalar", 0, LEFT, whole)
         add_x1(0, RIGHT, back)
-        interleave_x2("scalar", 0, RIGHT, whole)
 
         multiply_r(1, LEFT, tiles)
         add_x1(1, LEFT, tiles)
         quantise_x2(0, LEFT)
-        shared(1, LEFT)
+        shared(1, LEFT, LAST_SHARES[0])
+        shared(0, RIGHT, LAST_SHARES[1])
         multiply_r(1, RIGHT, tiles)
         add_x1(1, RIGHT, tiles)
         interleave_x2("scalar", 1, RIGHT, whole)

@@ -261,8 +261,9 @@ def tile_household_bracket_response_t2_kernel(
                     close_bank(("turn", g, half, pair))[:].rearrange("p i u m -> p i m u"),
                 )
 
-        def quantise_x1(g, half):
-            quantise(x1q[g][half][:], x1q_scales[g][half][:], staged["x1_grouped", g, half][:])
+        def quantise_x1(g, half, pairs):
+            part = slice(2 * P * pairs[0], 2 * P * (pairs[-1] + 1))
+            quantise(x1q[g][half][:, part], x1q_scales[g][half][:, part], staged["x1_grouped", g, half][:, part, :])
 
         def multiply_r(g, half, tiles):
             for t in tiles:
@@ -410,28 +411,29 @@ def tile_household_bracket_response_t2_kernel(
                 multiply_a(2, RIGHT, t, k)
         round_x1("scalar", 0, LEFT, tiles)
         add_x(2, LEFT, tiles[1:])
-        round_x1("scalar", 2, LEFT, front)
-        round_x1("gpsimd", 2, LEFT, back)
-        turn_x1(0, LEFT)
+        round_x1("scalar", 2, LEFT, tiles[:3])
+        round_x1("gpsimd", 2, LEFT, tiles[3:])
         add_x(2, RIGHT, tiles)
-        regroup_x1("scalar", 0, LEFT, pairs)
-        round_x1("gpsimd", 2, RIGHT, front)
-        round_x1("scalar", 2, RIGHT, back)
+        round_x1("gpsimd", 2, RIGHT, tiles[:1])
+        round_x1("scalar", 2, RIGHT, tiles[1:])
         multiply_a_tiles(0, RIGHT, front)
         add_x(0, RIGHT, front)
+        turn_x1(0, LEFT)
         turn_x1(2, LEFT)
         turn_x1(2, RIGHT)
-        regroup_x1("scalar", 2, LEFT, pairs)
-        regroup_x1("vector", 2, RIGHT, pairs[:1])
-        regroup_x1("scalar", 2, RIGHT, pairs[1:])
         multiply_a_tiles(0, RIGHT, back)
+        for pair in pairs:
+            for half in range(HALVES):
+                regroup_x1("vector" if (half, pair) == (RIGHT, 0) else "scalar", 2, half, [pair])
+            for half in range(HALVES):
+                quantise_x1(2, half, [pair])
+            add_x(0, RIGHT, [back[pair]])
+        regroup_x1("scalar", 0, LEFT, pairs)
         nc.scalar.copy(out=factors[:], in_=prop[:])
-        quantise_x1(2, LEFT)
-        quantise_x1(2, RIGHT)
-        add_x(0, RIGHT, back)
         round_x1("scalar", 0, RIGHT, front)
         round_x1("gpsimd", 0, RIGHT, back)
-        round_x1("scalar", 1, LEFT, tiles)
+        round_x1("scalar", 1, LEFT, front)
+        round_x1("gpsimd", 1, LEFT, back)
 
         for half in range(HALVES):
             multiply_r(2, half, tiles)
@@ -442,12 +444,12 @@ def tile_household_bracket_response_t2_kernel(
         turn_x1(1, LEFT)
         regroup_x1("scalar", 0, RIGHT, pairs)
         regroup_x1("scalar", 1, LEFT, pairs)
-        quantise_x1(0, LEFT)
-        quantise_x1(0, RIGHT)
+        quantise_x1(0, LEFT, pairs)
+        quantise_x1(0, RIGHT, pairs)
 
         multiply_a_tiles(1, RIGHT, tiles)
         add_x(1, RIGHT, tiles[:1])
-        quantise_x1(1, LEFT)
+        quantise_x1(1, LEFT, pairs)
         add_x(1, RIGHT, tiles[1:])
         round_x1("scalar", 1, RIGHT, tiles[:1])
         round_x1("gpsimd", 1, RIGHT, tiles[1:3])
@@ -463,7 +465,7 @@ def tile_household_bracket_response_t2_kernel(
         quantise_x2(2, LEFT)
         quantise_x2(2, RIGHT)
         multiply_r(0, RIGHT, tiles)
-        quantise_x1(1, RIGHT)
+        quantise_x1(1, RIGHT, pairs)
         add_x1_aside(0, RIGHT, 0)
         add_x1_aside(0, RIGHT, 1)
         interleave_x2("scalar", 0, LEFT, whole)

@@ -29,14 +29,14 @@ OUT_TILES = G // P
 BANKS = 8
 E2M1_BYTES = 2
 EARLY = BANKS // PACK
-PLAIN = EARLY
-B_ORDER = (PLAIN, 0, 1)
+PAIRED = EARLY
+B_ORDER = (PAIRED, 0, 1)
 WARM_UP_PASSES = 3
 RUN = 4
 SCALAR_SHARE = 176
 GPSIMD_SHARE = 208
 VECTOR_SHARE = 64
-LAST_SHARES = (224, 128)
+LAST_LEFT_SHARE, LAST_RIGHT_SHARE = 224, 144
 MOVED_SHARE = 208
 
 
@@ -81,9 +81,9 @@ def tile_household_bracket_response_t2_kernel(
         a_last = kept([P, GROUPS, E2M1_BYTES * K_PASS], U8, "a_last")
         r_words = kept([P, HALVES, E2M1_BYTES * C], U8, "r_words")
         b_words = kept([P, GROUPS, E2M1_BYTES * G], U8, "b_words")
-        x_plain = [kept([P, PACK, HALF], BF16, f"x_plain_{half}") for half in range(HALVES)]
+        x_paired = [kept([P, PACK, HALF], BF16, f"x_paired_{half}") for half in range(HALVES)]
         prop = kept([P, EARLY, PACK], BF16, "prop")
-        prop_plain = kept([P, PACK, 2], BF16, "prop_plain")
+        prop_paired = kept([P, PACK, 2], BF16, "prop_paired")
         rates = kept([P, OUT_TILES, C], BF16, "rates")
 
         def load_scales(plane, scales):
@@ -117,16 +117,16 @@ def tile_household_bracket_response_t2_kernel(
         for g in range(GROUPS):
             load_x(g, RIGHT)
         for half in range(HALVES):
-            rows = x[K_PASS * PLAIN :, columns(half)].rearrange("(a t e) c -> e a t c", t=PACK, e=2)
+            rows = x[K_PASS * PAIRED :, columns(half)].rearrange("(a t e) c -> e a t c", t=PACK, e=2)
             for e in range(2):
-                nc.sync.dma_start(out=x_plain[half][e:P:2, :, :], in_=rows[e, :, :, :])
+                nc.sync.dma_start(out=x_paired[half][e:P:2, :, :], in_=rows[e, :, :, :])
         load_scales(r_scales, reclass_scales)
         load_words(r_words, reclass_words)
-        nc.sync.dma_start(out=prop[:], in_=propensity[: K_PASS * PLAIN].rearrange("(g p t) -> p g t", p=P, t=PACK))
+        nc.sync.dma_start(out=prop[:], in_=propensity[: K_PASS * PAIRED].rearrange("(g p t) -> p g t", p=P, t=PACK))
         for e in range(2):
             nc.sync.dma_start(
-                out=prop_plain[e:P:2, :, 0:1],
-                in_=propensity[K_PASS * PLAIN :].rearrange("(a t e) -> a t e", t=PACK, e=2)[:, :, e : e + 1],
+                out=prop_paired[e:P:2, :, 0:1],
+                in_=propensity[K_PASS * PAIRED :].rearrange("(a t e) -> a t e", t=PACK, e=2)[:, :, e : e + 1],
                 allow_slow_non_contiguous=True,
             )
         load_scales(b_scales, bracket_scales)
@@ -186,7 +186,7 @@ def tile_household_bracket_response_t2_kernel(
 
         def reorder_pairs(reordered, arrived, pair):
             nc.scalar.copy(
-                out=reordered[:, PLAIN, :, :, :].bitcast(pair).rearrange("p t k (a i) -> p k a t i", i=RUN),
+                out=reordered[:, PAIRED, :, :, :].bitcast(pair).rearrange("p t k (a i) -> p k a t i", i=RUN),
                 in_=arrived[:].bitcast(pair).rearrange("p k (a i t) -> p k a t i", i=RUN, t=PACK),
             )
 
@@ -229,7 +229,7 @@ def tile_household_bracket_response_t2_kernel(
                 nc.vector.tensor_tensor(
                     out=x1[g][:, t, columns(half)],
                     in0=close_bank((1, g, half, t))[:],
-                    in1=(x_plain[half] if g == PLAIN else x_in[g][half])[:, t, :],
+                    in1=(x_paired[half] if g == PAIRED else x_in[g][half])[:, t, :],
                     op=ADD,
                 )
 
@@ -285,24 +285,22 @@ def tile_household_bracket_response_t2_kernel(
                 nc.vector.scalar_tensor_tensor(
                     out=x2[:, t, :],
                     in0=close_bank((2, g, half, t))[:],
-                    scalar=prop_plain[:, t, 0:1] if g == PLAIN else prop[:, g, t : t + 1],
+                    scalar=prop_paired[:, t, 0:1] if g == PAIRED else prop[:, g, t : t + 1],
                     in1=x1[g][:, t, columns(half)],
                     op0=MULT,
                     op1=ADD,
                 )
 
         def move_x2(half, tiles):
-            moved = stage("x2_moved", PLAIN, half, [P, PACK, HALF], bufs=2)
+            moved = stage("x2_moved", PAIRED, half, [P, PACK, HALF], bufs=HALVES)
             for t in tiles:
                 u, v = divmod(t, 2)
-                nc.sync.dma_start(out=moved[u:P:2, 2 * v : 2 * v + 2, :], in_=staged["x2", PLAIN, half][:, t, :])
+                nc.sync.dma_start(out=moved[u:P:2, 2 * v : 2 * v + 2, :], in_=staged["x2", PAIRED, half][:, t, :])
 
-        def add_x1_aside(g, half, t):
+        def add_x1_aside(g, half, t, factor):
             x2 = stage("x2", g, half, [P, PACK, HALF])
             scaled = work.tile([P, HALF], F32, name="scaled", bufs=2)
-            nc.scalar.activation(
-                out=scaled[:], in_=close_bank((2, g, half, t))[:], func=COPY, scale=factors[:, g, t : t + 1]
-            )
+            nc.scalar.activation(out=scaled[:], in_=close_bank((2, g, half, t))[:], func=COPY, scale=factor)
             nc.gpsimd.tensor_tensor(out=x2[:, t, :], in0=scaled[:], in1=x1[g][:, t, columns(half)], op=ADD)
 
         x2q = [kept([P, C], U32, f"x2q_{g}") for g in range(GROUPS)]
@@ -310,7 +308,7 @@ def tile_household_bracket_response_t2_kernel(
 
         def interleave_x2(engine, g, half, part):
             grouped = stage("x2_grouped", g, half, [P, HALF, PACK], tag="grouped")
-            interleave(engine, grouped[:, part, :], staged["x2_moved" if g == PLAIN else "x2", g, half][:, :, part])
+            interleave(engine, grouped[:, part, :], staged["x2_moved" if g == PAIRED else "x2", g, half][:, :, part])
 
         def quantise_x2(g, half):
             quantise(x2q[g][:, columns(half)], x2q_scales[g][:, columns(half)], staged["x2_grouped", g, half][:])
@@ -338,7 +336,7 @@ def tile_household_bracket_response_t2_kernel(
                 )
                 queues[j % len(queues)].dma_start(out=out[P * j : P * (j + 1), columns(half)], in_=response)
 
-        def shared(g, half, gpsimd_share):
+        def interleave_x2_shared(g, half, gpsimd_share):
             interleave_x2("gpsimd", g, half, slice(0, gpsimd_share))
             interleave_x2("scalar", g, half, slice(gpsimd_share, HALF))
 
@@ -347,8 +345,8 @@ def tile_household_bracket_response_t2_kernel(
         front, back = tiles[:2], tiles[2:]
         pairs = range(PACK // 2)
 
-        factors = kept([P, EARLY, PACK], F32, "factors")
         early = slice(0, EARLY)
+        factors = kept([P, len(front)], F32, "factors")
 
         zeros = kept([P, P, PACK], BF16, "zeros")
         zero_codes = kept([P, P], U32, "zero_codes")
@@ -406,6 +404,7 @@ def tile_household_bracket_response_t2_kernel(
         interleave_x("vector", 2, RIGHT, slice(0, VECTOR_SHARE))
         add_x(2, LEFT, tiles[:1])
         quantise_x(2, RIGHT)
+
         for k in range(GROUPS):
             for t in tiles:
                 multiply_a(2, RIGHT, t, k)
@@ -416,6 +415,7 @@ def tile_household_bracket_response_t2_kernel(
         add_x(2, RIGHT, tiles)
         round_x1("gpsimd", 2, RIGHT, tiles[:1])
         round_x1("scalar", 2, RIGHT, tiles[1:])
+
         multiply_a_tiles(0, RIGHT, front)
         add_x(0, RIGHT, front)
         turn_x1(0, LEFT)
@@ -429,7 +429,7 @@ def tile_household_bracket_response_t2_kernel(
                 quantise_x1(2, half, [pair])
             add_x(0, RIGHT, [back[pair]])
         regroup_x1("scalar", 0, LEFT, pairs)
-        nc.scalar.copy(out=factors[:], in_=prop[:])
+        nc.scalar.copy(out=factors[:], in_=prop[:, 0, : len(front)])
         round_x1("scalar", 0, RIGHT, front)
         round_x1("gpsimd", 0, RIGHT, back)
         round_x1("scalar", 1, LEFT, front)
@@ -466,29 +466,29 @@ def tile_household_bracket_response_t2_kernel(
         quantise_x2(2, RIGHT)
         multiply_r(0, RIGHT, tiles)
         quantise_x1(1, RIGHT, pairs)
-        add_x1_aside(0, RIGHT, 0)
-        add_x1_aside(0, RIGHT, 1)
+        for t in front:
+            add_x1_aside(0, RIGHT, t, factors[:, t : t + 1])
         interleave_x2("scalar", 0, LEFT, whole)
         add_x1(0, RIGHT, back)
 
         multiply_r(1, LEFT, tiles)
         add_x1(1, LEFT, tiles)
         quantise_x2(0, LEFT)
-        shared(1, LEFT, LAST_SHARES[0])
-        shared(0, RIGHT, LAST_SHARES[1])
+        interleave_x2_shared(1, LEFT, LAST_LEFT_SHARE)
+        interleave_x2_shared(0, RIGHT, LAST_RIGHT_SHARE)
         multiply_r(1, RIGHT, tiles)
         add_x1(1, RIGHT, tiles)
-        interleave_x2("scalar", 1, RIGHT, whole)
         quantise_x2(1, LEFT)
         quantise_x2(0, RIGHT)
+        interleave_x2_shared(1, RIGHT, LAST_RIGHT_SHARE)
 
         for k in B_ORDER:
             multiply_b(LEFT, k, tiles)
-        multiply_b(RIGHT, 2, tiles)
+        multiply_b(RIGHT, B_ORDER[0], tiles)
         finish(LEFT, front, [nc.sync])
         quantise_x2(1, RIGHT)
         finish(LEFT, back, [nc.scalar, nc.sync])
         for j in tiles:
-            multiply_b(RIGHT, 0, [j])
-            multiply_b(RIGHT, 1, [j])
+            for k in B_ORDER[1:]:
+                multiply_b(RIGHT, k, [j])
         finish(RIGHT, tiles, [nc.scalar, nc.sync])

@@ -32,6 +32,7 @@ EARLY = BANKS // PACK
 PAIRED = EARLY
 B_ORDER = (PAIRED, 0, 1)
 WARM_UP_PASSES = 3
+ALIGN = 256
 RUN = 4
 SCALAR_SHARE = 176
 GPSIMD_SHARE = 208
@@ -60,8 +61,8 @@ def tile_household_bracket_response_t2_kernel(
         psum = ctx.enter_context(tc.psum_pool(name="psum", bufs=1))
         ctx.enter_context(tc.manual_schedule())
 
-        def kept(shape, dtype, name):
-            return keep.tile(shape, dtype, name=name, align_bytes=64)
+        def kept(shape, dtype, name, align=64):
+            return keep.tile(shape, dtype, name=name, align_bytes=align)
 
         def columns(half):
             return slice(HALF * half, HALF * (half + 1))
@@ -174,8 +175,8 @@ def tile_household_bracket_response_t2_kernel(
         def quantise(codes, scales, grouped):
             nc.vector.quantize_mx(out=codes.bitcast(FP8X4), scales=scales, in_=grouped.rearrange("p c t -> p (c t)"))
 
-        a_words = kept([P, GROUPS, PACK, GROUPS, E2M1_BYTES * P], U8, "a_words")
-        a_scales = kept([P, GROUPS, PACK, GROUPS, P], U8, "a_scales")
+        a_words = kept([P, GROUPS, PACK, GROUPS, E2M1_BYTES * P], U8, "a_words", ALIGN)
+        a_scales = kept([P, GROUPS, PACK, GROUPS, P], U8, "a_scales", ALIGN)
 
         def reorder_early_words(engine, groups, k):
             copy(
@@ -194,8 +195,8 @@ def tile_household_bracket_response_t2_kernel(
             scales_in = plane.rearrange("p k (g m t) -> p g t k m", g=EARLY, t=PACK)
             nc.vector.tensor_copy(out=a_scales[:, groups, :, passes, :], in_=scales_in[:, groups, :, :, :])
 
-        xq = [kept([P, C], U32, f"xq_{g}") for g in range(GROUPS)]
-        xq_scales = [kept([P, C], U8, f"xq_scales_{g}") for g in range(GROUPS)]
+        xq = [kept([P, C], U32, f"xq_{g}", ALIGN) for g in range(GROUPS)]
+        xq_scales = [kept([P, C], U8, f"xq_scales_{g}", ALIGN) for g in range(GROUPS)]
 
         def interleave_x(engine, g, half, part):
             grouped = stage("x_grouped", g, half, [P, HALF, PACK], tag="grouped")
@@ -348,7 +349,7 @@ def tile_household_bracket_response_t2_kernel(
         early = slice(0, EARLY)
         factors = kept([P, len(front)], F32, "factors")
 
-        zeros = kept([P, P, PACK], BF16, "zeros")
+        zeros = stage("zeros", 0, LEFT, [P, P, PACK], tag="x1_grouped")
         zero_codes = kept([P, P], U32, "zero_codes")
         zero_scales = kept([P, P], U8, "zero_scales")
         nc.vector.memset(zeros[:].rearrange("p c t -> p (c t)").bitcast(I32), 0)

from contextlib import ExitStack

import concourse.mybir as mybir
from concourse.masks import make_identity

H, C, G = 1536, 1024, 512
FLOPS = 2 * (H * H * C + H * C * C + H * G * C)

F32 = mybir.dt.float32
BF16 = mybir.dt.bfloat16
I32 = mybir.dt.int32
U32 = mybir.dt.uint32
U16 = mybir.dt.uint16
U8 = mybir.dt.uint8
FP8X4 = mybir.dt.float8_e4m3fn_x4
FP4X4 = mybir.dt.float4_e2m1fn_x4
ADD = mybir.AluOpType.add
MULT = mybir.AluOpType.mult
COPY = mybir.ActivationFunctionType.Copy

P = 128
PACK = 4
K_PASS = P * PACK
GROUPS = H // K_PASS
HALVES = C // K_PASS
HALF = K_PASS
LEFT, RIGHT = range(HALVES)
OUT_TILES = G // P
BANKS = 8
E2M1_BYTES = 2
EARLY = BANKS // PACK
PAIRED = EARLY
B_ORDER = (PAIRED, 0, 1)
WARM_UP_PASSES = 3
ALIGN = 256
RUN = 4
SCALAR_SHARE = 176
GPSIMD_SHARE = 208
VECTOR_SHARE = 64
LAST_LEFT_SHARE, LAST_RIGHT_SHARE = 224, 144
MOVED_SHARE = 208


def tile_household_bracket_response_t2_kernel(
    tc,
    x,
    transfer_words,
    transfer_scales,
    reclass_words,
    reclass_scales,
    bracket_words,
    bracket_scales,
    propensity,
    rate,
    out,
):
    nc = tc.nc
    with ExitStack() as ctx:
        keep = ctx.enter_context(tc.tile_pool(name="keep", bufs=1))
        work = ctx.enter_context(tc.tile_pool(name="work", bufs=3))
        psum = ctx.enter_context(tc.psum_pool(name="psum", bufs=1))
        ctx.enter_context(tc.manual_schedule())

        def kept(shape, dtype, name, align=64):
            return keep.tile(shape, dtype, name=name, align_bytes=align)

        def columns(half):
            return slice(HALF * half, HALF * (half + 1))

        a_scales_first = kept([P, 1, EARLY * K_PASS], U8, "a_scales_first")
        a_scales_early = kept([P, GROUPS - 1, EARLY * K_PASS], U8, "a_scales_early")
        a_scales_last = kept([P, GROUPS, K_PASS], U8, "a_scales_last")
        r_scales = kept([P, HALVES, C], U8, "r_scales")
        b_scales = kept([P, GROUPS, G], U8, "b_scales")
        for plane in (a_scales_first, a_scales_early, a_scales_last, r_scales, b_scales):
            nc.vector.memset(plane[:].bitcast(I32), 0)
        identity = kept([P, P], F32, "identity")
        make_identity(nc, identity[:])

        x_in = [[kept([P, PACK, HALF], BF16, f"x_{g}_{half}") for half in range(HALVES)] for g in range(GROUPS)]
        a_early = [kept([P, EARLY, E2M1_BYTES * K_PASS], U8, f"a_early_{k}") for k in range(GROUPS)]
        a_last = kept([P, GROUPS, E2M1_BYTES * K_PASS], U8, "a_last")
        r_words = kept([P, HALVES, E2M1_BYTES * C], U8, "r_words")
        b_words = kept([P, GROUPS, E2M1_BYTES * G], U8, "b_words")
        x_paired = [kept([P, PACK, HALF], BF16, f"x_paired_{half}") for half in range(HALVES)]
        prop = kept([P, EARLY, PACK], BF16, "prop")
        prop_paired = kept([P, PACK, 2], BF16, "prop_paired")
        rates = kept([P, OUT_TILES, C], BF16, "rates")

        def load_scales(plane, scales):
            words = plane[:].bitcast(I32)
            for q in range(4):
                nc.sync.dma_start(
                    out=words[32 * q : 32 * q + 4, :, :],
                    in_=scales[:, 4 * q : 4 * q + 4, :].rearrange("k r n -> r k n").bitcast(I32),
                )

        def load_words(tile, words):
            nc.sync.dma_start(out=tile[:].bitcast(I32), in_=words.rearrange("k p n -> p k n").bitcast(I32))

        def load_x(g, half):
            rows = x[K_PASS * g : K_PASS * (g + 1), columns(half)]
            nc.sync.dma_start(out=x_in[g][half][:], in_=rows.rearrange("(p t) c -> p t c", t=PACK))

        def load_a_early(k):
            words = transfer_words[k, :, : E2M1_BYTES * EARLY * K_PASS].rearrange("p (g n) -> p g n", g=EARLY)
            nc.sync.dma_start(out=a_early[k][:].bitcast(I32), in_=words.bitcast(I32))

        for k in range(GROUPS):
            load_x(k, LEFT)
            if k == 0:
                load_scales(a_scales_first, transfer_scales[:1, :, : EARLY * K_PASS])
            if k == 1:
                load_scales(a_scales_early, transfer_scales[1:, :, : EARLY * K_PASS])
            load_a_early(k)
        load_scales(a_scales_last, transfer_scales[:, :, EARLY * K_PASS :])
        load_words(a_last, transfer_words[:, :, E2M1_BYTES * EARLY * K_PASS :])
        for g in range(GROUPS):
            load_x(g, RIGHT)
        for half in range(HALVES):
            rows = x[K_PASS * PAIRED :, columns(half)].rearrange("(a t e) c -> e a t c", t=PACK, e=2)
            for e in range(2):
                nc.sync.dma_start(out=x_paired[half][e:P:2, :, :], in_=rows[e, :, :, :])
        load_scales(r_scales, reclass_scales)
        load_words(r_words, reclass_words)
        nc.sync.dma_start(out=prop[:], in_=propensity[: K_PASS * PAIRED].rearrange("(g p t) -> p g t", p=P, t=PACK))
        for e in range(2):
            nc.sync.dma_start(
                out=prop_paired[e:P:2, :, 0:1],
                in_=propensity[K_PASS * PAIRED :].rearrange("(a t e) -> a t e", t=PACK, e=2)[:, :, e : e + 1],
                allow_slow_non_contiguous=True,
            )
        load_scales(b_scales, bracket_scales)
        load_words(b_words, bracket_words)
        nc.sync.dma_start(out=rates[:], in_=rate.rearrange("(j p) c -> p j c", p=P))

        closed_banks = list(range(BANKS))
        open_banks = {}

        def open_bank(key, shape):
            bank = closed_banks.pop(0)
            tile = psum.tile(shape, F32, name="acc", tag=f"bank_{bank}")
            open_banks[key] = bank, tile
            return tile

        def close_bank(key):
            bank, tile = open_banks.pop(key)
            closed_banks.append(bank)
            return tile

        staged = {}
        ROUNDED_BUFS = 4

        def stage(kind, g, half, shape, bufs=3, tag=None, dtype=BF16):
            if (kind, g, half) not in staged:
                tile = work.tile(shape, dtype, name=kind, tag=tag or kind, bufs=bufs, align_bytes=64)
                staged[kind, g, half] = tile
            return staged[kind, g, half]

        def copy(engine, out_ap, in_ap):
            if engine == "vector":
                nc.vector.tensor_copy(out=out_ap, in_=in_ap)
            elif engine == "gpsimd":
                nc.gpsimd.tensor_scalar(out=out_ap, in0=in_ap, scalar1=1.0, scalar2=0.0, op0=MULT, op1=ADD)
            else:
                nc.scalar.copy(out=out_ap, in_=in_ap)

        def interleave(engine, grouped, unit):
            copy(
                engine,
                grouped.rearrange("p (c i) t -> p c t i", i=RUN),
                unit.rearrange("p t (c i) -> p c t i", i=RUN),
            )

        def quantise(codes, scales, grouped):
            nc.vector.quantize_mx(out=codes.bitcast(FP8X4), scales=scales, in_=grouped.rearrange("p c t -> p (c t)"))

        a_words = kept([P, GROUPS, PACK, GROUPS, E2M1_BYTES * P], U8, "a_words", ALIGN)
        a_scales = kept([P, GROUPS, PACK, GROUPS, P], U8, "a_scales", ALIGN)

        def reorder_early_words(engine, groups, k):
            copy(
                engine,
                a_words[:, groups, :, k, :].bitcast(U16).rearrange("p g t (m i) -> p g m t i", i=RUN),
                a_early[k][:, groups, :].bitcast(U16).rearrange("p g (m i t) -> p g m t i", i=RUN, t=PACK),
            )

        def reorder_pairs(reordered, arrived, pair):
            nc.scalar.copy(
                out=reordered[:, PAIRED, :, :, :].bitcast(pair).rearrange("p t k (a i) -> p k a t i", i=RUN),
                in_=arrived[:].bitcast(pair).rearrange("p k (a i t) -> p k a t i", i=RUN, t=PACK),
            )

        def reorder_early_scales(plane, groups, passes):
            scales_in = plane.rearrange("p k (g m t) -> p g t k m", g=EARLY, t=PACK)
            nc.vector.tensor_copy(out=a_scales[:, groups, :, passes, :], in_=scales_in[:, groups, :, :, :])

        xq = [kept([P, C], U32, f"xq_{g}", ALIGN) for g in range(GROUPS)]
        xq_scales = [kept([P, C], U8, f"xq_scales_{g}", ALIGN) for g in range(GROUPS)]

        def interleave_x(engine, g, half, part):
            grouped = stage("x_grouped", g, half, [P, HALF, PACK], tag="grouped")
            interleave(engine, grouped[:, part, :], x_in[g][half][:, :, part])

        def quantise_x(g, half):
            quantise(xq[g][:, columns(half)], xq_scales[g][:, columns(half)], staged["x_grouped", g, half][:])

        x1 = [kept([P, PACK, C], F32, f"x1_{g}") for g in range(GROUPS)]

        def multiply_a(g, half, t, k):
            if k == 0:
                open_bank((1, g, half, t), [P, HALF])
            nc.tensor.matmul_mx(
                out=open_banks[1, g, half, t][1][:],
                lhsT=a_words[:, g, t, k, :].bitcast(FP4X4),
                lhsT_scale=a_scales[:, g, t, k, :],
                rhs=xq[k][:, columns(half)].bitcast(FP8X4),
                rhs_scale=xq_scales[k][:, columns(half)],
                start=(k == 0),
                stop=(k == GROUPS - 1),
            )

        def multiply_a_tiles(g, half, tiles):
            for t in tiles:
                for k in range(GROUPS):
                    multiply_a(g, half, t, k)

        def add_x(g, half, tiles):
            for t in tiles:
                nc.vector.tensor_tensor(
                    out=x1[g][:, t, columns(half)],
                    in0=close_bank((1, g, half, t))[:],
                    in1=(x_paired[half] if g == PAIRED else x_in[g][half])[:, t, :],
                    op=ADD,
                )

        x1q = [[kept([P, K_PASS], U32, f"x1q_{g}_{half}") for half in range(HALVES)] for g in range(GROUPS)]
        x1q_scales = [[kept([P, K_PASS], U8, f"x1q_scales_{g}_{half}") for half in range(HALVES)] for g in range(GROUPS)]

        def round_x1(engine, g, half, tiles):
            rounded = stage("x1_rounded", g, half, [P, PACK, 2, P, 2], ROUNDED_BUFS)
            for t in tiles:
                row = x1[g][:, t, columns(half)]
                copy(engine, rounded[:, t, :, :, :], row.rearrange("p (w u e) -> p u w e", u=2, e=2))

        def turn_x1(g, half):
            rounded = staged["x1_rounded", g, half]
            for pair in range(PACK // 2):
                turned = open_bank(("turn", g, half, pair), [P, 2, 2, P])
                for i in range(2):
                    for u in range(2):
                        words = rounded[:, 2 * pair + i, u, :, :].rearrange("p w e -> p (w e)").bitcast(F32)
                        nc.tensor.transpose(turned[:, i, u, :], words, identity[:])

        def regroup_x1(engine, g, half, pairs):
            grouped = stage("x1_grouped", g, half, [P, K_PASS, PACK])
            for pair in pairs:
                words = grouped[:, 2 * P * pair : 2 * P * (pair + 1), :].rearrange("p m v -> p (m v)").bitcast(F32)
                copy(
                    engine,
                    words.rearrange("p (i m u) -> p i m u", i=2, u=2),
                    close_bank(("turn", g, half, pair))[:].rearrange("p i u m -> p i m u"),
                )

        def quantise_x1(g, half, pairs):
            part = slice(2 * P * pairs[0], 2 * P * (pairs[-1] + 1))
            quantise(x1q[g][half][:, part], x1q_scales[g][half][:, part], staged["x1_grouped", g, half][:, part, :])

        def multiply_r(g, half, tiles):
            for t in tiles:
                acc = open_bank((2, g, half, t), [P, HALF])
                for k in range(HALVES):
                    nc.tensor.matmul_mx(
                        out=acc[:],
                        lhsT=x1q[g][k][:, P * t : P * (t + 1)].bitcast(FP8X4),
                        lhsT_scale=x1q_scales[g][k][:, P * t : P * (t + 1)],
                        rhs=r_words[:, k, E2M1_BYTES * HALF * half : E2M1_BYTES * HALF * (half + 1)].bitcast(FP4X4),
                        rhs_scale=r_scales[:, k, columns(half)],
                        start=(k == 0),
                        stop=(k == HALVES - 1),
                    )

        def add_x1(g, half, tiles):
            x2 = stage("x2", g, half, [P, PACK, HALF])
            for t in tiles:
                nc.vector.scalar_tensor_tensor(
                    out=x2[:, t, :],
                    in0=close_bank((2, g, half, t))[:],
                    scalar=prop_paired[:, t, 0:1] if g == PAIRED else prop[:, g, t : t + 1],
                    in1=x1[g][:, t, columns(half)],
                    op0=MULT,
                    op1=ADD,
                )

        def move_x2(half, tiles):
            moved = stage("x2_moved", PAIRED, half, [P, PACK, HALF], bufs=HALVES)
            for t in tiles:
                u, v = divmod(t, 2)
                nc.sync.dma_start(out=moved[u:P:2, 2 * v : 2 * v + 2, :], in_=staged["x2", PAIRED, half][:, t, :])

        def add_x1_aside(g, half, t, factor):
            x2 = stage("x2", g, half, [P, PACK, HALF])
            scaled = work.tile([P, HALF], F32, name="scaled", bufs=2)
            nc.scalar.activation(out=scaled[:], in_=close_bank((2, g, half, t))[:], func=COPY, scale=factor)
            nc.gpsimd.tensor_tensor(out=x2[:, t, :], in0=scaled[:], in1=x1[g][:, t, columns(half)], op=ADD)

        x2q = [kept([P, C], U32, f"x2q_{g}") for g in range(GROUPS)]
        x2q_scales = [kept([P, C], U8, f"x2q_scales_{g}") for g in range(GROUPS)]

        def interleave_x2(engine, g, half, part):
            grouped = stage("x2_grouped", g, half, [P, HALF, PACK], tag="grouped")
            interleave(engine, grouped[:, part, :], staged["x2_moved" if g == PAIRED else "x2", g, half][:, :, part])

        def quantise_x2(g, half):
            quantise(x2q[g][:, columns(half)], x2q_scales[g][:, columns(half)], staged["x2_grouped", g, half][:])

        def multiply_b(half, k, out_tiles):
            for j in out_tiles:
                if k == B_ORDER[0]:
                    open_bank((3, half, j), [P, HALF])
                nc.tensor.matmul_mx(
                    out=open_banks[3, half, j][1][:],
                    lhsT=b_words[:, k, E2M1_BYTES * P * j : E2M1_BYTES * P * (j + 1)].bitcast(FP4X4),
                    lhsT_scale=b_scales[:, k, P * j : P * (j + 1)],
                    rhs=x2q[k][:, columns(half)].bitcast(FP8X4),
                    rhs_scale=x2q_scales[k][:, columns(half)],
                    start=(k == B_ORDER[0]),
                    stop=(k == B_ORDER[-1]),
                )

        def finish(half, out_tiles, queues):
            for j in out_tiles:
                pair = stage("response", j // 2, half, [P, 2, HALF], ROUNDED_BUFS, tag="x1_rounded", dtype=F32)
                response = pair[:, j % 2, :]
                nc.vector.tensor_tensor(
                    out=response, in0=close_bank((3, half, j))[:], in1=rates[:, j, columns(half)], op=MULT
                )
                queues[j % len(queues)].dma_start(out=out[P * j : P * (j + 1), columns(half)], in_=response)

        def interleave_x2_shared(g, half, gpsimd_share):
            interleave_x2("gpsimd", g, half, slice(0, gpsimd_share))
            interleave_x2("scalar", g, half, slice(gpsimd_share, HALF))

        whole = slice(0, HALF)
        tiles = range(PACK)
        front, back = tiles[:2], tiles[2:]
        pairs = range(PACK // 2)

        early = slice(0, EARLY)
        factors = kept([P, len(front)], F32, "factors")

        zeros = stage("zeros", 0, LEFT, [P, P, PACK], tag="x1_grouped")
        zero_codes = kept([P, P], U32, "zero_codes")
        zero_scales = kept([P, P], U8, "zero_scales")
        nc.vector.memset(zeros[:].rearrange("p c t -> p (c t)").bitcast(I32), 0)
        quantise(zero_codes[:], zero_scales[:], zeros[:])
        unread = open_bank("warm-up", [P, HALF])
        for repeat in range(WARM_UP_PASSES):
            nc.tensor.matmul_mx(
                out=unread[:],
                lhsT=zero_codes[:].bitcast(FP8X4),
                lhsT_scale=zero_scales[:],
                rhs=a_scales_first[:, 0, :].bitcast(FP4X4),
                rhs_scale=a_scales_first[:, 0, :HALF],
                start=True,
                stop=True,
            )
        close_bank("warm-up")

        for k in range(GROUPS):
            interleave_x("scalar", k, LEFT, slice(0, SCALAR_SHARE))
            interleave_x("vector", k, LEFT, slice(SCALAR_SHARE, HALF))
            if k == 0:
                reorder_early_scales(a_scales_first[:], slice(0, 1), slice(0, 1))
                reorder_early_words("scalar", slice(0, 1), k)
                quantise_x(k, LEFT)
                reorder_early_scales(a_scales_first[:], slice(1, 2), slice(0, 1))
                reorder_early_words("vector", slice(1, 2), k)
            elif k == 1:
                reorder_early_scales(a_scales_early[:, :1, :], early, slice(1, 2))
                quantise_x(k, LEFT)
                reorder_early_scales(a_scales_early[:, 1:, :], early, slice(2, GROUPS))
                for g in range(EARLY):
                    reorder_early_words("scalar", slice(g, g + 1), k)
            else:
                reorder_early_words("scalar", slice(0, 1), k)
                quantise_x(k, LEFT)
                reorder_early_words("vector", slice(1, 2), k)
            for g in range(EARLY):
                for t in tiles:
                    multiply_a(g, LEFT, t, k)

        reorder_pairs(a_scales, a_scales_last, U16)
        reorder_pairs(a_words, a_last, U32)
        for g in range(EARLY):
            interleave_x("gpsimd", g, RIGHT, slice(0, GPSIMD_SHARE))
            interleave_x("scalar", g, RIGHT, slice(GPSIMD_SHARE, HALF))
        interleave_x("scalar", 2, RIGHT, slice(VECTOR_SHARE, HALF))
        add_x(0, LEFT, tiles)
        multiply_a_tiles(2, LEFT, tiles)
        add_x(1, LEFT, tiles[:3])
        quantise_x(0, RIGHT)
        add_x(1, LEFT, tiles[3:])
        quantise_x(1, RIGHT)
        interleave_x("vector", 2, RIGHT, slice(0, VECTOR_SHARE))
        add_x(2, LEFT, tiles[:1])
        quantise_x(2, RIGHT)

        for k in range(GROUPS):
            for t in tiles:
                multiply_a(2, RIGHT, t, k)
        round_x1("scalar", 0, LEFT, tiles)
        add_x(2, LEFT, tiles[1:])
        round_x1("scalar", 2, LEFT, tiles[:3])
        round_x1("gpsimd", 2, LEFT, tiles[3:])
        add_x(2, RIGHT, tiles)
        round_x1("gpsimd", 2, RIGHT, tiles[:1])
        round_x1("scalar", 2, RIGHT, tiles[1:])

        multiply_a_tiles(0, RIGHT, front)
        add_x(0, RIGHT, front)
        turn_x1(0, LEFT)
        turn_x1(2, LEFT)
        turn_x1(2, RIGHT)
        multiply_a_tiles(0, RIGHT, back)
        for pair in pairs:
            for half in range(HALVES):
                regroup_x1("vector" if (half, pair) == (RIGHT, 0) else "scalar", 2, half, [pair])
            for half in range(HALVES):
                quantise_x1(2, half, [pair])
            add_x(0, RIGHT, [back[pair]])
        regroup_x1("scalar", 0, LEFT, pairs)
        nc.scalar.copy(out=factors[:], in_=prop[:, 0, : len(front)])
        round_x1("scalar", 0, RIGHT, front)
        round_x1("gpsimd", 0, RIGHT, back)
        round_x1("scalar", 1, LEFT, front)
        round_x1("gpsimd", 1, LEFT, back)

        for half in range(HALVES):
            multiply_r(2, half, tiles)
            for t in tiles:
                add_x1(2, half, [t])
                move_x2(half, [t])
        turn_x1(0, RIGHT)
        turn_x1(1, LEFT)
        regroup_x1("scalar", 0, RIGHT, pairs)
        regroup_x1("scalar", 1, LEFT, pairs)
        quantise_x1(0, LEFT, pairs)
        quantise_x1(0, RIGHT, pairs)

        multiply_a_tiles(1, RIGHT, tiles)
        add_x(1, RIGHT, tiles[:1])
        quantise_x1(1, LEFT, pairs)
        add_x(1, RIGHT, tiles[1:])
        round_x1("scalar", 1, RIGHT, tiles[:1])
        round_x1("gpsimd", 1, RIGHT, tiles[1:3])
        interleave_x2("scalar", 2, LEFT, whole)
        round_x1("scalar", 1, RIGHT, tiles[3:])
        interleave_x2("gpsimd", 2, RIGHT, slice(MOVED_SHARE, HALF))
        interleave_x2("scalar", 2, RIGHT, slice(0, MOVED_SHARE))

        multiply_r(0, LEFT, tiles)
        add_x1(0, LEFT, tiles)
        turn_x1(1, RIGHT)
        regroup_x1("scalar", 1, RIGHT, pairs)
        quantise_x2(2, LEFT)
        quantise_x2(2, RIGHT)
        multiply_r(0, RIGHT, tiles)
        quantise_x1(1, RIGHT, pairs)
        for t in front:
            add_x1_aside(0, RIGHT, t, factors[:, t : t + 1])
        interleave_x2("scalar", 0, LEFT, whole)
        add_x1(0, RIGHT, back)

        multiply_r(1, LEFT, tiles)
        add_x1(1, LEFT, tiles)
        quantise_x2(0, LEFT)
        interleave_x2_shared(1, LEFT, LAST_LEFT_SHARE)
        interleave_x2_shared(0, RIGHT, LAST_RIGHT_SHARE)
        multiply_r(1, RIGHT, tiles)
        add_x1(1, RIGHT, tiles)
        quantise_x2(1, LEFT)
        quantise_x2(0, RIGHT)
        interleave_x2_shared(1, RIGHT, LAST_RIGHT_SHARE)

        for k in B_ORDER:
            multiply_b(LEFT, k, tiles)
        multiply_b(RIGHT, B_ORDER[0], tiles)
        finish(LEFT, front, [nc.sync])
        quantise_x2(1, RIGHT)
        finish(LEFT, back, [nc.scalar, nc.sync])
        for j in tiles:
            for k in B_ORDER[1:]:
                multiply_b(RIGHT, k, [j])
        finish(RIGHT, tiles, [nc.scalar, nc.sync])
